import numpy as np, ml_dtypes
CORES = [2,3,42,43,82,83,122,123]
N = 8
BF = ml_dtypes.bfloat16
def gentries(a):
    return np.ascontiguousarray(a.reshape(8, 16, -1).transpose(0, 2, 1)).reshape(8, -1)
def gtable(e):
    e = np.asarray(e); return np.ascontiguousarray(e.reshape(8, -1, 16).transpose(0, 2, 1)).reshape(128, -1).astype(np.int32)
D, NB, S, NEED, RO = 2048, 128, 32, 5, 4
P = S // 2; M = NB * P; W = D + M
TOP, NEAR = 255, 16
def parts(rng):
    pat = 2 * rng.integers(0, 2, (N, 8, 16, 1)) - 1; sgn = 2 * rng.integers(0, 2, (N, 8, 1, D)) - 1
    amp = rng.random((N, 8, 1, D)) * np.where(rng.random((N, 8, 1, D)) < 0.88, 49.5, 126.5)
    x = np.clip(np.rint(127.5 + pat * sgn * amp + 8.8 * rng.standard_normal((N, 8, 16, D))), 0, TOP).astype(np.int64)
    return x, rng.integers(0, 2 * W, (N, 8, D)), rng.integers(0, 2 * W, (N, 8, D)), rng.integers(0, 2 * W, (N, 8, NB, S)), rng.integers(0, 2, (N, 8, NB))
def pack(x, k0, k1, L, f):
    return {"faces": np.ascontiguousarray(x.reshape(N, 128, D)).astype(np.float32).astype(BF), "kid0": k0.astype(np.int32), "kid1": k1.astype(np.int32),
            "belts": np.stack([gtable(a.reshape(8, -1)) for a in L]), "flip": f.astype(np.int32)}
def planted(rng, z, n, few):
    x, k0, k1, L, f = z; cs = np.array([0, 1, 7, 8, 9, 10, 15, 16])
    hit = np.argsort(np.argsort(rng.random((N, 8, NB, P)), axis=-1), axis=-1) < n[..., None]
    for g in range(8):
        o = rng.permutation(D); sen = rng.integers(0, 2, D); c = np.zeros(D, np.int64); c[o] = cs[(np.arange(D) // 4) % 8]
        bl, fa, pt = o[1::4], o[2::4], o[3::4]; hi = fa[c[fa] >= 9]; lo = fa[c[fa] < 9]; sh = (N, 16, len(fa))
        close = np.where(rng.random(sh) < 0.5, NEAR, rng.integers(0, NEAR + 1, sh)); far = np.where(rng.random(sh) < 0.5, NEAR + 1, rng.integers(NEAR + 1, TOP + 1, sh))
        v = np.where(np.argsort(rng.random(sh), axis=1) < c[fa], close, far)
        y = x[:, g]; y[:, :, fa] = np.where(sen[fa] == 1, TOP - v, v); y[:, :, bl] = TOP * sen[bl]
        def twin(a):
            return 2 * D * ((a < M) & (rng.random(a.shape) < 0.5))
        def good(a):
            return 2 * a + sen[a] + twin(a)
        def some(a):
            return np.full((N, NB, P), a[int(rng.integers(0, len(a)))]) if few[g] else a[rng.integers(0, len(a), (N, NB, P))]
        q0 = k0[:, g]; q1 = k1[:, g]
        q0[:, pt] = good(bl[rng.integers(0, len(bl), (N, len(pt)))]); q1[:, pt] = good(bl[rng.integers(0, len(bl), (N, len(pt)))]) ^ 1
        lh = good(np.where(hit[:, g], some(hi), some(lo))); pk = some(pt); lk = 2 * pk + rng.integers(0, 2, pk.shape) + twin(pk)
        k = (2 * np.arange(P) + f[:, g, :, None]) % S; l = L[:, g]
        np.put_along_axis(l, k, lk, 2); np.put_along_axis(l, (k + 1) % S, lh, 2)
    return x, k0, k1, L, f
def setup_inputs(rng):
    return pack(*parts(rng))
def setup_inputs_spread(rng):
    x, k0, k1, L, f = parts(rng)
    pat = 2 * rng.integers(0, 2, (N, 8, 16, 1)) - 1; sgn = 2 * rng.integers(0, 2, (N, 8, 1, D)) - 1; amp = np.exp2(7.5 * rng.random((N, 8, 1, D)) - 0.5)
    x = np.clip(np.rint(127.5 + pat * sgn * amp + 5.5 * rng.standard_normal((N, 8, 16, D))), 0, TOP).astype(np.int64)
    x = np.where(rng.random((N, 8, 1, D)) < 0.125, rng.integers(0, TOP + 1, x.shape), x)
    z = []
    for a in (k0, k1, L):
        e = np.minimum((2 * W * rng.random(a.shape) ** 3).astype(np.int64), 2 * W - 1); e[:, 1::2] = 2 * W - 1 - e[:, 1::2]; z.append(e)
    f = (rng.random((N, 8, NB)) < 0.1 + 0.8 * rng.random((N, 8, 1))).astype(np.int64)
    return pack(x, z[0], z[1], z[2], f)
def mixends(rng, shape):
    return np.where(rng.random(shape) < 0.75, (2 * W - 1) * rng.integers(0, 2, shape), rng.integers(0, 2 * W, shape))
def setup_inputs_ends(rng):
    kind = rng.integers(0, 3, (N, 8, 1, D)); x = TOP * np.where(kind == 2, rng.integers(0, 2, (N, 8, 16, D)), kind)
    k0 = mixends(rng, (N, 8, D)); k1 = mixends(rng, (N, 8, D)); k0[..., M - 1] = 0; k1[..., 0] = 0
    f = rng.integers(0, 2, (N, 8, NB)); f[..., 0] = 0; f[..., NB - 1] = 1
    for q in (0, 1, N - 1): x[q, :, :, M - 1] = TOP - x[q, :, :, 0]
    L = mixends(rng, (N, 8, NB, S)); ks = ((np.arange(S) - f[..., None]) & 1) == 0; hs = (2 * W - 1) * rng.integers(0, 2, L.shape)
    calm = np.where(ks, 0, hs); wild = np.where(ks, 2 * W - 1, hs); full = np.where(ks, 2 * W - 1, 0)
    L[:, :, NB - 1] = full[:, :, NB - 1]; L[:, :, NB - 2] = 0
    L[0] = calm[0]; L[1] = calm[1]; L[1, 7, NB - 1] = full[1, 7, NB - 1]; L[N - 1] = wild[N - 1]
    return pack(x, k0, k1, L, f)
def setup_inputs_corners(rng):
    x, k0, k1, L, f = parts(rng); own = 2 * np.arange(D)
    for a in (k0, k1):
        w = rng.integers(0, 8, a.shape); e = rng.integers(0, 2, a.shape)
        a[...] = np.where(w == 0, own + e, np.where(w == 1, e, np.where(w == 2, 2 * W - 2 + e, np.where(w == 3, own[::-1] + e, a))))
    w = rng.integers(0, 6, (N, 8, NB, 1)); one = rng.integers(0, 2 * W, (N, 8, NB, 1))
    old = np.where(w == 0, one, np.where(w == 1, 0, np.where(w == 2, 2 * W - 1, L)))
    n = rng.choice(np.array([0, 1, NEED - 1, NEED, NEED + 1, P]), (N, 8, NB)); n[N - 1, 7, NB - 1] = P; n[0, 0, 0] = NEED; n[1, 0, 0] = NEED - 1
    x, k0, k1, L, f = planted(rng, (x, k0, k1, L, f), n, np.zeros(8, np.int64))
    m = rng.random((N, 8, NB, 1)) < 0.25; m[N - 1, 7, NB - 1] = False; m[:2, 0, 0] = False
    return pack(x, k0, k1, np.where(m, old, L), f)
def setup_inputs_crowd(rng):
    n = np.zeros((N, 8, NB), np.int64); low = np.array([0, NEED - 1]); top = np.array([NEED, P])
    for q in range(N):
        n[q] = rng.choice(low if q % 4 < 2 else top, (8, NB))
        if q % 4 == 1: n[q, 7, NB - 1] = P
        if q % 4 == 2: n[q, 7, NB - 1] = NEED - 1
    return pack(*planted(rng, parts(rng), n, 1 - np.arange(8) % 2))
def setup_inputs_stale(rng):
    x, k0, k1, L, f = parts(rng); z = int(rng.integers(0, N)); y = (z + 2) % N
    sh = (N, 16, D)
    for g in range(8):
        o = rng.permutation(D); sen = rng.integers(0, 2, D); bl, h1, h2, al, pt = o[0::5], o[1::5], o[2::5], o[3::5], o[4::5]
        c = rng.choice(np.array([0, 1, 7, 8]), (N, D)); c[:, al] = 16
        c[z, pt] = rng.choice(np.array([10, 16]), len(pt)); c[y, pt] = 9; c[z, h2] = 9; c[y, h1] = 9
        close = np.where(rng.random(sh) < 0.5, NEAR, rng.integers(0, NEAR + 1, sh)); far = np.where(rng.random(sh) < 0.5, NEAR + 1, rng.integers(NEAR + 1, TOP + 1, sh))
        v = np.where(np.argsort(rng.random(sh), axis=1) < c[:, None, :], close, far); v[:, :, bl] = 0
        x[:, g] = np.where(sen == 1, TOP - v, v)
        b0 = bl[rng.integers(0, len(bl), (N, D))]; b1 = bl[rng.integers(0, len(bl), (N, D))]
        k0[:, g] = 2 * b0 + sen[b0]; k1[:, g] = (2 * b1 + sen[b1]) ^ 1
        hp = h2[rng.integers(0, len(h2), (N, NB, P))]; hp[z] = h1[rng.integers(0, len(h1), (NB, P))]
        if 1 <= g <= 5:
            for q in (z, y):
                i = NB - 1 if g == 5 else int(rng.integers(0, NB))
                hp[q, i] = al[rng.integers(0, len(al), P)]
        pk = pt[rng.integers(0, len(pt), (N, NB, P))]
        k = (2 * np.arange(P) + f[:, g, :, None]) % S; l = L[:, g]
        np.put_along_axis(l, k, (2 * pk + sen[pk]) ^ 1, 2); np.put_along_axis(l, (k + 1) % S, 2 * hp + sen[hp], 2)
    return pack(x, k0, k1, L, f)
def check_inputs(d):
    bad = []
    for k, lo, hi in (("faces", 0, TOP), ("kid0", 0, 2 * W - 1), ("kid1", 0, 2 * W - 1), ("belts", 0, 2 * W - 1), ("flip", 0, 1)):
        v = np.asarray(d[k]).astype(np.float64)
        if not (np.min(v) >= lo and np.max(v) <= hi): bad.append("range of " + k)
        if np.any(v != np.floor(v)): bad.append("whole numbers in " + k)
    return bad
def values(x, e):
    v = np.take_along_axis(x, (e >> 1)[:, :, None, :], 3)
    return np.where((e & 1)[:, :, None, :] == 1, TOP - v, v)
def reference(faces, kid0, kid1, belts, flip):
    x = faces.astype(np.float32).astype(np.int32).reshape(N, 8, 16, D); x = np.concatenate([x, x[..., :M]], axis=3)
    k0 = kid0.astype(np.int64); k0 = np.concatenate([k0, k0[..., :M]], axis=2)
    k1 = kid1.astype(np.int64); k1 = np.concatenate([k1, k1[..., :M]], axis=2)
    L = np.stack([gentries(a) for a in belts]).astype(np.int64).reshape(N, 8, NB, S); f = flip.astype(np.int64)
    A = np.zeros(N, np.int64); new = 2 * (D + np.arange(M)).reshape(NB, P)
    for t in range(RO):
        if t > 0:
            L = np.roll(L, 1, axis=0); f = np.roll(f, 1, axis=0)
        k = (2 * np.arange(P) + f[..., None]) % S; h = (k + 1) % S
        lk = np.take_along_axis(L, k, 3); lh = np.take_along_axis(L, h, 3)
        e = lk.reshape(N, 8, M); w = lh.reshape(N, 8, M); odd = (e & 1) == 1
        c0 = np.take_along_axis(k0, e >> 1, 2); c1 = np.take_along_axis(k1, e >> 1, 2)
        a = np.where(odd, c1 ^ 1, c0); b = np.where(odd, c0 ^ 1, c1); u = b ^ 1
        fu = values(x, u); fw = values(x, w)
        near = np.add.reduce((np.abs(fu - fw) <= NEAR).astype(np.int64), axis=2)
        split = (near >= 9 + (A & 1)[:, None, None]).reshape(N, 8, NB, P)
        opens = np.add.reduce(split.astype(np.int64), axis=3) >= NEED
        go = split & opens[..., None]; gm = go.reshape(N, 8, M)
        x = np.concatenate([x[..., :D], np.where(gm[:, :, None, :], (fu + fw) >> 1, x[..., D:])], axis=3)
        k0 = np.concatenate([k0[..., :D], np.where(gm, u, k0[..., D:])], axis=2)
        k1 = np.concatenate([k1[..., :D], np.where(gm, w, k1[..., D:])], axis=2)
        l2 = np.array(L)
        np.put_along_axis(l2, k, np.where(go, a.reshape(N, 8, NB, P), lk), 3); np.put_along_axis(l2, h, np.where(go, new, lh), 3)
        L = np.where(opens[..., None], l2, L ^ 1); f = np.where(opens, f, 1 - f)
        A = np.add.reduce((~opens).astype(np.int64).reshape(N, 8 * NB), axis=1)
    return {"yx": x.reshape(N, 128, W).astype(np.float32).astype(BF), "y0": k0.astype(np.float32), "y1": k1.astype(np.float32),
            "yb": np.stack([gtable(q.reshape(8, -1)) for q in L]).astype(np.float32), "yf": f.astype(np.float32)}

@@ -1,0 +1,706 @@
+import numpy as np
+from concourse.mybir import dt, AluOpType as A, AxisListType, ActivationFunctionType as F
+
+F32, BF, I32, U16 = "float32", "bfloat16", "int32", "uint16"
+SCRATCH = {}
+for _n, _w, _d in [
+    ("ft", 8192, BF), ("kt", 4096, BF), ("yv", 10240, F32), ("g1", 2048, BF), ("fw", 2048, BF), ("dd", 2048, BF),
+    ("ind", 2048, BF), ("land0", 264, F32), ("land1", 264, F32), ("land2", 264, F32), ("land3", 264, F32),
+    ("snd0", 264, F32), ("snd1", 264, F32), ("snd2", 264, F32), ("snd3", 264, F32), ("ofh", 128, U16), ("ofb", 8, U16),
+    ("old", 512, F32), ("s2", 128, F32), ("ab", 128, F32), ("abi", 128, I32), ("ofk", 128, U16), ("ofu", 128, U16),
+    ("sd", 128, F32), ("cand", 768, F32), ("spl", 128, BF), ("uu", 128, F32), ("dpr", 256, F32), ("x0", 256, F32), ("pt0", 256, F32),
+    ("pt1", 256, F32), ("ptu", 128, U16), ("hl", 512, BF), ("sc0", 16, F32), ("sc1", 16, F32), ("sco", 16, F32),
+    ("ff", 8, F32), ("fn", 8, F32), ("fnb", 16, BF), ("thr", 16, F32),
+    ("ki", 256, I32), ("bi", 256, I32), ("fi", 128, I32), ("fb", 128, BF), ("t1", 256, I32), ("t2", 256, F32),
+    ("t3", 256, F32), ("kv", 256, F32), ("t4", 256, I32), ("t5", 256, F32), ("t6", 256, F32), ("bv", 256, F32),
+    ("kf", 256, F32), ("ramp", 160, F32), ("iv", 128, F32), ("ig", 128, F32), ("pi", 8, I32), ("ci", 8, I32),
+    ("cf", 32, F32), ("bc", 144, BF), ("cm", 144, BF), ("cd", 144, BF), ("cp", 144, BF), ("cr", 144, BF),
+    ("b8", 144, BF), ("idp", 160, BF), ("nid", 128, BF), ("hid", 128, BF), ("wm", 128, BF), ("i32", 128, BF), ("si", 640, BF), ("su", 640, BF),
+    ("oh", 144, BF), ("im", 768, F32), ("fm", 768, F32), ("shf", 256, F32), ("one", 160, F32), ("neg", 128, F32), ("oneb", 160, BF),
+    ("li", 64, F32), ("lt", 32, F32), ("lu", 32, U16), ("tr0", 256, F32), ("tr1", 256, F32), ("tr2", 256, F32),
+    ("tr3", 256, F32), ("fin", 256, F32), ("hy", 512, F32), ("lf", 8, F32), ("lfu", 8, U16), ("yb1", 256, F32),
+    ("yb2", 256, F32), ("yfo", 128, F32),
+]:
+    SCRATCH[_n] = ("sbuf", [128, _w], _d)
+PSUM = ["xa", "xb", "z0", "z1", "cn", "nw", "db", "rb"]
+for _n in PSUM:
+    SCRATCH[_n] = ("psum", [128, 512], F32)
+NDMA = 30
+SEMAPHORES = (["ev", "ea", "ep", "eg"] + ["%s%d%s" % (_a, _t, _b) for _a in ("arr", "out") for _t in (1, 2, 3) for _b in "kh"]
+              + ["dm%d" % _i for _i in range(NDMA)])
+
+CY = 1.5 * 2.0 ** 23
+C2 = 1.5 * 2.0 ** 24
+C32 = 1.5 * 2.0 ** 28
+
+
+def R(name, a, b, step=1, p=None):
+    return (name, a, b, step, p)
+
+
+def IND(win, off):
+    return ("*", win, off)
+
+
+def _mask(s):
+    m = 0
+    for c in (range(s[1], s[2], s[3]) if s[3] > 0 else range(s[1], -1 if s[2] is None else s[2], s[3])):
+        m |= 1 << c
+    return m
+
+
+PLAN = {"pe": 0.42, "gat": 1.56, "hop": 2600.0, "wake": 60.0, "seed": 1, "mean": 0.1, "sign": 1, "steps": 30000, "heat": 120.0, "own": (2, 3), "gq": 512, "sq": 512}
+_PLANS = {}
+
+
+def _len(s):
+    if s[0] == "*":
+        return 16 * _len(s[2])
+    return len(range(s[1], s[2], s[3]) if s[3] > 0 else range(s[1], -1 if s[2] is None else s[2], s[3]))
+
+
+def _cost(e, out, a, b=None):
+    n = _len(out)
+    if a[0] == "*":
+        return (50 if e == "v" else 65) + n * PLAN["gat"] * 0.83
+    k = 1.0
+    if b is not None:
+        k = 1.0 if a[0] in PSUM or b[0] in PSUM else 2.0
+    elif e == "v" and SCRATCH[out[0]][2] in (BF, U16) and SCRATCH[a[0]][2] in (BF, U16):
+        k = 0.5
+    return (50 if e == "v" else 65) + max(64, n * k) * 0.83
+
+
+def _edges(ops):
+    hist, masks, out = {}, {}, []
+    for n, o in enumerate(ops):
+        deps = {}
+        acc = [(s, False) for s in o["r"]] + [(s, True) for s in o["w"]]
+        for s, wr in acc:
+            if s[1:4] not in masks:
+                masks[s[1:4]] = _mask(s)
+            m = masks[s[1:4]]
+            for m2, n2, w2 in hist.get(s[0], ()):
+                if (wr or w2) and m & m2:
+                    deps[n2] = deps.get(n2, False) or (w2 and not wr)
+        for s, wr in acc:
+            hist.setdefault(s[0], []).append((masks[s[1:4]], n, wr))
+        out.append(deps)
+    return out
+
+
+def _plan(ops, edges):
+    n = len(ops)
+    pre = [set(d) for d in edges]
+    for i, o in enumerate(ops):
+        if o["k"] == "x":
+            pre[i].add(max(j for j in range(i) if ops[j]["k"] == "r" and ops[j]["sem"][0][3:] == o["sem"][0][3:]))
+    post = [[] for _ in ops]
+    for i in range(n):
+        for j in pre[i]:
+            post[j].append(i)
+    prio = [0.0] * n
+    for i in range(n - 1, -1, -1):
+        prio[i] = min(c for _, c in ops[i]["alt"].values()) + ops[i]["lat"] + PLAN["wake"] + max([prio[j] for j in post[i]] + [0.0])
+    post = [set(p) for p in post]
+    banks = [set(s[0] for s in o["r"] + o["w"] if s[0] in PSUM) for o in ops]
+    pre = [[j for j in p if not any(j in pre[k] for k in p)] for p in pre]
+    wake = PLAN["wake"]
+    cost = [{e: c for e, (_, c) in o["alt"].items()} for o in ops]
+    lat = [o["lat"] + wake for o in ops]
+    banks = [sorted(b) for b in banks]
+
+    def place(seq, eng, base, start, end):
+        busy = {k: list(v) for k, v in base.items()}
+        for i in seq:
+            t = 0.0
+            for j in pre[i]:
+                if end[j] > t:
+                    t = end[j]
+            e = eng[i]
+            c = cost[i][e]
+            mine = busy.setdefault(e, [])
+            while True:
+                t1 = t
+                k = len(mine)
+                while k and mine[k - 1][1] > t:
+                    k -= 1
+                while k < len(mine) and mine[k][0] < t + c:
+                    t = mine[k][1]
+                    k += 1
+                for b in banks[i]:
+                    for s0, s1, e2 in reversed(busy.setdefault(b, [])):
+                        if e2 != e and s1 + wake > t and s0 < t + c + wake:
+                            t = s1 + wake
+                if t == t1 or not banks[i]:
+                    break
+            mine.insert(k, (t, t + c))
+            for b in banks[i]:
+                busy[b].append((t, t + c, e))
+            start[i], end[i] = t, t + c + lat[i]
+        return max(end[i] for i in seq) + PLAN["mean"] * sum(end[i] for i in seq) / len(seq), busy
+
+    part, left = [], set(range(n))
+    for w in [i for i in range(n) if ops[i]["k"] == "r"][1::2]:
+        mine, todo = set(), [w - 1, w]
+        while todo:
+            i = todo.pop()
+            if i in left:
+                left.discard(i)
+                mine.add(i)
+                todo += pre[i]
+        part.append(mine)
+    part.append(left)
+    rng = np.random.RandomState(PLAN["seed"])
+    eng = [("a" if "a" in c else list(c)[0]) for c in cost]
+    start, end, base = [0.0] * n, [0.0] * n, {}
+    for mine in part:
+        seq = sorted(mine, key=lambda i: (-prio[i], i))
+        m = len(seq)
+        flex = [i for i in seq if len(cost[i]) > 1]
+        best, _ = place(seq, eng, base, start, end)
+        top = (best, seq, list(eng))
+        steps = PLAN["steps"]
+        rnd = rng.rand(steps, 5).tolist()
+        for it in range(steps):
+            r0, r1, r2, r3, r4 = rnd[it]
+            s2, e2 = seq, eng
+            if r0 < 0.35:
+                e2 = list(eng)
+                i = flex[int(r1 * len(flex))]
+                e2[i] = "v" if eng[i] == "a" else "a"
+                j = flex[int(r2 * len(flex))]
+                if r3 < 0.5 and eng[j] != eng[i]:
+                    e2[j] = eng[i]
+            else:
+                s2 = list(seq)
+                p = int(r1 * m)
+                i = s2.pop(p)
+                q = p
+                if r2 < 0.5:
+                    far = max(0, p - 1 - int(r3 * 30))
+                    while q > far and i not in post[s2[q - 1]]:
+                        q -= 1
+                else:
+                    far = min(m - 1, p + 1 + int(r3 * 30))
+                    while q < far and s2[q] not in post[i]:
+                        q += 1
+                if q == p:
+                    continue
+                s2.insert(q, i)
+            v, _ = place(s2, e2, base, start, end)
+            if v <= best + PLAN["heat"] * (1.0 - it / steps) * r4:
+                best, seq, eng = v, s2, e2
+                if v < top[0]:
+                    top = (v, s2, list(e2))
+        _, seq, eng = top
+        v, busy = place(seq, eng, base, start, end)
+        base = {k: [x for x in l if x[1] > v - 12000.0] for k, l in busy.items()}
+        for k in "vapgs":
+            base[k] = [(0.0, max(0.0, v - 12000.0))] + base.get(k, [])
+    return [(i, eng[i]) for i in sorted(range(n), key=lambda i: (start[i], i))]
+
+
+def rank_program(g, core, T, topo):
+    rank = T.rank_of(core)
+    if rank is None:
+        return
+    N = len(T.cores)
+    nxt, prv = T.cores[(rank + 1) % N], T.cores[(rank - 1) % N]
+    ops = []
+
+    def ap(s):
+        if isinstance(s, tuple):
+            if s[0] == "*":
+                return ap(s[1]).indirect(ap(s[2]))
+            ps = slice(None) if s[4] is None else slice(*s[4])
+            cs = slice(s[1], s[2]) if s[3] == 1 else slice(s[1], s[2], s[3])
+            return T[s[0]][ps, cs]
+        return s
+
+    def flat(l):
+        o = []
+        for s in l:
+            if isinstance(s, tuple):
+                o += [s[1], s[2]] if s[0] == "*" else [s]
+        return o
+
+    def add(eng, fn, rd, wr, cost, kind="c", sem=None, lat=0.0):
+        ops.append({"alt": {eng: (fn, cost)}, "r": flat(rd), "w": flat(wr), "k": kind, "sem": sem, "lat": lat})
+
+    def either():
+        o = ops.pop()
+        ops[-1]["alt"].update(o["alt"])
+        ops[-1]["r"] = ops[-1]["r"] + [s for s in o["r"] if s not in ops[-1]["r"]]
+
+    def ts(out, in0, s1, s2, o0, o1=None):
+        if o1 is None:
+            add("v", lambda: g.vector.tensor_scalar(ap(out), ap(in0), ap(s1), None, o0), [in0, s1], [out], _cost("v", out, in0))
+        else:
+            add("v", lambda: g.vector.tensor_scalar(ap(out), ap(in0), ap(s1), ap(s2), o0, o1), [in0, s1, s2], [out], _cost("v", out, in0))
+
+    def tt(out, a, b, op):
+        add("v", lambda: g.vector.tensor_tensor(ap(out), ap(a), ap(b), op), [a, b], [out], _cost("v", out, a, b))
+
+    def cp(out, a):
+        add("v", lambda: g.vector.tensor_copy(ap(out), ap(a)), [a], [out], _cost("v", out, a))
+
+    def ms(out, c):
+        add("v", lambda: g.vector.memset(ap(out), c), [], [out], _cost("v", out, out))
+
+    def scan(out, d0, d1, o0, o1):
+        add("v", lambda: g.vector.tensor_tensor_scan(ap(out), ap(d0), ap(d1), 0.0, o0, o1), [d0, d1], [out], _cost("v", out, d0))
+
+    def act(out, a, scale=1.0, bias=0.0, func=F.Identity, acc=None):
+        add("a", lambda: g.scalar.activation(ap(out), ap(a), func, bias=ap(bias), scale=ap(scale), accum_out=ap(acc)),
+            [a, scale, bias], [out, acc], _cost("a", out, a))
+
+    def lin(eng, out, a, scale=1.0, bias=0.0):
+        if "a" in eng:
+            act(out, a, scale, bias)
+        if "v" in eng:
+            if scale == 1.0 and bias == 0.0:
+                cp(out, a)
+            elif bias == 0.0:
+                ts(out, a, scale, None, A.mult)
+            else:
+                ts(out, a, scale, bias, A.mult, A.add)
+        if len(eng) == 2:
+            either()
+
+    def mm(groups):
+        def fn():
+            for out, terms in groups:
+                for n, (l, r) in enumerate(terms):
+                    ins = g.tensor.matmul(ap(out), ap(l), ap(r), n == 0, n == len(terms) - 1)
+            return ins
+        c = sum(max(min(64, _len(l)), _len(r)) * (4 if SCRATCH[l[0]][2] == F32 else 1) * PLAN["pe"] for _, terms in groups for l, r in terms)
+        add("p", fn, [x for _, terms in groups for t in terms for x in t], [o for o, _ in groups], c)
+
+    def iota(out, pat, base, cm):
+        if SCRATCH[out[0]][2] == I32:
+            add("g", lambda: g.iota(ap(out), pat, base, cm), [], [out], 130 + 1.66 * _len(out))
+        else:
+            add("g", lambda: g.iota(ap(out), pat, base, cm, allow_small_or_imprecise_dtypes=True), [], [out], 130 + 1.66 * _len(out))
+
+    def asel(out, a, pat, base, cm):
+        add("g", lambda: g.affine_select(ap(out), ap(a), pat, A.is_equal, 0.0, base, cm), [a], [out], 170 + 1.66 * _len(out))
+
+    ndma = [0]
+
+    def dma(q, out, a, kb, after=()):
+        sem = "dm%d" % ndma[0]
+        ndma[0] += 1
+        add(q, lambda: (g.sync if q == "s" else g.scalar).dma_start(ap(out), ap(a)), [a] + list(after), [out], 60.0 + 4.0 * kb, "d", (sem, 16), 1900.0)
+
+    def send(t, w, a, b):
+        rid, pid, _ = topo.addr(nxt)
+        m = topo.mask(core, nxt)
+        add("g", lambda: g.remote_dma(T["land%d" % t][:, a:b], T["snd%d" % (t - 1)][:, a:b], T.sem["arr%d%s" % (t, w)],
+                                      T.sem["out%d%s" % (t, w)], pid, rid, m),
+            [R("snd%d" % (t - 1), a, b)], [], 300.0, "r", ("out%d%s" % (t, w), len(topo.engines(core, nxt))), PLAN["hop"])
+
+    def recv(t, w, a, b):
+        add("x", None, [], [R("land%d" % t, a, b)], 0.0, "x", ("arr%d%s" % (t, w), len(topo.engines(prv, core))))
+
+    def col(k):
+        return R("cf", k, k + 1)
+    CJ, CG, CJ3, CJQ, CLO, CGG, CG15, CPC, CSI, CWM, CWP, CWR, CX8 = range(13)
+    MK, MQ, MB = 16, 20, 24
+
+    dma("s", R("ki", 0, 128), T.kid0[:], 64)
+    dma("a", R("ki", 128, 256), T.kid1[:], 64)
+    dma("s", R("bi", 0, 256), T.belts[:], 128)
+    dma("a", R("fi", 0, 128, 1, (0, 8)), T.flip[:], 4)
+    dma("s", R("ft", 4096, 5120), T.faces[:, 0:1024], 256)
+    dma("s", R("ft", 5120, 6144), T.faces[:, 1024:2048], 256)
+    dma("s", R("ft", 6144, 8192), T.faces[:], 512)
+
+    iota(R("pi", 0, 1), [[1, 1]], 0, 1)
+    iota(R("ramp", 0, 160), [[1, 160]], 0, 0)
+    iota(R("iv", 0, 128), [[-64, 8], [-2, 16]], 0, 0)
+    ms(R("oneb", 0, 160), 1.0)
+    ms(R("sc0", 0, 16), 0.0)
+    ms(R("sc1", 0, 16), 256.0)
+    ms(R("thr", 0, 16), 0.0)
+    pi = R("pi", 0, 1)
+    ts(R("ci", 0, 1), pi, 15, None, A.bitwise_and)
+    ts(R("ci", 1, 2), pi, 112, None, A.bitwise_and)
+    ts(R("ci", 2, 3), pi, 3, None, A.bitwise_and)
+    ts(R("ci", 3, 4), pi, 2, 3, A.arith_shift_right, A.bitwise_and)
+    ts(R("ci", 4, 5), pi, 2, 1, A.arith_shift_right, A.bitwise_and)
+    ts(R("ci", 5, 6), pi, 4, 1, A.arith_shift_right, A.bitwise_and)
+    cp(R("cf", 0, 6), R("ci", 0, 6))
+    asel(R("b8", 0, 144, 1, (0, 8)), R("oneb", 0, 144, 1, (0, 8)), [[1, 144]], -15, -16)
+    iota(R("pt0", 0, 256), [[16, 128], [-2048, 2]], 2048, 0)
+    ts(col(CSI), col(CG), col(CJQ), 12.0, A.add, A.add)
+    ts(R("cf", MK, MK + 4), R("ramp", 0, 4), col(CJ3), None, A.is_equal)
+    ts(col(CPC), col(CG), 4.0, col(CJ), A.mult, A.add)
+    ts(R("oh", 0, 144), R("ramp", 0, 144), col(CSI), None, A.is_equal)
+    lin("av", col(CG15), col(CG), 1.0, 15.0)
+    for a in range(4):
+        lin("av", R("si", 160 * a, 160 * a + 144), R("oh", 0, 144), col(MK + a))
+    for n, k in enumerate((0, -16, 1, -15, 2, -14)):
+        ts(R("im", 128 * n, 128 * n + 128), R("iv", 0, 128), col(CPC), float(k), A.add, A.is_equal)
+    ts(R("im", 512 + 15, 640, 16), R("iv", 15, 128, 16), col(CPC), -30.0, A.add, A.is_equal)
+    iota(R("neg", 0, 128), [[0, 128]], -1, 0)
+    iota(R("one", 0, 128), [[0, 128]], 1, 0)
+    asel(R("idp", 0, 160), R("oneb", 0, 160), [[1, 160]], -12, -1)
+    asel(R("shf", 0, 128), R("neg", 0, 128), [[-1, 128]], -1, 1)
+    asel(R("shf", 128, 256), R("neg", 0, 128), [[-1, 128]], 1, 1)
+    asel(R("shf", 15, 128, 16), R("neg", 0, 8), [[-16, 8]], 0, 1)
+    asel(R("shf", 128, 256, 16), R("neg", 0, 8), [[-16, 8]], -15, 1)
+    asel(R("nid", 0, 128), R("neg", 0, 128), [[1, 128]], 0, -1)
+    iota(R("ig", 0, 128), [[16, 8], [0, 16]], 0, 0)
+    iota(R("li", 0, 16), [[1, 8], [128, 2]], 0, 0)
+    iota(R("li", 16, 32), [[16, 2], [32, 8]], 0, 0)
+    iota(R("li", 32, 48), [[0, 8], [-256, 2]], 128, 0)
+    iota(R("li", 48, 64), [[-32, 2], [0, 8]], 16, 0)
+    for n, k in enumerate((0, -16, 1, -15, 2, -14)):
+        asel(R("fm", 128 * n, 128 * n + 128), R("one", 0, 128), [[32, 8], [1, 16]], -k, -2)
+    asel(R("fm", 512, 640, 16), R("one", 0, 8), [[32, 8]], 30, -2)
+
+    def to_val(dst, src, ti, tsh, te):
+        ts(ti, src, 1, None, A.bitwise_and)
+        ts(te, src, 0.5, None, A.add)
+        ts(tsh, ti, -1.0, 0.5, A.mult, A.add)
+        tt(dst, tsh, te, A.mult)
+
+    PIECE = (0, 256, 128, 384)
+
+    def hilo(src):
+        lin("av", R("hl", 0, 256), src)
+        tt(R("hl", 256, 512), src, R("hl", 0, 256), A.subtract)
+
+    def ext(w, i):
+        return R(w, 15 - i, 143 - i)
+
+    to_val(R("db", 0, 256), R("ki", 0, 256), R("t1", 0, 256), R("t2", 0, 256), R("t3", 0, 256))
+    cp(R("fb", 0, 128, 1, (0, 8)), R("fi", 0, 128, 1, (0, 8)))
+    hilo(R("db", 0, 256))
+    mm([(R("cn", 128, 136), [(R("b8", 15 - x, 143 - x, 1, (0, 8)), R("fb", x, 128, 16, (0, 8))) for x in range(16)])])
+    mm([(R("rb", 128 * a, 128 * a + 128),
+         [(R("si", 160 * a + 12 - 4 * r, 160 * a + 140 - 4 * r), R("hl", PIECE[r], PIECE[r] + 128)) for r in range(4)])
+        for a in range(4)])
+    ts(R("cf", MB, MB + 4), R("cf", MK, MK + 4), col(CLO), 0.25, A.mult, A.mult)
+    to_val(R("bv", 0, 256), R("bi", 0, 256), R("t4", 0, 256), R("t5", 0, 256), R("t6", 0, 256))
+    mm([(R("z0", 128 * n, 128 * n + 128), [(R("im", 256 * n + 128 * b, 256 * n + 128 * b + 128), R("bv", b, 256, 2)) for b in range(2)])
+        for n in range(3)])
+    for a in (0, 1024):
+        lin("av", R("ft", 2047 - a, 1023 if a == 0 else None, -1), R("ft", 4096 + a, 5120 + a), -1.0, 255.0)
+        lin("av", R("ft", 4095 - a, 3071 - a, -1), R("ft", 4096 + a, 5120 + a), -1.0, 255.0)
+    for jl in range(4):
+        lin("av", R("kt", 512 * jl, 512 * jl + 512), R("rb", 0, 512), col(MK + jl), col(MB + jl))
+    dma("s", T.yx[:, 0:2048], T.faces[:], 512, after=[R("kt", 0, 2048)])
+    ts(R("pt0", 0, 256), R("pt0", 0, 256), col(CJ), None, A.add)
+    cp(R("sc0", 1, 16, 2), R("cn", 128, 136))
+    lin("av", R("land0", 0, 8), R("cn", 128, 136))
+    lin("av", R("sc1", 1, 16, 2), R("pt0", 1, 16, 2))
+    ts(col(CWM), col(CJ), 7.5, 0.5, A.is_lt, A.subtract)
+    scan(R("sco", 0, 16), R("sc0", 0, 16), R("sc1", 0, 16), A.mult, A.add)
+    ts(R("bc", 0, 144), R("ramp", 0, 144), col(CG15), None, A.is_equal)
+    cp(R("ofb", 0, 8), R("sco", 1, 16, 2))
+    lin("av", R("cand", 0, 256), R("z0", 0, 256), 1.0, 0.25)
+    lin("av", R("cand", 256, 512), R("z0", 128, 384), 1.0, 0.25)
+    lin("av", R("cm", 0, 144), R("bc", 0, 144), col(CWM))
+    lin("av", R("land0", 8, 136), IND(R("cand", 0, 384), R("ofb", 0, 8)))
+    lin("av", R("cd", 0, 144), R("bc", 0, 144), -0.5 if PLAN["sign"] else -1.0)
+    lin("av", R("land0", 136, 264), IND(R("cand", 128, 512), R("ofb", 0, 8)))
+
+    def late_constants():
+        lin("av", R("nw", 128, 256), R("pt0", 0, 256, 2), 1.0, 0.5)
+        ms(R("nw", 256, 512, 2), 0.0)
+        ts(R("wm", 0, 128), R("ig", 0, 128), col(CG), None, A.is_equal)
+        lin("av", R("i32", 0, 128), R("idp", 12, 140), 32.0)
+        ts(R("cf", CWP, CWP + 1), col(CJ), 7.5, None, A.is_lt)
+        ts(R("cf", CWR, CWR + 1), col(CJ), 7.5, None, A.is_gt)
+        lin("av", R("cp", 0, 144), R("bc", 0, 144), col(CWP))
+        lin("av", R("cr", 0, 144), R("bc", 0, 144), col(CWR))
+        lin("av", R("hid", 0, 128), R("idp", 12, 140), 0.5)
+        ts(R("cf", MQ, MQ + 4), R("ramp", 0, 4), col(CJQ), None, A.is_equal)
+
+    def later_constants():
+        for a in range(4):
+            lin("av", R("su", 160 * a, 160 * a + 160), R("idp", 0, 160), col(MQ + a))
+
+    def last_constants():
+        cp(R("kf", 0, 256), R("ki", 0, 256))
+        dma("s", T.y0[:, 0:2048], R("kf", 0, 128), 64, after=[R("kt", 0, 2048)])
+        dma("s", T.y1[:, 0:2048], R("kf", 128, 256), 64, after=[R("kt", 0, 2048)])
+        ts(col(CX8), col(CJ), 8.0, None, A.mult)
+        ts(R("lt", 16, 32), R("li", 48, 64), col(CGG), col(CJ), A.mult, A.add)
+        ts(R("lt", 0, 16), R("li", 32, 48), col(CGG), col(CX8), A.mult, A.add)
+        tt(R("lt", 0, 32), R("lt", 0, 32), R("li", 0, 32), A.add)
+        cp(R("lu", 0, 32), R("lt", 0, 32))
+
+    FT = R("ft", 0, 8192)
+    GO = R("nw", 257, 512, 2)
+    PR = R("db", 256, 512)
+
+    def gather(eng, out, a, b, win, offbuf, off0, scale=1.0, bias=0.0, base=0):
+        lin(eng, R(out, base + a, base + b), IND(win, R(offbuf, off0 + a // 16, off0 + b // 16)), scale, bias)
+
+    def prep(t):
+        L = "land%d" % t
+        K = R(L, 8, 136)
+        if t > 0:
+            recv(t, "k", 0, 136)
+            recv(t, "h", 136, 264)
+        ts(R("ofh", 0, 128), R(L, 136, 264), 4095.5, None, A.add)
+        if PLAN["sign"]:
+            act(R("s2", 0, 128), K, 1.0, 0.0, F.Sign)
+            act(R("ab", 0, 128), K, 0.5, 0.0, F.Abs)
+        else:
+            ts(R("s2", 0, 128), K, 0.0, 0.5, A.is_gt, A.subtract)
+            tt(R("ab", 0, 128), R("s2", 0, 128), K, A.mult)
+            act(R("ab", 0, 128), K, 0.5, 0.0, F.Abs)
+            either()
+        if t == 0:
+            ts(R("abi", 0, 128), R("ab", 0, 128), 2.0, -0.5, A.mult, A.add)
+            ts(R("abi", 0, 128), R("abi", 0, 128), 2047, None, A.bitwise_and)
+            cp(R("ofk", 0, 128), R("abi", 0, 128))
+        else:
+            ts(R("ofk", 0, 128), R("ab", 0, 128), 2.0, -0.5, A.mult, A.add)
+
+    def visit(t):
+        L, S, last = "land%d" % t, "snd%d" % t, t == 3
+        KT = R("kt", 0, 2048 if t == 0 else 4096)
+        yb = 2048 * (t + 1)
+        FF, K, H, KH = R(L, 0, 8), R(L, 8, 136), R(L, 136, 264), R(L, 8, 264)
+        FN = R(S, 0, 8)
+
+        def kid(e, a, b):
+            gather(e, "g1", a, b, KT, "ofk", 0)
+
+        def fw(e, a, b):
+            gather(e, "fw", a, b, FT, "ofh", 0)
+
+        def extract(c):
+            X = "xa" if c == 0 else "xb"
+            mm([(R(X, 64 * n, 64 * n + 64), [(ext(w, i), R("g1", 1024 * c + i, 1024 * c + 1024, 16)) for i in range(16)])
+                for n, w in enumerate(("cd", "cm"))])
+
+        def kids_of(c):
+            X = "xa" if c == 0 else "xb"
+            lo, hi = 64 * c, 64 * c + 64
+            tt(R("sd", lo, hi), R(X, 0, 64), R("s2", lo, hi), A.mult)
+            tt(R("uu", lo, hi), R(X, 64, 128), R("sd", lo, hi), A.add)
+            tt(R("nw", lo, hi), R(X, 64, 128), R("sd", lo, hi), A.subtract)
+            ts(R("ofu", lo, hi), R("uu", lo, hi), 4095.5, None, A.add)
+
+        def diff(a, b):
+            tt(R("dd", a, b), IND(FT, R("ofu", a // 16, b // 16)), R("fw", a, b), A.subtract)
+
+        def near(a, b):
+            ts(R("ind", a, b), R("dd", a, b), C32, C32, A.add, A.is_equal)
+
+        def count(c):
+            mm([(R("cn", 64 * c, 64 * c + 64), [(ext("bc", i), R("ind", 1024 * c + i, 1024 * c + 1024, 16)) for i in range(16)])])
+
+        def q_(n, q):
+            return R(n, 512 * q, 512 * q + 512)
+        ID, HID, NID = R("idp", 12, 140), R("hid", 0, 128), R("nid", 0, 128)
+
+        def mean(q, own):
+            mm([(R("z%d" % (q % 2), 0, 512), [(HID, q_("dd", q)), (HID if own else ID, q_("fw", q))])])
+
+        def rnd(q):
+            lin("av", R("yv", yb + 512 * q, yb + 512 * q + 512), R("z%d" % (q % 2), 0, 512), 1.0 - 2.0 ** -10, CY)
+
+        def values(q):
+            if q in PLAN["own"]:
+                X = R("xa" if q % 2 == 0 else "xb", 0, 512)
+                gather("a", "dd", 512 * q, 512 * q + 512, FT, "ofu", 0)
+                mm([(X, [(ID, q_("dd", q)), (NID, q_("fw", q))])])
+                ts(q_("ind", q), X, C32, C32, A.add, A.is_equal)
+            else:
+                diff(512 * q, 512 * q + 512)
+                near(512 * q, 512 * q + 512)
+
+        GQ = PLAN["gq"]
+        for a in range(0, 2048, GQ):
+            kid("av", a, a + GQ)
+        extract(0)
+        extract(1)
+        mm([(R("rb", 0, 128), [(R("shf", 0, 128), K)]), (R("rb", 128, 256), [(R("shf", 128, 256), H)])])
+        for a in range(0, 2048, GQ):
+            fw("av", a, a + GQ)
+        kids_of(0)
+        kids_of(1)
+        if t == 0:
+            late_constants()
+            for n, w in enumerate(("cp", "cr")):
+                mm([(R("db", 256 + 128 * n, 384 + 128 * n), [(ext(w, i), R("kt", i, 2048, 16)) for i in range(16)])])
+        for q in range(4):
+            values(q)
+        count(0)
+        count(1)
+        lin("av", R("sc1", 0, 16, 2), FF, 256.0, 256.0)
+        tt(R("db", 0, 256), R("nw", 0, 256), KH, A.subtract)
+        if t > 0:
+            act(R("thr", 8, 16), R("cn", 136, 144), -1.0, 0.0, F.Identity, R("thr", 1, 2))
+            lin("av", R("thr", 2, 3), R("thr", 1, 2), 1.0, C2)
+            lin("av", R("thr", 3, 4), R("thr", 2, 3), 1.0, -C2)
+            act(R("thr", 0, 1), R("thr", 3, 4), -1.0, R("thr", 1, 2), F.Abs)
+        lin("av", R("cand", 384, 640), R("rb", 0, 256))
+        lin("av", R("cand", 256, 384), H, -1.0)
+        lin("av", R("cand", 640, 768), K, -1.0)
+        tt(R("dpr", 0, 128), R("uu", 0, 128), R("db", 256, 384), A.subtract)
+        tt(R("dpr", 128, 256), H, R("db", 384, 512), A.subtract)
+        ts(R("spl", 0, 128), R("cn", 0, 128), R("thr", 0, 1), 8.5, A.subtract, A.is_ge)
+        mm([(R("cn", 128, 136), [(ext("bc", x), R("spl", x, 128, 16)) for x in range(16)])])
+        mm([(R("rb", 0, 128), [(R("wm", 0, 128), R("spl", 0, 128)), (R("i32", 0, 128), R("spl", 0, 128))])])
+        for q in range(4):
+            mean(q, q in PLAN["own"])
+            rnd(q)
+        if t == 0:
+            later_constants()
+            for a in range(0, 2048, 512):
+                lin("av", R("yv", a, a + 512), R("ft", 4096 + a, 4608 + a), 1.0, CY)
+        tt(R("db", 0, 128), R("db", 0, 128), R("spl", 0, 128), A.mult)
+        tt(R("db", 128, 256), R("db", 128, 256), R("spl", 0, 128), A.mult)
+        ts(R("sc0", 1, 16, 2), R("cn", 128, 136), 4.5, None, A.is_lt)
+        tt(R("cand", 0, 256), R("db", 0, 256), KH, A.add)
+        scan(R("sco", 0, 16), R("sc0", 0, 16), R("sc1", 0, 16), A.mult, A.add)
+        tt(FN, FF, R("sc0", 1, 16, 2), A.not_equal)
+        cp(R("ofb", 0, 8), R("sco", 1, 16, 2))
+        OFF = R("ofb", 0, 8)
+        lin("av", R(S, 8, 136), IND(R("cand", 0, 640), OFF))
+        lin("av", R(S, 136, 264), IND(R("cand", 128, 768), OFF))
+        if not last:
+            send(t + 1, "k", 0, 136)
+            send(t + 1, "h", 136, 264)
+            mm([(R("cn", 136, 144), [(R("one", 0, 128), R("sc0", 1, 16, 2))])])
+        pa, pb = ("pt0", "pt1") if t % 2 == 0 else ("pt1", "pt0")
+        YV = R("yv", 0, yb + 2048)
+
+        def pointers():
+            ts(GO, R("rb", 0, 128), 36.5, None, A.is_ge)
+            scan(R(pb, 0, 256), R("nw", 256, 512), R(pa, 0, 256), A.mult, A.max)
+            tt(R("dpr", 0, 128), GO, R("dpr", 0, 128), A.mult)
+            cp(R("ptu", 0, 128), R(pb, 1, 256, 2))
+            if not last:
+                lin("av", R(pb, 0, 256, 2), R(pb, 0, 256, 2), 1.0, 2048.0)
+
+        def select(e, a, b):
+            gather(e, "ft", a, b, YV, "ptu", 0, 1.0, -CY, 6144)
+            if last:
+                dma("s", T.yx[:, 2048 + a:2048 + b], R("ft", 6144 + a, 6144 + b), (b - a) // 4)
+
+        def turn(a, b):
+            lin("av", R("ft", 2047 - a, (2047 - b) if b < 2048 else None, -1), R("ft", 6144 + a, 6144 + b), -1.0, 255.0)
+
+        def kids_new(out):
+            tt(R("dpr", 128, 256), GO, R("dpr", 128, 256), A.mult)
+            tt(out, PR, R("dpr", 0, 256), A.add)
+
+        if not last:
+            pointers()
+            for a in range(0, 2048, PLAN["sq"]):
+                select("av", a, a + PLAN["sq"])
+                turn(a, a + PLAN["sq"])
+            kids_new(PR)
+            hilo(PR)
+            for h, B in enumerate(("xa", "rb")):
+                mm([(R(B, a, 256, 4), [(R("su", 160 * a + 12 + 4 * a - 4 * r, 160 * a + 140 + 4 * a - 4 * r),
+                                        R("hl", PIECE[r] + 64 * h, PIECE[r] + 64 * h + 64)) for r in range(4)]) for a in range(4)])
+            for jl in range(4):
+                lin("av", R("kt", 2048 + jl, 3072, 4), R("xa", 0, 256), col(MK + jl))
+            for jl in range(4):
+                lin("av", R("kt", 3072 + jl, 4096, 4), R("rb", 0, 256), col(MK + jl))
+            prep(t + 1)
+            if t == 1:
+                last_constants()
+        else:
+            fk, fh = R(S, 8, 136), R(S, 136, 264)
+
+            def fm(n):
+                return R("fm", 128 * n, 128 * n + 128)
+            mm([(R("xa", 0, 128), [(fm(0), fk), (fm(2), fh)]), (R("xa", 128, 256), [(fm(2), fk), (fm(4), fh)]),
+                (R("xa", 256, 384), [(fm(1), fk), (fm(3), fh)]), (R("xa", 384, 512), [(fm(3), fk), (fm(5), fh)])])
+            pointers()
+            for a in range(0, 2048, 512):
+                select("av", a, a + 512)
+            kids_new(R("old", 256, 512))
+            lin("av", R("fnb", 0, 8), FN)
+            lin("av", R("lf", 0, 8), FN, 128.0)
+            lin("av", R("tr0", 0, 256), IND(R("old", 256, 512), R("lu", 0, 16)))
+            mm([(R("xb", x, 128, 16, (0, 8)), [(R("idp", 12 + x, 140, 16), R("fnb", 0, 8))]) for x in range(16)])
+            tt(R("lf", 0, 8), R("lf", 0, 8), R("sc1", 1, 16, 2), A.add)
+            add("v", lambda: g.vector.transpose(ap(R("tr1", 0, 256)), ap(R("tr0", 0, 256))), [R("tr0", 0, 256)], [R("tr1", 0, 256)], 262.0)
+            cp(R("lfu", 0, 8), R("lf", 0, 8))
+            lin("av", R("hy", 0, 512), R("xa", 0, 512))
+            lin("av", R("tr2", 0, 256), IND(R("tr1", 0, 256), R("lu", 16, 32)), 2.0, -1.0)
+            lin("av", R("nw", 0, 256), R("tr2", 0, 256), -1.0, -1.0)
+            for b in range(2):
+                lin("av", R("yb1", b, 256, 2), IND(R("hy", 256 * b, 256 * b + 256), R("lfu", 0, 8)), 2.0, -1.0)
+            tt(R("tr3", 0, 256), R("nw", 0, 256), R("tr2", 0, 256), A.max)
+            dma("s", T.y0[:, 2048:4096], R("tr3", 0, 128), 64)
+            for gq in range(8):
+                dma("s", T.y1[gq ^ 1, 2048:4096], R("tr3", 128, 256, 1, (16 * gq, 16 * gq + 16)), 8)
+            lin("av", R("db", 0, 256), R("yb1", 0, 256), -1.0, -1.0)
+            tt(R("yb2", 0, 256), R("db", 0, 256), R("yb1", 0, 256), A.max)
+            lin("av", R("yfo", 0, 128, 1, (0, 8)), R("xb", 0, 128, 1, (0, 8)))
+            dma("s", T.yb[:], R("yb2", 0, 256), 128)
+            dma("s", T.yf[:], R("yfo", 0, 128, 1, (0, 8)), 4)
+
+    prep(0)
+    for t in range(4):
+        visit(t)
+
+    key = repr(sorted(PLAN.items()))
+    if key not in _PLANS:
+        edges = _edges(ops)
+        _PLANS[key] = (edges, _plan(ops, edges))
+    edges, order = _PLANS[key]
+    pos = {i: n for n, (i, _) in enumerate(order)}
+    for i, e in order:
+        ops[i]["e"] = e
+        ops[i]["fn"] = ops[i]["alt"][e][0]
+        ops[i]["pre"] = edges[i]
+    ops = [ops[i] for i, _ in order]
+    bank = {}
+    for n, o in enumerate(ops):
+        deps = set()
+        for j, raw in o["pre"].items():
+            deps.add(pos[j])
+        for s in o["r"] + o["w"]:
+            if s[0] in PSUM:
+                deps.update(n2 for e2, n2 in bank.setdefault(s[0], {}).items() if e2 != o["e"])
+        for s in o["r"] + o["w"]:
+            if s[0] in PSUM:
+                bank[s[0]][o["e"]] = n
+        newest = {}
+        for d in deps:
+            k = ops[d]["e"] if ops[d]["k"] == "c" else d
+            newest[k] = max(newest.get(k, -1), d)
+        o["deps"] = sorted(newest.values())
+    seen = {}
+    for o in ops:
+        keep = []
+        for d in o["deps"]:
+            k = (o["e"], ops[d]["e"] if ops[d]["k"] == "c" else d)
+            if seen.get(k, -1) < d:
+                seen[k] = d
+                keep.append(d)
+                ops[d]["need"] = True
+        o["deps"] = keep
+    cnt = {"v": 0, "a": 0, "p": 0, "g": 0}
+    for o in ops:
+        if o["k"] == "c" and o.get("need"):
+            cnt[o["e"]] += 1
+            o["sem"] = ("e" + o["e"], cnt[o["e"]])
+    Q = {"v": g.vector, "a": g.scalar, "p": g.tensor, "g": g, "s": g.sync}
+    for o in ops:
+        if o["k"] == "x":
+            continue
+        for d in o["deps"]:
+            Q[o["e"]].wait_ge(T.sem[ops[d]["sem"][0]], ops[d]["sem"][1])
+        ins = o["fn"]()
+        if o["k"] == "d":
+            ins.then_inc(T.sem[o["sem"][0]], 16)
+        elif o["k"] == "c" and o.get("need"):
+            ins.then_inc(T.sem[o["sem"][0]], 1)
+    for o in ops:
+        if o["k"] in "dr" and not o.get("need"):
+            (g if o["k"] == "r" else g.sync).wait_ge(T.sem[o["sem"][0]], o["sem"][1])

@@ -16,16 +16,16 @@ for _n, _w, _d in [
     ("kf", 256, F32), ("ramp", 160, F32), ("iv", 128, F32), ("ig", 128, F32), ("pi", 8, I32), ("ci", 8, I32),
     ("cf", 32, F32), ("bc", 144, BF), ("cm", 144, BF), ("cd", 144, BF), ("cp", 144, BF), ("cr", 144, BF),
     ("b8", 144, BF), ("idp", 160, BF), ("nid", 128, BF), ("hid", 128, BF), ("wm", 128, BF), ("i32", 128, BF), ("si", 640, BF), ("su", 640, BF),
-    ("oh", 144, BF), ("im", 768, F32), ("fm", 768, F32), ("shf", 256, F32), ("one", 160, F32), ("neg", 128, F32), ("oneb", 160, BF),
+    ("oh", 144, BF), ("im", 768, F32), ("fm", 768, F32), ("shf", 256, F32), ("one", 160, F32), ("neg", 256, F32), ("oneb", 160, BF),
     ("li", 64, F32), ("lt", 32, F32), ("lu", 32, U16), ("tr0", 256, F32), ("tr1", 256, F32), ("tr2", 256, F32),
-    ("tr3", 256, F32), ("fin", 256, F32), ("hy", 512, F32), ("lf", 8, F32), ("lfu", 8, U16), ("yb1", 256, F32),
+    ("tr3", 256, F32), ("fin", 256, F32), ("hy", 1024, F32), ("lf", 8, F32), ("lfu", 8, U16), ("yb1", 256, F32),
     ("yb2", 256, F32), ("yfo", 128, F32),
 ]:
     SCRATCH[_n] = ("sbuf", [128, _w], _d)
 PSUM = ["xa", "xb", "z0", "z1", "cn", "nw", "db", "rb"]
 for _n in PSUM:
     SCRATCH[_n] = ("psum", [128, 512], F32)
-NDMA = 30
+NDMA = 34
 SEMAPHORES = (["ev", "ea", "ep", "eg"] + ["%s%d%s" % (_a, _t, _b) for _a in ("arr", "out") for _t in (1, 2, 3) for _b in "kh"]
               + ["dm%d" % _i for _i in range(NDMA)])
 
@@ -49,7 +49,8 @@ def _mask(s):
     return m
 
 
-PLAN = {"pe": 0.42, "gat": 1.56, "hop": 2600.0, "wake": 60.0, "seed": 1, "mean": 0.1, "sign": 1, "steps": 30000, "heat": 120.0, "own": (2, 3), "gq": 512, "sq": 512}
+PLAN = {"pe": 0.42, "gat": 1.56, "hop": 4000.0, "wake": 90.0, "ov": 60, "oa": 100, "pec": 0, "crit": 0.3, "due": 0.0, "early": ("yv",), "big": 1, "tq": 1024,
+        "fq": ((0, 512), (512, 1024), (1024, 1536), (1536, 2048)), "seed": 1, "mean": 0.1, "sign": 1, "steps": 44000, "heat": 250.0, "own": (3,), "gq": 512, "sq": 512}
 _PLANS = {}
 
 
@@ -62,13 +63,13 @@ def _len(s):
 def _cost(e, out, a, b=None):
     n = _len(out)
     if a[0] == "*":
-        return (50 if e == "v" else 65) + n * PLAN["gat"] * 0.83
+        return PLAN["ov" if e == "v" else "oa"] + n * PLAN["gat"] * 0.83
     k = 1.0
     if b is not None:
         k = 1.0 if a[0] in PSUM or b[0] in PSUM else 2.0
     elif e == "v" and SCRATCH[out[0]][2] in (BF, U16) and SCRATCH[a[0]][2] in (BF, U16):
         k = 0.5
-    return (50 if e == "v" else 65) + max(64, n * k) * 0.83
+    return PLAN["ov" if e == "v" else "oa"] + max(64, n * k) * 0.83
 
 
 def _edges(ops):
@@ -109,14 +110,17 @@ def _plan(ops, edges):
     cost = [{e: c for e, (_, c) in o["alt"].items()} for o in ops]
     lat = [o["lat"] + wake for o in ops]
     banks = [sorted(b) for b in banks]
+    why = [-1] * n
+    lastw = max(i for i in range(n) if ops[i]["k"] == "r")
+    due = [PLAN["due"] if i < lastw and any(s[0] in PLAN["early"] for s in o["w"]) else 0.0 for i, o in enumerate(ops)]
 
     def place(seq, eng, base, start, end):
         busy = {k: list(v) for k, v in base.items()}
         for i in seq:
-            t = 0.0
+            t, y = 0.0, -1
             for j in pre[i]:
                 if end[j] > t:
-                    t = end[j]
+                    t, y = end[j], j
             e = eng[i]
             c = cost[i][e]
             mine = busy.setdefault(e, [])
@@ -126,23 +130,24 @@ def _plan(ops, edges):
                 while k and mine[k - 1][1] > t:
                     k -= 1
                 while k < len(mine) and mine[k][0] < t + c:
-                    t = mine[k][1]
+                    t, y = mine[k][1], mine[k][2]
                     k += 1
                 for b in banks[i]:
-                    for s0, s1, e2 in reversed(busy.setdefault(b, [])):
+                    for s0, s1, e2, j in reversed(busy.setdefault(b, [])):
                         if e2 != e and s1 + wake > t and s0 < t + c + wake:
-                            t = s1 + wake
+                            t, y = s1 + wake, j
                 if t == t1 or not banks[i]:
                     break
-            mine.insert(k, (t, t + c))
+            mine.insert(k, (t, t + c, i))
+            why[i] = y
             for b in banks[i]:
-                busy[b].append((t, t + c, e))
+                busy[b].append((t, t + c, e, i))
             start[i], end[i] = t, t + c + lat[i]
-        return max(end[i] for i in seq) + PLAN["mean"] * sum(end[i] for i in seq) / len(seq), busy
+        return max(end[i] + due[i] for i in seq) + PLAN["mean"] * sum(end[i] for i in seq) / len(seq), busy
 
     part, left = [], set(range(n))
     for w in [i for i in range(n) if ops[i]["k"] == "r"][1::2]:
-        mine, todo = set(), [w - 1, w]
+        mine, todo = set(), [w - 1, w] + [i for i in range(w) if due[i]]
         while todo:
             i = todo.pop()
             if i in left:
@@ -154,27 +159,38 @@ def _plan(ops, edges):
     rng = np.random.RandomState(PLAN["seed"])
     eng = [("a" if "a" in c else list(c)[0]) for c in cost]
     start, end, base = [0.0] * n, [0.0] * n, {}
-    for mine in part:
-        seq = sorted(mine, key=lambda i: (-prio[i], i))
+    seq = []
+    for w in range(len(part) - 1):
+        mine, fixed = part[w] | part[w + 1], part[w] if w < len(part) - 2 else part[w] | part[w + 1]
+        seq = [i for i in seq if i in mine]
+        seq += sorted(mine - set(seq), key=lambda i: (i not in part[w], -prio[i], i))
         m = len(seq)
         flex = [i for i in seq if len(cost[i]) > 1]
         best, _ = place(seq, eng, base, start, end)
         top = (best, seq, list(eng))
         steps = PLAN["steps"]
-        rnd = rng.rand(steps, 5).tolist()
+        rnd = rng.rand(steps, 6).tolist()
+
+        def chain():
+            i, c = max(mine, key=lambda i: end[i] + due[i]), []
+            while i in mine:
+                c.append(i)
+                i = why[i]
+            return c, [i for i in c if len(cost[i]) > 1] or flex
+        crit, cflex = chain()
         for it in range(steps):
-            r0, r1, r2, r3, r4 = rnd[it]
+            r0, r1, r2, r3, r4, r5 = rnd[it]
             s2, e2 = seq, eng
             if r0 < 0.35:
                 e2 = list(eng)
-                i = flex[int(r1 * len(flex))]
+                i = cflex[int(r1 * len(cflex))] if r5 < PLAN["crit"] else flex[int(r1 * len(flex))]
                 e2[i] = "v" if eng[i] == "a" else "a"
                 j = flex[int(r2 * len(flex))]
                 if r3 < 0.5 and eng[j] != eng[i]:
                     e2[j] = eng[i]
             else:
                 s2 = list(seq)
-                p = int(r1 * m)
+                p = seq.index(crit[int(r1 * len(crit))]) if r5 < PLAN["crit"] else int(r1 * m)
                 i = s2.pop(p)
                 q = p
                 if r2 < 0.5:
@@ -191,14 +207,18 @@ def _plan(ops, edges):
             v, _ = place(s2, e2, base, start, end)
             if v <= best + PLAN["heat"] * (1.0 - it / steps) * r4:
                 best, seq, eng = v, s2, e2
+                crit, cflex = chain()
                 if v < top[0]:
                     top = (v, s2, list(e2))
         _, seq, eng = top
         v, busy = place(seq, eng, base, start, end)
-        base = {k: [x for x in l if x[1] > v - 12000.0] for k, l in busy.items()}
-        for k in "vapgs":
-            base[k] = [(0.0, max(0.0, v - 12000.0))] + base.get(k, [])
-    return [(i, eng[i]) for i in sorted(range(n), key=lambda i: (start[i], i))]
+        v = max(end[i] for i in fixed)
+        base = {k: [x for x in l if (x[1] > v - 12000.0 or k in "gs") and x[-1] not in part[w + 1] and x[-1] >= 0] for k, l in busy.items()}
+        for k in "vap":
+            base[k] = [(0.0, max(0.0, v - 12000.0), -1)] + base.get(k, [])
+    order = sorted(range(n), key=lambda i: (start[i], i))
+    loads = [i for i in range(n) if ops[i]["k"] == "d" and not edges[i]]
+    return [(i, eng[i]) for i in loads + [i for i in order if i not in loads]]
 
 
 def rank_program(g, core, T, topo):
@@ -283,15 +303,23 @@ def rank_program(g, core, T, topo):
         else:
             add("g", lambda: g.iota(ap(out), pat, base, cm, allow_small_or_imprecise_dtypes=True), [], [out], 130 + 1.66 * _len(out))
 
-    def asel(out, a, pat, base, cm):
-        add("g", lambda: g.affine_select(ap(out), ap(a), pat, A.is_equal, 0.0, base, cm), [a], [out], 170 + 1.66 * _len(out))
+    def asel(out, a, pat, base, cm, op=A.is_equal):
+        add("g", lambda: g.affine_select(ap(out), ap(a), pat, op, 0.0, base, cm), [a], [out], 170 + 1.66 * _len(out))
+
+    def band(out, a, pat, cm, lo, hi):
+        asel(out, a, pat, -lo, cm, A.is_ge)
+        asel(out, out, [[-s, c] for s, c in pat], hi, -cm, A.is_ge)
 
     ndma = [0]
 
     def dma(q, out, a, kb, after=()):
         sem = "dm%d" % ndma[0]
         ndma[0] += 1
-        add(q, lambda: (g.sync if q == "s" else g.scalar).dma_start(ap(out), ap(a)), [a] + list(after), [out], 60.0 + 4.0 * kb, "d", (sem, 16), 1900.0)
+        if q == "g":
+            add(q, lambda: g.dma_start(ap(out), ap(a), accum_op=A.add), [out] + list(after), [out], 1000.0, "d", (sem, 16), 1900.0 + 8.0 * kb)
+        else:
+            add(q, lambda: (g.sync if q == "s" else g.scalar).dma_start(ap(out), ap(a)), [a] + list(after), [out],
+                60.0 + (4.0 * kb if q == "s" else 0.0), "d", (sem, 16), 1900.0 + (4.0 * kb if q == "a" else 0.0))
 
     def send(t, w, a, b):
         rid, pid, _ = topo.addr(nxt)
@@ -337,7 +365,9 @@ def rank_program(g, core, T, topo):
     ts(R("cf", MK, MK + 4), R("ramp", 0, 4), col(CJ3), None, A.is_equal)
     ts(col(CPC), col(CG), 4.0, col(CJ), A.mult, A.add)
     ts(R("oh", 0, 144), R("ramp", 0, 144), col(CSI), None, A.is_equal)
-    lin("av", col(CG15), col(CG), 1.0, 15.0)
+    for w, lo, hi in (("bc", 0, 15), ("cp", 0, 7), ("cr", 8, 15)):
+        iota(R(w, 0, 144), [[0, 144]], 0, 0)
+        band(R(w, 15, 143, 16), R("oneb", 0, 8), [[-16, 8]], 1, lo, hi)
     for a in range(4):
         lin("av", R("si", 160 * a, 160 * a + 144), R("oh", 0, 144), col(MK + a))
     for n, k in enumerate((0, -16, 1, -15, 2, -14)):
@@ -351,7 +381,16 @@ def rank_program(g, core, T, topo):
     asel(R("shf", 15, 128, 16), R("neg", 0, 8), [[-16, 8]], 0, 1)
     asel(R("shf", 128, 256, 16), R("neg", 0, 8), [[-16, 8]], -15, 1)
     asel(R("nid", 0, 128), R("neg", 0, 128), [[1, 128]], 0, -1)
-    iota(R("ig", 0, 128), [[16, 8], [0, 16]], 0, 0)
+    if PLAN["pec"]:
+        asel(R("neg", 128, 256), R("neg", 0, 128), [[1, 128]], 0, -1)
+    band(R("wm", 0, 128), R("oneb", 0, 128), [[-16, 8], [0, 16]], 1, 0, 15)
+    for w, c in (("i32", 32), ("hid", 2)):
+        iota(R(w, 0, 128), [[0, 128]], c, 0)
+        asel(R(w, 0, 128), R(w, 0, 128), [[1, 128]], 0, -1)
+    for a in range(4):
+        band(R("su", 160 * a, 160 * a + 160), R("idp", 0, 160), [[0, 10], [1, 16]], 0, (4 * a - 4) % 16, (4 * a - 4) % 16 + 3)
+    for a in range(0, 2048, 512):
+        iota(R("yv", a, a + 512), [[0, 512]], int(CY), 0)
     iota(R("li", 0, 16), [[1, 8], [128, 2]], 0, 0)
     iota(R("li", 16, 32), [[16, 2], [32, 8]], 0, 0)
     iota(R("li", 32, 48), [[0, 8], [-256, 2]], 128, 0)
@@ -379,26 +418,28 @@ def rank_program(g, core, T, topo):
     cp(R("fb", 0, 128, 1, (0, 8)), R("fi", 0, 128, 1, (0, 8)))
     hilo(R("db", 0, 256))
     mm([(R("cn", 128, 136), [(R("b8", 15 - x, 143 - x, 1, (0, 8)), R("fb", x, 128, 16, (0, 8))) for x in range(16)])])
-    mm([(R("rb", 128 * a, 128 * a + 128),
-         [(R("si", 160 * a + 12 - 4 * r, 160 * a + 140 - 4 * r), R("hl", PIECE[r], PIECE[r] + 128)) for r in range(4)])
-        for a in range(4)])
+    for h, B in enumerate(("rb", "xa")):
+        mm([(R(B, 128 * (a % 2), 128 * (a % 2) + 128),
+             [(R("si", 160 * a + 12 - 4 * r, 160 * a + 140 - 4 * r), R("hl", PIECE[r], PIECE[r] + 128)) for r in range(4)])
+            for a in (2 * h, 2 * h + 1)])
     ts(R("cf", MB, MB + 4), R("cf", MK, MK + 4), col(CLO), 0.25, A.mult, A.mult)
     to_val(R("bv", 0, 256), R("bi", 0, 256), R("t4", 0, 256), R("t5", 0, 256), R("t6", 0, 256))
     mm([(R("z0", 128 * n, 128 * n + 128), [(R("im", 256 * n + 128 * b, 256 * n + 128 * b + 128), R("bv", b, 256, 2)) for b in range(2)])
         for n in range(3)])
     for a in (0, 1024):
-        lin("av", R("ft", 2047 - a, 1023 if a == 0 else None, -1), R("ft", 4096 + a, 5120 + a), -1.0, 255.0)
         lin("av", R("ft", 4095 - a, 3071 - a, -1), R("ft", 4096 + a, 5120 + a), -1.0, 255.0)
+        dma("s", R("ft", 1024 - a, 2048 - a), R("ft", 3072 - a, 4096 - a), 256)
     for jl in range(4):
-        lin("av", R("kt", 512 * jl, 512 * jl + 512), R("rb", 0, 512), col(MK + jl), col(MB + jl))
-    dma("s", T.yx[:, 0:2048], T.faces[:], 512, after=[R("kt", 0, 2048)])
-    ts(R("pt0", 0, 256), R("pt0", 0, 256), col(CJ), None, A.add)
-    cp(R("sc0", 1, 16, 2), R("cn", 128, 136))
+        for h, B in enumerate(("rb", "xa")):
+            lin("av", R("kt", 512 * jl + 256 * h, 512 * jl + 256 * h + 256), R(B, 0, 256), col(MK + jl), col(MB + jl))
+    dma("g", R("yv", 0, 2048), T.faces[:], 1024, after=[R("kt", 0, 8)])
+    dma("s", T.yx[:, 0:2048], T.faces[:], 512, after=[R("yv", 0, 8)])
+    lin("av", R("pt0", 0, 256), R("pt0", 0, 256), 1.0, col(CJ))
+    lin("av", R("sc0", 1, 16, 2), R("cn", 128, 136))
     lin("av", R("land0", 0, 8), R("cn", 128, 136))
     lin("av", R("sc1", 1, 16, 2), R("pt0", 1, 16, 2))
     ts(col(CWM), col(CJ), 7.5, 0.5, A.is_lt, A.subtract)
     scan(R("sco", 0, 16), R("sc0", 0, 16), R("sc1", 0, 16), A.mult, A.add)
-    ts(R("bc", 0, 144), R("ramp", 0, 144), col(CG15), None, A.is_equal)
     cp(R("ofb", 0, 8), R("sco", 1, 16, 2))
     lin("av", R("cand", 0, 256), R("z0", 0, 256), 1.0, 0.25)
     lin("av", R("cand", 256, 512), R("z0", 128, 384), 1.0, 0.25)
@@ -410,18 +451,6 @@ def rank_program(g, core, T, topo):
     def late_constants():
         lin("av", R("nw", 128, 256), R("pt0", 0, 256, 2), 1.0, 0.5)
         ms(R("nw", 256, 512, 2), 0.0)
-        ts(R("wm", 0, 128), R("ig", 0, 128), col(CG), None, A.is_equal)
-        lin("av", R("i32", 0, 128), R("idp", 12, 140), 32.0)
-        ts(R("cf", CWP, CWP + 1), col(CJ), 7.5, None, A.is_lt)
-        ts(R("cf", CWR, CWR + 1), col(CJ), 7.5, None, A.is_gt)
-        lin("av", R("cp", 0, 144), R("bc", 0, 144), col(CWP))
-        lin("av", R("cr", 0, 144), R("bc", 0, 144), col(CWR))
-        lin("av", R("hid", 0, 128), R("idp", 12, 140), 0.5)
-        ts(R("cf", MQ, MQ + 4), R("ramp", 0, 4), col(CJQ), None, A.is_equal)
-
-    def later_constants():
-        for a in range(4):
-            lin("av", R("su", 160 * a, 160 * a + 160), R("idp", 0, 160), col(MQ + a))
 
     def last_constants():
         cp(R("kf", 0, 256), R("ki", 0, 256))
@@ -502,10 +531,10 @@ def rank_program(g, core, T, topo):
         ID, HID, NID = R("idp", 12, 140), R("hid", 0, 128), R("nid", 0, 128)
 
         def mean(q, own):
-            mm([(R("z%d" % (q % 2), 0, 512), [(HID, q_("dd", q)), (HID if own else ID, q_("fw", q))])])
+            mm([(R("z%d" % (q % 2), 0, 512), [(ID, q_("dd", q)), (ID if own else HID, q_("fw", q))])])
 
         def rnd(q):
-            lin("av", R("yv", yb + 512 * q, yb + 512 * q + 512), R("z%d" % (q % 2), 0, 512), 1.0 - 2.0 ** -10, CY)
+            lin("av", R("yv", yb + 512 * q, yb + 512 * q + 512), R("z%d" % (q % 2), 0, 512), 0.5 - 2.0 ** -11, CY)
 
         def values(q):
             if q in PLAN["own"]:
@@ -513,7 +542,10 @@ def rank_program(g, core, T, topo):
                 gather("a", "dd", 512 * q, 512 * q + 512, FT, "ofu", 0)
                 mm([(X, [(ID, q_("dd", q)), (NID, q_("fw", q))])])
                 ts(q_("ind", q), X, C32, C32, A.add, A.is_equal)
-            else:
+            elif q == 0 and PLAN["big"]:
+                diff(0, 1024)
+                near(0, 1024)
+            elif q != 1 or not PLAN["big"]:
                 diff(512 * q, 512 * q + 512)
                 near(512 * q, 512 * q + 512)
 
@@ -522,9 +554,8 @@ def rank_program(g, core, T, topo):
             kid("av", a, a + GQ)
         extract(0)
         extract(1)
-        mm([(R("rb", 0, 128), [(R("shf", 0, 128), K)]), (R("rb", 128, 256), [(R("shf", 128, 256), H)])])
-        for a in range(0, 2048, GQ):
-            fw("av", a, a + GQ)
+        for a, b in PLAN["fq"]:
+            fw("av", a, b)
         kids_of(0)
         kids_of(1)
         if t == 0:
@@ -535,16 +566,34 @@ def rank_program(g, core, T, topo):
             values(q)
         count(0)
         count(1)
-        lin("av", R("sc1", 0, 16, 2), FF, 256.0, 256.0)
+        def slots(b, k, h, X, at, scale):
+            def fm(n):
+                return R("fm", 128 * n, 128 * n + 128)
+            mm([(R(X, 0, 128), [(fm(b), k), (fm(2 + b), h)]), (R(X, 128, 256), [(fm(2 + b), k), (fm(4 + b), h)])])
+            act(R("hy", 512 * b + at, 512 * b + at + 256), R(X, 0, 256), scale, -0.5, F.Abs)
+
         tt(R("db", 0, 256), R("nw", 0, 256), KH, A.subtract)
         if t > 0:
             act(R("thr", 8, 16), R("cn", 136, 144), -1.0, 0.0, F.Identity, R("thr", 1, 2))
-            lin("av", R("thr", 2, 3), R("thr", 1, 2), 1.0, C2)
-            lin("av", R("thr", 3, 4), R("thr", 2, 3), 1.0, -C2)
+            ts(R("thr", 3, 4), R("thr", 1, 2), C2, -C2, A.add, A.add)
             act(R("thr", 0, 1), R("thr", 3, 4), -1.0, R("thr", 1, 2), F.Abs)
-        lin("av", R("cand", 384, 640), R("rb", 0, 256))
-        lin("av", R("cand", 256, 384), H, -1.0)
-        lin("av", R("cand", 640, 768), K, -1.0)
+        if last:
+            for b in range(2):
+                slots(b, K, H, "z%d" % b, 256, -2.0)
+            lin("av", R("lf", 0, 8), FF, 128.0)
+            tt(R("sc1", 1, 16, 2), R("sc1", 1, 16, 2), R("lf", 0, 8), A.add)
+            ms(R("sc1", 0, 16, 2), 256.0)
+        elif PLAN["pec"]:
+            lin("av", R("sc1", 0, 16, 2), FF, 256.0, 256.0)
+            mm([(R("rb", 0, 128), [(R("neg", 128, 256), H)]), (R("rb", 128, 256), [(R("shf", 0, 128), K)]),
+                (R("rb", 256, 384), [(R("shf", 128, 256), H)]), (R("rb", 384, 512), [(R("neg", 128, 256), K)])])
+            lin("av", R("cand", 256, 768), R("rb", 0, 512))
+        else:
+            lin("av", R("sc1", 0, 16, 2), FF, 256.0, 256.0)
+            mm([(R("rb", 0, 128), [(R("shf", 0, 128), K)]), (R("rb", 128, 256), [(R("shf", 128, 256), H)])])
+            lin("av", R("cand", 384, 640), R("rb", 0, 256))
+            lin("av", R("cand", 256, 384), H, -1.0)
+            lin("av", R("cand", 640, 768), K, -1.0)
         tt(R("dpr", 0, 128), R("uu", 0, 128), R("db", 256, 384), A.subtract)
         tt(R("dpr", 128, 256), H, R("db", 384, 512), A.subtract)
         ts(R("spl", 0, 128), R("cn", 0, 128), R("thr", 0, 1), 8.5, A.subtract, A.is_ge)
@@ -553,10 +602,6 @@ def rank_program(g, core, T, topo):
         for q in range(4):
             mean(q, q in PLAN["own"])
             rnd(q)
-        if t == 0:
-            later_constants()
-            for a in range(0, 2048, 512):
-                lin("av", R("yv", a, a + 512), R("ft", 4096 + a, 4608 + a), 1.0, CY)
         tt(R("db", 0, 128), R("db", 0, 128), R("spl", 0, 128), A.mult)
         tt(R("db", 128, 256), R("db", 128, 256), R("spl", 0, 128), A.mult)
         ts(R("sc0", 1, 16, 2), R("cn", 128, 136), 4.5, None, A.is_lt)
@@ -565,9 +610,9 @@ def rank_program(g, core, T, topo):
         tt(FN, FF, R("sc0", 1, 16, 2), A.not_equal)
         cp(R("ofb", 0, 8), R("sco", 1, 16, 2))
         OFF = R("ofb", 0, 8)
-        lin("av", R(S, 8, 136), IND(R("cand", 0, 640), OFF))
-        lin("av", R(S, 136, 264), IND(R("cand", 128, 768), OFF))
         if not last:
+            lin("av", R(S, 8, 136), IND(R("cand", 0, 640), OFF))
+            lin("av", R(S, 136, 264), IND(R("cand", 128, 768), OFF))
             send(t + 1, "k", 0, 136)
             send(t + 1, "h", 136, 264)
             mm([(R("cn", 136, 144), [(R("one", 0, 128), R("sc0", 1, 16, 2))])])
@@ -598,7 +643,8 @@ def rank_program(g, core, T, topo):
             pointers()
             for a in range(0, 2048, PLAN["sq"]):
                 select("av", a, a + PLAN["sq"])
-                turn(a, a + PLAN["sq"])
+            for a in range(0, 2048, PLAN["tq"]):
+                turn(a, a + PLAN["tq"])
             kids_new(PR)
             hilo(PR)
             for h, B in enumerate(("xa", "rb")):
@@ -612,36 +658,24 @@ def rank_program(g, core, T, topo):
             if t == 1:
                 last_constants()
         else:
-            fk, fh = R(S, 8, 136), R(S, 136, 264)
-
-            def fm(n):
-                return R("fm", 128 * n, 128 * n + 128)
-            mm([(R("xa", 0, 128), [(fm(0), fk), (fm(2), fh)]), (R("xa", 128, 256), [(fm(2), fk), (fm(4), fh)]),
-                (R("xa", 256, 384), [(fm(1), fk), (fm(3), fh)]), (R("xa", 384, 512), [(fm(3), fk), (fm(5), fh)])])
+            for b in range(2):
+                slots(b, R("cand", 0, 128), R("cand", 128, 256), "xa" if b == 0 else "xb", 0, 2.0)
             pointers()
             for a in range(0, 2048, 512):
                 select("av", a, a + 512)
             kids_new(R("old", 256, 512))
             lin("av", R("fnb", 0, 8), FN)
-            lin("av", R("lf", 0, 8), FN, 128.0)
-            lin("av", R("tr0", 0, 256), IND(R("old", 256, 512), R("lu", 0, 16)))
-            mm([(R("xb", x, 128, 16, (0, 8)), [(R("idp", 12 + x, 140, 16), R("fnb", 0, 8))]) for x in range(16)])
-            tt(R("lf", 0, 8), R("lf", 0, 8), R("sc1", 1, 16, 2), A.add)
+            act(R("tr0", 0, 256), IND(R("old", 256, 512), R("lu", 0, 16)), 2.0, -0.5, F.Abs)
+            mm([(R("z1", x, 128, 16, (0, 8)), [(R("idp", 12 + x, 140, 16), R("fnb", 0, 8))]) for x in range(16)])
             add("v", lambda: g.vector.transpose(ap(R("tr1", 0, 256)), ap(R("tr0", 0, 256))), [R("tr0", 0, 256)], [R("tr1", 0, 256)], 262.0)
-            cp(R("lfu", 0, 8), R("lf", 0, 8))
-            lin("av", R("hy", 0, 512), R("xa", 0, 512))
-            lin("av", R("tr2", 0, 256), IND(R("tr1", 0, 256), R("lu", 16, 32)), 2.0, -1.0)
-            lin("av", R("nw", 0, 256), R("tr2", 0, 256), -1.0, -1.0)
+            lin("av", R("tr2", 0, 256), IND(R("tr1", 0, 256), R("lu", 16, 32)), 1.0, -0.5)
             for b in range(2):
-                lin("av", R("yb1", b, 256, 2), IND(R("hy", 256 * b, 256 * b + 256), R("lfu", 0, 8)), 2.0, -1.0)
-            tt(R("tr3", 0, 256), R("nw", 0, 256), R("tr2", 0, 256), A.max)
-            dma("s", T.y0[:, 2048:4096], R("tr3", 0, 128), 64)
+                lin("av", R("yb1", b, 256, 2), IND(R("hy", 512 * b, 512 * b + 512), OFF), 1.0, -0.5)
+            dma("s", T.y0[:, 2048:4096], R("tr2", 0, 128), 64)
             for gq in range(8):
-                dma("s", T.y1[gq ^ 1, 2048:4096], R("tr3", 128, 256, 1, (16 * gq, 16 * gq + 16)), 8)
-            lin("av", R("db", 0, 256), R("yb1", 0, 256), -1.0, -1.0)
-            tt(R("yb2", 0, 256), R("db", 0, 256), R("yb1", 0, 256), A.max)
-            lin("av", R("yfo", 0, 128, 1, (0, 8)), R("xb", 0, 128, 1, (0, 8)))
-            dma("s", T.yb[:], R("yb2", 0, 256), 128)
+                dma("s" if gq % 2 else "a", T.y1[gq ^ 1, 2048:4096], R("tr2", 128, 256, 1, (16 * gq, 16 * gq + 16)), 8)
+            lin("av", R("yfo", 0, 128, 1, (0, 8)), R("z1", 0, 128, 1, (0, 8)))
+            dma("s", T.yb[:], R("yb1", 0, 256), 128)
             dma("s", T.yf[:], R("yfo", 0, 128, 1, (0, 8)), 4)
 
     prep(0)

@@ -4,34 +4,41 @@ from concourse.mybir import dt, AluOpType as A, AxisListType, ActivationFunction
 F32, BF, I32, U16 = "float32", "bfloat16", "int32", "uint16"
 SCRATCH = {}
 for _n, _w, _d in [
-    ("ft", 8192, BF), ("kt", 4096, BF), ("yv", 10240, F32), ("g1", 2048, BF), ("fw", 2048, BF), ("dd", 2048, BF),
-    ("ind", 2048, BF), ("land0", 264, F32), ("land1", 264, F32), ("land2", 264, F32), ("land3", 264, F32),
-    ("snd0", 264, F32), ("snd1", 264, F32), ("snd2", 264, F32), ("snd3", 264, F32), ("ofh", 128, U16), ("ofb", 8, U16),
-    ("old", 512, F32), ("s2", 128, F32), ("ab", 128, F32), ("abi", 128, I32), ("ofk", 128, U16), ("ofu", 128, U16),
-    ("sd", 128, F32), ("cand", 768, F32), ("spl", 128, BF), ("uu", 128, F32), ("dpr", 256, F32), ("x0", 256, F32), ("pt0", 256, F32),
-    ("pt1", 256, F32), ("ptu", 128, U16), ("hl", 512, BF), ("sc0", 16, F32), ("sc1", 16, F32), ("sco", 16, F32),
-    ("ff", 8, F32), ("fn", 8, F32), ("fnb", 16, BF), ("thr", 16, F32),
+    ("ft", 8208, BF), ("kt", 8192, BF), ("nidf", 128, F32), ("ra", 128, BF), ("rb", 128, BF), ("rc", 128, F32), ("ab", 128, F32), ("rr", 128, BF), ("ng", 128, BF),
+    ("two", 128, BF), ("ik2", 128, BF), ("gi", 256, BF), ("yv", 10240, F32), ("pt0", 256, F32), ("pt1", 256, F32), ("ptu", 128, U16),
+    ("w0", 128, BF), ("dg", 256, BF), ("fs", 2048, BF), ("lj", 2048, BF), ("g1", 2048, BF), ("fw", 2048, BF), ("dd", 2048, BF),
+    ("ind", 2048, BF), ("wn", 784, F32), ("c0", 384, F32), ("land0", 272, U16), ("land1", 272, U16), ("land2", 272, U16), ("land3", 272, U16),
+    ("snd0", 272, U16), ("snd1", 272, U16), ("snd2", 272, U16), ("ofb", 8, U16), ("fx", 16, F32),
+    ("old", 256, F32), ("abi", 128, I32), ("ofk", 128, U16), ("ofu", 128, U16), ("ramp", 8, F32),
+    ("sd", 128, F32), ("spl", 128, BF), ("gz", 128, BF), ("gn", 128, BF), ("uu", 256, F32), ("mv", 128, F32),
+    ("h0", 512, BF), ("hl", 1024, BF), ("sc0", 16, F32), ("sc1", 16, F32), ("sco", 16, F32), ("fnb", 16, BF), ("thr", 16, F32),
     ("ki", 256, I32), ("bi", 256, I32), ("fi", 128, I32), ("fb", 128, BF), ("t1", 256, I32), ("t2", 256, F32),
-    ("t3", 256, F32), ("kv", 256, F32), ("t4", 256, I32), ("t5", 256, F32), ("t6", 256, F32), ("bv", 256, F32),
-    ("kf", 256, F32), ("ramp", 160, F32), ("iv", 128, F32), ("ig", 128, F32), ("pi", 8, I32), ("ci", 8, I32),
-    ("cf", 32, F32), ("bc", 144, BF), ("cm", 144, BF), ("cd", 144, BF), ("cp", 144, BF), ("cr", 144, BF),
-    ("b8", 144, BF), ("idp", 160, BF), ("nid", 128, BF), ("hid", 128, BF), ("wm", 128, BF), ("i32", 128, BF), ("si", 640, BF), ("su", 640, BF),
-    ("oh", 144, BF), ("im", 768, F32), ("fm", 768, F32), ("shf", 256, F32), ("one", 160, F32), ("neg", 256, F32), ("oneb", 160, BF),
+    ("t4", 256, I32), ("t5", 256, F32), ("ke", 256, I32), ("bv", 256, F32),
+    ("kf", 256, F32), ("iv", 384, F32), ("pi", 8, I32), ("ci", 8, I32), ("cf", 32, F32), ("ex", 864, BF), ("e8", 16, BF),
+    ("b8", 144, BF), ("idp", 160, BF), ("nid", 128, BF), ("hid", 128, BF), ("wm", 128, BF), ("wf", 128, BF), ("wh", 128, BF),
+    ("ik", 128, BF), ("idf", 128, F32), ("zb", 128, BF), ("zf", 128, F32), ("eps", 128, BF),
+    ("im", 768, F32), ("fm", 768, F32), ("fmb", 768, BF), ("shf", 256, F32), ("one", 128, F32), ("oneb", 160, BF),
     ("li", 64, F32), ("lt", 32, F32), ("lu", 32, U16), ("tr0", 256, F32), ("tr1", 256, F32), ("tr2", 256, F32),
-    ("tr3", 256, F32), ("fin", 256, F32), ("hy", 1024, F32), ("lf", 8, F32), ("lfu", 8, U16), ("yb1", 256, F32),
-    ("yb2", 256, F32), ("yfo", 128, F32),
+    ("hy", 1024, F32), ("lf", 8, F32), ("yb1", 256, F32), ("yfo", 128, F32),
 ]:
     SCRATCH[_n] = ("sbuf", [128, _w], _d)
-PSUM = ["xa", "xb", "z0", "z1", "cn", "nw", "db", "rb"]
+PSUM = ["xa", "xb", "cn", "ms", "u0", "u1", "u2", "u3"]
 for _n in PSUM:
     SCRATCH[_n] = ("psum", [128, 512], F32)
-NDMA = 34
-SEMAPHORES = (["ev", "ea", "ep", "eg"] + ["%s%d%s" % (_a, _t, _b) for _a in ("arr", "out") for _t in (1, 2, 3) for _b in "kh"]
-              + ["dm%d" % _i for _i in range(NDMA)])
+NDMA = 90
+SEMAPHORES = ["ev", "ea", "ep", "eg"] + ["%s%d%d" % (_a, _t, _h) for _a in ("arr", "out") for _t in (1, 2, 3) for _h in (0, 1)] + ["dm%d" % _i for _i in range(NDMA)]
 
 CY = 1.5 * 2.0 ** 23
 C2 = 1.5 * 2.0 ** 24
+C16 = 1.5 * 2.0 ** 27
+FAR = 16384.0
 C32 = 1.5 * 2.0 ** 28
+KEEP = 2.0 ** -17
+CFACE = 1.5 * 2.0 ** 40
+CKID = 1.5 * 2.0 ** 39
+MID = 4103.5
+POS, UP = 4112, 6160
+WK, WF_, WH_, WSK, WCK, WCH, WEND = 64, 128, 136, 200, 264, 328, 392
 
 
 def R(name, a, b, step=1, p=None):
@@ -42,22 +49,35 @@ def IND(win, off):
     return ("*", win, off)
 
 
-def _mask(s):
+def _cols(s):
+    return range(s[1], s[2], s[3]) if s[3] > 0 else range(s[1], -1 if s[2] is None else s[2], s[3])
+
+
+def _bits(r):
     m = 0
-    for c in (range(s[1], s[2], s[3]) if s[3] > 0 else range(s[1], -1 if s[2] is None else s[2], s[3])):
+    for c in r:
         m |= 1 << c
     return m
 
 
-PLAN = {"pe": 0.42, "gat": 1.56, "hop": 4000.0, "wake": 90.0, "ov": 60, "oa": 100, "pec": 0, "crit": 0.3, "due": 0.0, "early": ("yv",), "big": 1, "tq": 1024,
-        "fq": ((0, 512), (512, 1024), (1024, 1536), (1536, 2048)), "seed": 1, "mean": 0.1, "sign": 1, "steps": 44000, "heat": 250.0, "own": (3,), "gq": 512, "sq": 512}
+PLAN = {"sel": (0, 1), "split": (0, 1, 2, 3), "pe": 0.5, "pf": 4.0, "gat": 1.56, "hop": 3500.0, "wake": 160.0, "ov": 60, "oa": 100, "big": 1, "tq": 1024, "dlat": 2000.0,
+        "fq": ((0, 512), (512, 1024), (1024, 1536), (1536, 2048)), "seed": 1, "mean": 0.03, "steps": 500, "heat": 150.0, "own": (3,), "cycle": 12400.0, "tries": 0, "shake": 2500.0, "warm": 200.0, "first": 5300.0, "pin": 4, "gq": 512,
+        "vadd": (), "tadd": (), "bias": 300.0, "span": 10000.0, "look": 8000.0, "sweeps": 24}
 _PLANS = {}
+STEP = {"flip": (2.2, "v"), "kids": (2.8, "a"), "pos": (3.1, "a"), "neg": (5.6, "v"), "belts": (3.0, "a"), "vals": (7.0, "a"), "marks": (1.5, "g"),
+        "conv0": (0.0, "v"), "conv1": (2.2, "v"), "fw0": (1.2, "a"), "fw1": (2.8, "a"), "fw2": (4.3, "a"), "fw3": (5.0, "a"),
+        "kid0": (2.0, "v"), "kid1": (2.0, "a"), "kid2": (4.2, "v"), "kid3": (4.2, "a"), "u0": (2.9, "v"), "u1": (5.1, "v"), "a0": (3.6, "p"), "a1": (5.8, "p"), "uu1": (7.0, "a"),
+        "val0": (3.6, "v"), "val1": (4.9, "v"), "val2": (6.6, "v"), "val3": (5.9, "a"), "count0": (6.0, "p"), "count1": (8.4, "p"), "kc": (7.6, "p"), "start": (-0.5, "p"),
+        "change0": (4.5, "p"), "change1": (5.7, "p"), "change2": (7.4, "p"), "change3": (6.8, "p"), "g": (3.0, "a"), "dk0": (5.8, "v"), "dk1": (7.5, "v"), "thr": (-1.0, "a"),
+        "round0": (6.7, "a"), "round1": (7.2, "a"), "round2": (8.2, "a"), "round3": (7.7, "a"), "spl0": (6.7, "v"), "spl1": (9.1, "v"), "open0": (7.6, "v"), "open1": (9.4, "v"),
+        "go0": (8.6, "a"), "go1": (9.2, "a"), "kids1": (9.6, "a"), "renew0": (9.0, "a"), "renew1": (9.8, "a"), "renew2": (11.0, "v"), "renew3": (11.0, "a"),
+        "turn0": (11.8, "v"), "turn1": (12.3, "v"), "slots": (10.0, "a"), "out0": (9.8, "a"), "out1": (11.0, "a")}
 
 
 def _len(s):
     if s[0] == "*":
         return 16 * _len(s[2])
-    return len(range(s[1], s[2], s[3]) if s[3] > 0 else range(s[1], -1 if s[2] is None else s[2], s[3]))
+    return len(_cols(s))
 
 
 def _cost(e, out, a, b=None):
@@ -78,14 +98,14 @@ def _edges(ops):
         deps = {}
         acc = [(s, False) for s in o["r"]] + [(s, True) for s in o["w"]]
         for s, wr in acc:
-            if s[1:4] not in masks:
-                masks[s[1:4]] = _mask(s)
-            m = masks[s[1:4]]
-            for m2, n2, w2 in hist.get(s[0], ()):
-                if (wr or w2) and m & m2:
+            if s[1:] not in masks:
+                masks[s[1:]] = (_bits(_cols(s)), _bits(range(128) if s[4] is None else range(*s[4])))
+            m, pm = masks[s[1:]]
+            for (m2, pm2), n2, w2 in hist.get(s[0], ()):
+                if (wr or w2) and m & m2 and pm & pm2:
                     deps[n2] = deps.get(n2, False) or (w2 and not wr)
         for s, wr in acc:
-            hist.setdefault(s[0], []).append((masks[s[1:4]], n, wr))
+            hist.setdefault(s[0], []).append((masks[s[1:]], n, wr))
         out.append(deps)
     return out
 
@@ -96,128 +116,250 @@ def _plan(ops, edges):
     for i, o in enumerate(ops):
         if o["k"] == "x":
             pre[i].add(max(j for j in range(i) if ops[j]["k"] == "r" and ops[j]["sem"][0][3:] == o["sem"][0][3:]))
+    pre = [[j for j in p if not any(j in pre[k] for k in p)] for p in pre]
+    loads = [i for i in range(n) if ops[i]["k"] == "d" and not edges[i]]
     post = [[] for _ in ops]
     for i in range(n):
         for j in pre[i]:
             post[j].append(i)
-    prio = [0.0] * n
-    for i in range(n - 1, -1, -1):
-        prio[i] = min(c for _, c in ops[i]["alt"].values()) + ops[i]["lat"] + PLAN["wake"] + max([prio[j] for j in post[i]] + [0.0])
-    post = [set(p) for p in post]
-    banks = [set(s[0] for s in o["r"] + o["w"] if s[0] in PSUM) for o in ops]
-    pre = [[j for j in p if not any(j in pre[k] for k in p)] for p in pre]
     wake = PLAN["wake"]
     cost = [{e: c for e, (_, c) in o["alt"].items()} for o in ops]
     lat = [o["lat"] + wake for o in ops]
-    banks = [sorted(b) for b in banks]
-    why = [-1] * n
-    lastw = max(i for i in range(n) if ops[i]["k"] == "r")
-    due = [PLAN["due"] if i < lastw and any(s[0] in PLAN["early"] for s in o["w"]) else 0.0 for i, o in enumerate(ops)]
+    banks = [sorted(set(s[0] for s in o["r"] + o["w"] if s[0] in PSUM)) for o in ops]
+    pe = [o["k"] == "c" and "p" in o["alt"] for o in ops]
+    fore = [[(j, 0.0 if pe[i] and pe[j] else lat[j]) for j in pre[i]] for i in range(n)]
+    aft = [[(j, 0.0 if pe[i] and pe[j] else lat[i]) for j in post[i]] for i in range(n)]
 
-    def place(seq, eng, base, start, end):
-        busy = {k: list(v) for k, v in base.items()}
-        for i in seq:
-            t, y = 0.0, -1
-            for j in pre[i]:
-                if end[j] > t:
-                    t, y = end[j], j
-            e = eng[i]
-            c = cost[i][e]
-            mine = busy.setdefault(e, [])
-            while True:
-                t1 = t
-                k = len(mine)
-                while k and mine[k - 1][1] > t:
-                    k -= 1
-                while k < len(mine) and mine[k][0] < t + c:
-                    t, y = mine[k][1], mine[k][2]
-                    k += 1
-                for b in banks[i]:
-                    for s0, s1, e2, j in reversed(busy.setdefault(b, [])):
-                        if e2 != e and s1 + wake > t and s0 < t + c + wake:
-                            t, y = s1 + wake, j
-                if t == t1 or not banks[i]:
-                    break
-            mine.insert(k, (t, t + c, i))
-            why[i] = y
+    def fit(busy, i, e, t):
+        c, mine = cost[i][e], busy[e]
+        while True:
+            t1 = t
+            k = len(mine)
+            while k and mine[k - 1][1] > t:
+                k -= 1
+            while k < len(mine) and mine[k][0] < t + c:
+                t = mine[k][1]
+                k += 1
             for b in banks[i]:
-                busy[b].append((t, t + c, e, i))
-            start[i], end[i] = t, t + c + lat[i]
-        return max(end[i] + due[i] for i in seq) + PLAN["mean"] * sum(end[i] for i in seq) / len(seq), busy
+                for s0, s1, e2 in busy[b]:
+                    if s1 + wake > t and s0 < t + c + wake and e2 != e:
+                        t = s1 + wake
+            if t == t1 or not banks[i]:
+                return t, k
 
-    part, left = [], set(range(n))
-    for w in [i for i in range(n) if ops[i]["k"] == "r"][1::2]:
-        mine, todo = set(), [w - 1, w] + [i for i in range(w) if due[i]]
-        while todo:
-            i = todo.pop()
-            if i in left:
-                left.discard(i)
-                mine.add(i)
-                todo += pre[i]
-        part.append(mine)
-    part.append(left)
+    def place(seq, eng, back, bias=None):
+        busy = {k: [] for k in list("vapgsx") + PSUM}
+        start, end = [0.0] * n, [0.0] * n
+        for i in (seq if back else loads + [i for i in seq if i > loads[-1]]):
+            t = lat[i] if back else 0.0
+            for j, d in (aft[i] if back else fore[i]):
+                if end[j] + d > t:
+                    t = end[j] + d
+            e = eng[i]
+            if bias is not None and len(cost[i]) > 1:
+                ta, tv = fit(busy, i, "a", t)[0] + cost[i]["a"], fit(busy, i, "v", t)[0] + cost[i]["v"]
+                e = eng[i] = "a" if ta <= tv + bias else "v"
+            t, k = fit(busy, i, e, t)
+            c = cost[i][e]
+            busy[e].insert(k, (t, t + c))
+            for b in banks[i]:
+                busy[b].append((t, t + c, e))
+            start[i], end[i] = t, t + c
+        return max(end[i] + lat[i] for i in range(n)) + PLAN["mean"] * sum(end) / n, start, end
+
+    def ranked(key):
+        key = list(key)
+        for i in range(n):
+            for j in pre[i]:
+                if key[j] > key[i]:
+                    key[i] = key[j]
+        return sorted(range(n), key=lambda i: key[i])
+
+    def justify(seq, eng, bias):
+        v, start, end = place(seq, eng, False, bias)
+        for _ in range(2):
+            _, _, e2 = place(sorted(range(n), key=lambda i: (-end[i], -i)), eng, True)
+            s2 = sorted(range(n), key=lambda i: (-e2[i], i))
+            v2, st2, en2 = place(s2, eng, False)
+            if v2 >= v - 1.0:
+                break
+            v, seq, start, end = v2, s2, st2, en2
+        return v, seq, start, end
+
+    prio = [0.0] * n
+    for i in range(n - 1, -1, -1):
+        prio[i] = min(cost[i].values()) + lat[i] + max([prio[j] for j in post[i]] + [0.0])
     rng = np.random.RandomState(PLAN["seed"])
     eng = [("a" if "a" in c else list(c)[0]) for c in cost]
-    start, end, base = [0.0] * n, [0.0] * n, {}
-    seq = []
-    for w in range(len(part) - 1):
-        mine, fixed = part[w] | part[w + 1], part[w] if w < len(part) - 2 else part[w] | part[w + 1]
-        seq = [i for i in seq if i in mine]
-        seq += sorted(mine - set(seq), key=lambda i: (i not in part[w], -prio[i], i))
-        m = len(seq)
-        flex = [i for i in seq if len(cost[i]) > 1]
-        best, _ = place(seq, eng, base, start, end)
-        top = (best, seq, list(eng))
-        steps = PLAN["steps"]
-        rnd = rng.rand(steps, 6).tolist()
+    key = [max(prio) - p for p in prio]
+    best, seq, start, end = justify(ranked(key), eng, PLAN["bias"])
+    zero = [start[i] for i in range(n) if ops[i]["k"] == "x"]
+    zero = [zero[0] - PLAN["cycle"]] + [zero[0] + k * PLAN["cycle"] for k in range(3)]
+    zero = [z - zero[0] + PLAN["first"] for z in zero] + [0.0]
+    for i, o in enumerate(ops):
+        key[i] = start[i]
+        if o["at"]:
+            x, e = STEP[o["at"][1]]
+            key[i] = zero[o["at"][0]] + 1000.0 * x
+            if e in cost[i]:
+                eng[i] = e
+        elif o["k"] == "c" and start[i] < zero[1]:
+            key[i] = 0.5 * (max(prio) - prio[i])
+    twin, seen = {}, {}
+    for i, o in enumerate(ops):
+        k = o["at"] or i
+        seen[k] = seen.get(k, 0) + 1
+        twin.setdefault((o["at"][1], seen[k]) if o["at"] and o["at"][0] in (1, 2) else i, []).append(i)
+    twin = [l for l in twin.values() if ops[l[0]]["k"] != "x" and l[0] not in loads]
+    cur = place(ranked(key), eng, False)[0]
+    keep = (cur, key, eng)
+    for it, (r0, r1, r2, r3) in enumerate(rng.rand(PLAN["tries"], 4).tolist()):
+        k2, e2, l = list(key), eng, twin[int(r0 * len(twin))]
+        if r1 < 0.3 and len(cost[l[0]]) > 1:
+            e2 = list(eng)
+            for i in l:
+                e2[i] = "v" if eng[l[0]] == "a" else "a"
+        else:
+            for i in l:
+                k2[i] += (r2 - 0.5) * PLAN["shake"]
+        x = place(ranked(k2), e2, False)[0]
+        if x <= cur + PLAN["warm"] * r3 * (1.0 - it / PLAN["tries"]):
+            cur, key, eng = x, k2, e2
+            if x < keep[0]:
+                keep = (x, k2, e2)
+    eng = list(keep[2])
+    best, seq, start, end = justify(ranked(keep[1]), eng, None)
+    posts = [set(p) for p in post]
+    span, look = PLAN["span"], PLAN["look"]
+    for sweep in range(PLAN["sweeps"]):
+        t0 = -rng.rand() * span * 0.5
+        while t0 < best:
+            seq = sorted(range(n), key=lambda i: (start[i], i))
+            _, _, tail = place(sorted(range(n), key=lambda i: (-end[i], -i)), eng, True)
+            head = [i for i in seq if start[i] < t0 or i in loads]
+            mine = [i for i in seq if t0 <= start[i] < t0 + span + look and i not in loads]
+            rest = [i for i in seq if start[i] >= t0 + span + look]
+            t0 += span * 0.5
+            if len(mine) < 2:
+                continue
+            base = {k: [] for k in list("vapgsx") + PSUM}
+            for i in head:
+                if end[i] > t0 - span:
+                    base[eng[i]].append((start[i], end[i], i))
+                    for b in banks[i]:
+                        base[b].append((start[i], end[i], eng[i], i))
+            floor = start[mine[0]]
+            inside = set(mine)
+            out = {i: max([d + tail[j] for j, d in aft[i] if j not in inside] + [lat[i]]) for i in mine}
+            nxt = {}
+            for i in reversed(rest):
+                nxt[eng[i]] = tail[i]
+            st, en, why = list(start), list(end), [-1] * n
 
-        def chain():
-            i, c = max(mine, key=lambda i: end[i] + due[i]), []
-            while i in mine:
-                c.append(i)
-                i = why[i]
-            return c, [i for i in c if len(cost[i]) > 1] or flex
-        crit, cflex = chain()
-        for it in range(steps):
-            r0, r1, r2, r3, r4, r5 = rnd[it]
-            s2, e2 = seq, eng
-            if r0 < 0.35:
-                e2 = list(eng)
-                i = cflex[int(r1 * len(cflex))] if r5 < PLAN["crit"] else flex[int(r1 * len(flex))]
-                e2[i] = "v" if eng[i] == "a" else "a"
-                j = flex[int(r2 * len(flex))]
-                if r3 < 0.5 and eng[j] != eng[i]:
-                    e2[j] = eng[i]
-            else:
-                s2 = list(seq)
-                p = seq.index(crit[int(r1 * len(crit))]) if r5 < PLAN["crit"] else int(r1 * m)
-                i = s2.pop(p)
-                q = p
-                if r2 < 0.5:
-                    far = max(0, p - 1 - int(r3 * 30))
-                    while q > far and i not in post[s2[q - 1]]:
-                        q -= 1
+            def attempt(s, e_):
+                busy = {k: list(l) for k, l in base.items()}
+                top, arg, tot = 0.0, -1, 0.0
+                for i in s:
+                    t, y = floor, -1
+                    for j, d in fore[i]:
+                        if en[j] + d > t:
+                            t, y = en[j] + d, j
+                    e = e_[i]
+                    c, q = cost[i][e], busy[e]
+                    while True:
+                        t1 = t
+                        k = len(q)
+                        while k and q[k - 1][1] > t:
+                            k -= 1
+                        while k < len(q) and q[k][0] < t + c:
+                            t, y = q[k][1], q[k][2]
+                            k += 1
+                        for b in banks[i]:
+                            for s0, s1, e2, j in busy[b]:
+                                if s1 + wake > t and s0 < t + c + wake and e2 != e:
+                                    t, y = s1 + wake, j
+                        if t == t1 or not banks[i]:
+                            break
+                    q.insert(k, (t, t + c, i))
+                    for b in banks[i]:
+                        busy[b].append((t, t + c, e, i))
+                    st[i], en[i], why[i] = t, t + c, y
+                    tot += t
+                    if t + c + out[i] > top:
+                        top, arg = t + c + out[i], i
+                for e, x in nxt.items():
+                    if e in "vap" and busy[e] and busy[e][-1][1] + x > top:
+                        top, arg = busy[e][-1][1] + x, busy[e][-1][2]
+                return top + PLAN["mean"] * tot / len(s), arg
+
+            def chain(i):
+                c = []
+                while i in inside:
+                    c.append(i)
+                    i = why[i]
+                return c
+            cur, arg = attempt(mine, eng)
+            crit, s1, e1 = chain(arg), mine, eng
+            keep = (cur, s1, e1)
+            flx = [i for i in mine if len(cost[i]) > 1 and (sweep >= PLAN["pin"] or not ops[i]["at"])]
+            for r0, r1, r2, r3, r4, r5 in rng.rand(PLAN["steps"], 6).tolist():
+                s2, e2 = s1, e1
+                if r0 < 0.25 and flx:
+                    cf = [i for i in crit if i in flx]
+                    i = cf[int(r1 * len(cf))] if r5 < 0.4 and cf else flx[int(r1 * len(flx))]
+                    e2 = list(e1)
+                    e2[i] = "v" if e1[i] == "a" else "a"
+                    j = flx[int(r2 * len(flx))]
+                    if r3 < 0.5 and e1[j] != e1[i]:
+                        e2[j] = e1[i]
+                elif r0 < 0.55 and len(crit) > 1:
+                    k = int(r1 * (len(crit) - 1))
+                    i, j = crit[k], crit[k + 1]
+                    p, q = s1.index(j), s1.index(i)
+                    if i in posts[j] or p > q:
+                        continue
+                    mid = s1[p:q + 1]
+                    if r2 < 0.5:
+                        need = {i}
+                        for y in reversed(mid):
+                            if posts[y] & need:
+                                need.add(y)
+                    else:
+                        late = {j}
+                        for y in mid:
+                            if any(y in posts[z] for z in late):
+                                late.add(y)
+                        need = set(mid) - late
+                    if j in need or i not in need:
+                        continue
+                    s2 = s1[:p] + [y for y in mid if y in need] + [y for y in mid if y not in need] + s1[q + 1:]
                 else:
-                    far = min(m - 1, p + 1 + int(r3 * 30))
-                    while q < far and s2[q] not in post[i]:
-                        q += 1
-                if q == p:
-                    continue
-                s2.insert(q, i)
-            v, _ = place(s2, e2, base, start, end)
-            if v <= best + PLAN["heat"] * (1.0 - it / steps) * r4:
-                best, seq, eng = v, s2, e2
-                crit, cflex = chain()
-                if v < top[0]:
-                    top = (v, s2, list(e2))
-        _, seq, eng = top
-        v, busy = place(seq, eng, base, start, end)
-        v = max(end[i] for i in fixed)
-        base = {k: [x for x in l if (x[1] > v - 12000.0 or k in "gs") and x[-1] not in part[w + 1] and x[-1] >= 0] for k, l in busy.items()}
-        for k in "vap":
-            base[k] = [(0.0, max(0.0, v - 12000.0), -1)] + base.get(k, [])
+                    s2 = list(s1)
+                    p = s1.index(crit[int(r1 * len(crit))]) if r5 < 0.5 and crit else int(r1 * len(s1))
+                    i = s2.pop(p)
+                    q = p
+                    if r2 < 0.5:
+                        far = max(0, p - 1 - int(r3 * 25))
+                        while q > far and i not in posts[s2[q - 1]]:
+                            q -= 1
+                    else:
+                        far = min(len(s2), p + 1 + int(r3 * 25))
+                        while q < far and s2[q] not in posts[i]:
+                            q += 1
+                    if q == p:
+                        continue
+                    s2.insert(q, i)
+                x, arg = attempt(s2, e2)
+                if x <= cur + PLAN["heat"] * r4 * (1.0 - sweep / PLAN["sweeps"]):
+                    cur, s1, e1, crit = x, s2, e2, chain(arg)
+                    if x < keep[0]:
+                        keep = (x, s2, e2)
+            attempt(keep[1], keep[2])
+            x, s2, st2, en2 = justify(head + sorted(mine, key=lambda i: (st[i], i)) + rest, list(keep[2]), None)
+            if x <= best + 30.0:
+                best, start, end, eng = x, st2, en2, keep[2]
+    end = [end[i] + lat[i] for i in range(n)]
     order = sorted(range(n), key=lambda i: (start[i], i))
-    loads = [i for i in range(n) if ops[i]["k"] == "d" and not edges[i]]
     return [(i, eng[i]) for i in loads + [i for i in order if i not in loads]]
 
 
@@ -246,7 +388,12 @@ def rank_program(g, core, T, topo):
         return o
 
     def add(eng, fn, rd, wr, cost, kind="c", sem=None, lat=0.0):
-        ops.append({"alt": {eng: (fn, cost)}, "r": flat(rd), "w": flat(wr), "k": kind, "sem": sem, "lat": lat})
+        ops.append({"alt": {eng: (fn, cost)}, "r": flat(rd), "w": flat(wr), "k": kind, "sem": sem, "lat": lat, "at": tag[0]})
+
+    tag = [None]
+
+    def step(t, name):
+        tag[0] = (t, name) if name in STEP else None
 
     def either():
         o = ops.pop()
@@ -288,13 +435,21 @@ def rank_program(g, core, T, topo):
         if len(eng) == 2:
             either()
 
+    def acc(terms, first=False, final=False):
+        def fn():
+            for n, (o, l, r) in enumerate(terms):
+                ins = g.tensor.matmul(ap(o), ap(l), ap(r), first and n == 0, final and n == len(terms) - 1)
+            return ins
+        c = sum(max(min(64, _len(l)), _len(r)) * (4 if SCRATCH[l[0]][2] == F32 else 1) * PLAN["pe"] + PLAN["pf"] for _, l, r in terms)
+        add("p", fn, [x for t in terms for x in t[1:]], sorted(set(t[0] for t in terms), key=repr), c)
+
     def mm(groups):
         def fn():
             for out, terms in groups:
                 for n, (l, r) in enumerate(terms):
                     ins = g.tensor.matmul(ap(out), ap(l), ap(r), n == 0, n == len(terms) - 1)
             return ins
-        c = sum(max(min(64, _len(l)), _len(r)) * (4 if SCRATCH[l[0]][2] == F32 else 1) * PLAN["pe"] for _, terms in groups for l, r in terms)
+        c = sum(max(min(64, _len(l)), _len(r)) * (4 if SCRATCH[l[0]][2] == F32 else 1) * PLAN["pe"] + PLAN["pf"] for _, terms in groups for l, r in terms)
         add("p", fn, [x for _, terms in groups for t in terms for x in t], [o for o, _ in groups], c)
 
     def iota(out, pat, base, cm):
@@ -303,219 +458,273 @@ def rank_program(g, core, T, topo):
         else:
             add("g", lambda: g.iota(ap(out), pat, base, cm, allow_small_or_imprecise_dtypes=True), [], [out], 130 + 1.66 * _len(out))
 
-    def asel(out, a, pat, base, cm, op=A.is_equal):
-        add("g", lambda: g.affine_select(ap(out), ap(a), pat, op, 0.0, base, cm), [a], [out], 170 + 1.66 * _len(out))
+    def asel(out, a, pat, base, cm, op=A.is_equal, fill=0.0):
+        add("g", lambda: g.affine_select(ap(out), ap(a), pat, op, fill, base, cm), [a], [out], 170 + 1.66 * _len(out))
 
     def band(out, a, pat, cm, lo, hi):
         asel(out, a, pat, -lo, cm, A.is_ge)
         asel(out, out, [[-s, c] for s, c in pat], hi, -cm, A.is_ge)
+
+    def diag(out, a, v):
+        asel(out, a, [[1, 128]], 0, -1, A.not_equal, v)
 
     ndma = [0]
 
     def dma(q, out, a, kb, after=()):
         sem = "dm%d" % ndma[0]
         ndma[0] += 1
-        if q == "g":
-            add(q, lambda: g.dma_start(ap(out), ap(a), accum_op=A.add), [out] + list(after), [out], 1000.0, "d", (sem, 16), 1900.0 + 8.0 * kb)
-        else:
-            add(q, lambda: (g.sync if q == "s" else g.scalar).dma_start(ap(out), ap(a)), [a] + list(after), [out],
-                60.0 + (4.0 * kb if q == "s" else 0.0), "d", (sem, 16), 1900.0 + (4.0 * kb if q == "a" else 0.0))
+        add(q, lambda: (g.sync if q == "s" else g.scalar).dma_start(ap(out), ap(a)), [a] + list(after), [out],
+            60.0 + (4.0 * kb if q == "s" else 0.0), "d", (sem, 16), PLAN["dlat"] + (4.0 * kb if q == "a" else 0.0))
 
-    def send(t, w, a, b):
+    def send(t, h):
         rid, pid, _ = topo.addr(nxt)
         m = topo.mask(core, nxt)
-        add("g", lambda: g.remote_dma(T["land%d" % t][:, a:b], T["snd%d" % (t - 1)][:, a:b], T.sem["arr%d%s" % (t, w)],
-                                      T.sem["out%d%s" % (t, w)], pid, rid, m),
-            [R("snd%d" % (t - 1), a, b)], [], 300.0, "r", ("out%d%s" % (t, w), len(topo.engines(core, nxt))), PLAN["hop"])
+        a, b = 136 * h, 136 * h + 136
+        add("g", lambda: g.remote_dma(T["land%d" % t][:, a:b], T["snd%d" % (t - 1)][:, a:b], T.sem["arr%d%d" % (t, h)], T.sem["out%d%d" % (t, h)], pid, rid, m),
+            [R("snd%d" % (t - 1), a, b)], [], 300.0, "r", ("out%d%d" % (t, h), len(topo.engines(core, nxt))), PLAN["hop"])
 
-    def recv(t, w, a, b):
-        add("x", None, [], [R("land%d" % t, a, b)], 0.0, "x", ("arr%d%s" % (t, w), len(topo.engines(prv, core))))
+    def recv(t, h):
+        add("x", None, [], [R("land%d" % t, 136 * h, 136 * h + 136)], 0.0, "x", ("arr%d%d" % (t, h), len(topo.engines(prv, core))))
 
     def col(k):
         return R("cf", k, k + 1)
-    CJ, CG, CJ3, CJQ, CLO, CGG, CG15, CPC, CSI, CWM, CWP, CWR, CX8 = range(13)
-    MK, MQ, MB = 16, 20, 24
+    CJ, CG, CGG, CJ3, CJQ, CPC, CX8, CM, CSD, MK = range(10)
+    ID, NID, HID, IK = R("idp", 12, 140), R("nid", 0, 128), R("hid", 0, 128), R("ik", 0, 128)
+    ZB, ZF, ONE = R("zb", 0, 128), R("zf", 0, 128), R("one", 0, 128)
+    EXT = {"bc": 0, "cu": 144, "ca": 288, "cp": 432, "cr": 576, "ch": 720}
+    W = "wn"
+
+    def win(h, a, b, p=None):
+        return R(W, WEND * h + a, WEND * h + b, 1, p)
+
+    def FF(h):
+        return win(h, WF_, WF_ + 4)
+
+    def K(h):
+        return win(h, WK, WF_)
+
+    def H(h):
+        return win(h, WH_, WSK)
+
+    def ext(w, i):
+        return R("ex", EXT[w] + 15 - i, EXT[w] + 143 - i)
 
     dma("s", R("ki", 0, 128), T.kid0[:], 64)
     dma("a", R("ki", 128, 256), T.kid1[:], 64)
     dma("s", R("bi", 0, 256), T.belts[:], 128)
     dma("a", R("fi", 0, 128, 1, (0, 8)), T.flip[:], 4)
-    dma("s", R("ft", 4096, 5120), T.faces[:, 0:1024], 256)
-    dma("s", R("ft", 5120, 6144), T.faces[:, 1024:2048], 256)
-    dma("s", R("ft", 6144, 8192), T.faces[:], 512)
+    SEL = PLAN["sel"]
+    PLUS = 0.0 if len(SEL) == 2 else 1.0
+
+    def FS(a, b):
+        return R("fs", a, b) if PLUS else R("ft", POS + a, POS + b)
+    dma("s", FS(0, 1024), T.faces[:, 0:1024], 256)
+    dma("s", FS(1024, 2048), T.faces[:, 1024:2048], 256)
+    if not PLUS:
+        dma("a", R("ft", UP, UP + 2048), T.faces[:], 512)
 
     iota(R("pi", 0, 1), [[1, 1]], 0, 1)
-    iota(R("ramp", 0, 160), [[1, 160]], 0, 0)
-    iota(R("iv", 0, 128), [[-64, 8], [-2, 16]], 0, 0)
+    iota(R("iv", 0, 384), [[-1, 3], [-64, 8], [-2, 16]], 0, 0)
+    ms(R("kt", 0, 2048), 0.0)
     ms(R("oneb", 0, 160), 1.0)
-    ms(R("sc0", 0, 16), 0.0)
-    ms(R("sc1", 0, 16), 256.0)
-    ms(R("thr", 0, 16), 0.0)
+    dma("a", R("ex", 0, 720), R("kt", 0, 720), 180)
+    iota(R("sc0", 0, 16), [[0, 16]], 0, 0)
+    iota(R("sc1", 0, 16), [[0, 16]], 128, 0)
+    iota(R("thr", 0, 16), [[0, 16]], 0, 0)
+    iota(R("ft", 4096, POS), [[0, 16]], 0, 0)
     pi = R("pi", 0, 1)
     ts(R("ci", 0, 1), pi, 15, None, A.bitwise_and)
     ts(R("ci", 1, 2), pi, 112, None, A.bitwise_and)
-    ts(R("ci", 2, 3), pi, 3, None, A.bitwise_and)
-    ts(R("ci", 3, 4), pi, 2, 3, A.arith_shift_right, A.bitwise_and)
-    ts(R("ci", 4, 5), pi, 2, 1, A.arith_shift_right, A.bitwise_and)
-    ts(R("ci", 5, 6), pi, 4, 1, A.arith_shift_right, A.bitwise_and)
-    cp(R("cf", 0, 6), R("ci", 0, 6))
+    ts(R("ci", 2, 3), pi, 4, 1, A.arith_shift_right, A.bitwise_and)
+    cp(R("cf", 0, 3), R("ci", 0, 3))
     asel(R("b8", 0, 144, 1, (0, 8)), R("oneb", 0, 144, 1, (0, 8)), [[1, 144]], -15, -16)
-    iota(R("pt0", 0, 256), [[16, 128], [-2048, 2]], 2048, 0)
-    ts(col(CSI), col(CG), col(CJQ), 12.0, A.add, A.add)
-    ts(R("cf", MK, MK + 4), R("ramp", 0, 4), col(CJ3), None, A.is_equal)
-    ts(col(CPC), col(CG), 4.0, col(CJ), A.mult, A.add)
-    ts(R("oh", 0, 144), R("ramp", 0, 144), col(CSI), None, A.is_equal)
-    for w, lo, hi in (("bc", 0, 15), ("cp", 0, 7), ("cr", 8, 15)):
-        iota(R(w, 0, 144), [[0, 144]], 0, 0)
-        band(R(w, 15, 143, 16), R("oneb", 0, 8), [[-16, 8]], 1, lo, hi)
-    for a in range(4):
-        lin("av", R("si", 160 * a, 160 * a + 144), R("oh", 0, 144), col(MK + a))
-    for n, k in enumerate((0, -16, 1, -15, 2, -14)):
-        ts(R("im", 128 * n, 128 * n + 128), R("iv", 0, 128), col(CPC), float(k), A.add, A.is_equal)
-    ts(R("im", 512 + 15, 640, 16), R("iv", 15, 128, 16), col(CPC), -30.0, A.add, A.is_equal)
-    iota(R("neg", 0, 128), [[0, 128]], -1, 0)
-    iota(R("one", 0, 128), [[0, 128]], 1, 0)
+    lin("av", col(CPC), col(CG), 4.0, col(CJ))
+    for b in range(2):
+        ts(R("im", 384 * b, 384 * b + 384), R("iv", 0, 384), col(CPC), -16.0 * b, A.add, A.is_equal)
+    iota(ZB, [[0, 128]], 0, 0)
+    iota(ONE, [[0, 128]], 1, 0)
+    iota(R("e8", 0, 8), [[0, 8]], 0, 0)
+    for w, rows in (("bc", ((15, 1.0),)), ("cu", ((15, -1.0), (7, 1.0))), ("ca", ((15, 0.5),)), ("cp", ((7, 1.0),)), ("cr", ((15, 1.0), (7, 0.0)))):
+        o, src = R("ex", EXT[w] + 15, EXT[w] + 143, 16), R("e8", 0, 8)
+        for hi, v in rows:
+            asel(o, src, [[-16, 8]], -hi, 1, A.is_gt, v)
+            src = o
+        asel(o, o, [[-16, 8]], 0, 1, A.is_ge)
     asel(R("idp", 0, 160), R("oneb", 0, 160), [[1, 160]], -12, -1)
-    asel(R("shf", 0, 128), R("neg", 0, 128), [[-1, 128]], -1, 1)
-    asel(R("shf", 128, 256), R("neg", 0, 128), [[-1, 128]], 1, 1)
-    asel(R("shf", 15, 128, 16), R("neg", 0, 8), [[-16, 8]], 0, 1)
-    asel(R("shf", 128, 256, 16), R("neg", 0, 8), [[-16, 8]], -15, 1)
-    asel(R("nid", 0, 128), R("neg", 0, 128), [[1, 128]], 0, -1)
-    if PLAN["pec"]:
-        asel(R("neg", 128, 256), R("neg", 0, 128), [[1, 128]], 0, -1)
-    band(R("wm", 0, 128), R("oneb", 0, 128), [[-16, 8], [0, 16]], 1, 0, 15)
-    for w, c in (("i32", 32), ("hid", 2)):
-        iota(R(w, 0, 128), [[0, 128]], c, 0)
-        asel(R(w, 0, 128), R(w, 0, 128), [[1, 128]], 0, -1)
-    for a in range(4):
-        band(R("su", 160 * a, 160 * a + 160), R("idp", 0, 160), [[0, 10], [1, 16]], 0, (4 * a - 4) % 16, (4 * a - 4) % 16 + 3)
-    for a in range(0, 2048, 512):
-        iota(R("yv", a, a + 512), [[0, 512]], int(CY), 0)
+    for w, v, off in (("nid", -1.0, 0.0), ("hid", 0.5, 0.0), ("wf", 1.0, -KEEP), ("wh", 0.5, -KEEP), ("idf", 1.0, 0.0), ("ik", CKID, 0.0), ("nidf", -1.0, 0.0),
+                      ("ra", -256.0, 0.0), ("rb", 0.0625, 0.0), ("rc", 256.0, 0.0)):
+        if PLUS or not (off or w == "hid"):
+            lin("av", R(w, 0, 128), ID, v - off, off)
+    band(R("w0", 0, 128), R("oneb", 0, 128), [[-16, 8], [0, 16]], 1, 0, 15)
+    diag(R("wm", 0, 128), R("w0", 0, 128), 33.0)
+    iota(R("dg", 0, 128), [[0, 8], [1, 16]], 0, 0)
+    ts(R("dg", 0, 128), R("dg", 0, 128), col(CJ), 64.0, A.not_equal, A.mult)
+    iota(R("dg", 128, 256), [[0, 128]], 0, 0)
+    iota(R("dg", 128, 256, 16), [[0, 8]], 128, 0)
+    iota(R("mv", 0, 128), [[16, 128]], 0, 0)
+    step(-1, "marks")
+    for a in ((0, 1024) if PLUS else ()):
+        asel(R("lj", a, a + 1024), R("kt", a, a + 1024), [[-1, 8], [-16, 8], [0, 16]], -(a // 128), 1, A.not_equal, CFACE)
+    step(1, "kid0")
     iota(R("li", 0, 16), [[1, 8], [128, 2]], 0, 0)
     iota(R("li", 16, 32), [[16, 2], [32, 8]], 0, 0)
     iota(R("li", 32, 48), [[0, 8], [-256, 2]], 128, 0)
     iota(R("li", 48, 64), [[-32, 2], [0, 8]], 16, 0)
-    for n, k in enumerate((0, -16, 1, -15, 2, -14)):
-        asel(R("fm", 128 * n, 128 * n + 128), R("one", 0, 128), [[32, 8], [1, 16]], -k, -2)
-    asel(R("fm", 512, 640, 16), R("one", 0, 8), [[32, 8]], 30, -2)
+    for w, src in (("fm", "one"), ("fmb", "oneb")):
+        for n, k in enumerate((0, -16, 1, -15, 2, -14)):
+            asel(R(w, 128 * n, 128 * n + 128), R(src, 0, 128), [[32, 8], [1, 16]], -k, -2)
+        asel(R(w, 512, 640, 16), R(src, 0, 8), [[32, 8]], 30, -2)
 
     def to_val(dst, src, ti, tsh, te):
         ts(ti, src, 1, None, A.bitwise_and)
-        ts(te, src, 0.5, None, A.add)
+        ts(te, src, 16.5, None, A.add)
         ts(tsh, ti, -1.0, 0.5, A.mult, A.add)
         tt(dst, tsh, te, A.mult)
 
+    PR = R("ms", 0, 256)
     PIECE = (0, 256, 128, 384)
 
-    def hilo(src):
-        lin("av", R("hl", 0, 256), src)
-        tt(R("hl", 256, 512), src, R("hl", 0, 256), A.subtract)
+    def piece(r, up):
+        return R("hl", 256 * r + 128 * up, 256 * r + 128 * up + 128)
 
-    def ext(w, i):
-        return R(w, 15 - i, 143 - i)
+    def hilo(w, src):
+        lin("av", R(w, 0, 256), src)
+        tt(R(w, 256, 512), src, R(w, 0, 256), A.subtract)
 
-    to_val(R("db", 0, 256), R("ki", 0, 256), R("t1", 0, 256), R("t2", 0, 256), R("t3", 0, 256))
+    def pieces(up):
+        for k in range(2):
+            lin("av", piece(2 * k, up), R("ms", 128 * k, 128 * k + 128))
+            tt(piece(2 * k + 1, up), R("ms", 128 * k, 128 * k + 128), piece(2 * k, up), A.subtract)
+
+    step(-1, "kids")
+    ts(R("t1", 0, 256), R("ki", 0, 256), 1, None, A.bitwise_and)
+    ts(R("xa", 256, 512), R("ki", 0, 256), 16.5, None, A.add)
+    ts(R("t2", 0, 256), R("t1", 0, 256), -1.0, 0.5, A.mult, A.add)
+    tt(R("xa", 256, 512), R("xa", 256, 512), R("t2", 0, 256), A.mult)
+    lin("av", R("xa", 0, 128), R("xa", 384, 512), -1.0, -0.25)
+    lin("av", R("xa", 128, 256), R("xa", 256, 384), 1.0, 0.25)
+    hilo("h0", R("xa", 0, 256))
+    for r, a in enumerate(PIECE):
+        dma("sa"[r % 2], R("kt", 0, 2048, 1, (4 * r, 128, 16)), R("h0", a, a + 128), 32)
+    step(-1, "flip")
     cp(R("fb", 0, 128, 1, (0, 8)), R("fi", 0, 128, 1, (0, 8)))
-    hilo(R("db", 0, 256))
     mm([(R("cn", 128, 136), [(R("b8", 15 - x, 143 - x, 1, (0, 8)), R("fb", x, 128, 16, (0, 8))) for x in range(16)])])
-    for h, B in enumerate(("rb", "xa")):
-        mm([(R(B, 128 * (a % 2), 128 * (a % 2) + 128),
-             [(R("si", 160 * a + 12 - 4 * r, 160 * a + 140 - 4 * r), R("hl", PIECE[r], PIECE[r] + 128)) for r in range(4)])
-            for a in (2 * h, 2 * h + 1)])
-    ts(R("cf", MB, MB + 4), R("cf", MK, MK + 4), col(CLO), 0.25, A.mult, A.mult)
-    to_val(R("bv", 0, 256), R("bi", 0, 256), R("t4", 0, 256), R("t5", 0, 256), R("t6", 0, 256))
-    mm([(R("z0", 128 * n, 128 * n + 128), [(R("im", 256 * n + 128 * b, 256 * n + 128 * b + 128), R("bv", b, 256, 2)) for b in range(2)])
+    ts(R("im", 256 + 15, 384, 16), R("iv", 15, 128, 16), col(CPC), -30.0, A.add, A.is_equal)
+    cp(R("bv", 0, 256), R("bi", 0, 256))
+    mm([(R("u0", 128 * n, 128 * n + 128), [(R("im", 384 * b + 128 * n, 384 * b + 128 * n + 128), R("bv", b, 256, 2)) for b in range(2)])
         for n in range(3)])
     for a in (0, 1024):
-        lin("av", R("ft", 4095 - a, 3071 - a, -1), R("ft", 4096 + a, 5120 + a), -1.0, 255.0)
-        dma("s", R("ft", 1024 - a, 2048 - a), R("ft", 3072 - a, 4096 - a), 256)
-    for jl in range(4):
-        for h, B in enumerate(("rb", "xa")):
-            lin("av", R("kt", 512 * jl + 256 * h, 512 * jl + 256 * h + 256), R(B, 0, 256), col(MK + jl), col(MB + jl))
-    dma("g", R("yv", 0, 2048), T.faces[:], 1024, after=[R("kt", 0, 8)])
-    dma("s", T.yx[:, 0:2048], T.faces[:], 512, after=[R("yv", 0, 8)])
-    lin("av", R("pt0", 0, 256), R("pt0", 0, 256), 1.0, col(CJ))
+        step(-1, "pos")
+        if PLUS:
+            lin("av", R("ft", POS + a, POS + a + 1024), R("fs", a, a + 1024), 1.0, 1.0)
+            dma("s", R("ft", UP + a, UP + a + 1024), R("ft", POS + a, POS + a + 1024), 256)
+        step(-1, "neg")
+        lin("av", R("ft", 4095 - a, 3071 - a, -1), FS(a, a + 1024), -1.0, 255.0 + PLUS)
+        dma("a", R("ft", 1024 - a, 2048 - a), R("ft", 3072 - a, 4096 - a), 256)
+    step(0, "round3")
+    for h in SEL:
+        lin("av", R("yv", 1024 * h, 1024 * h + 1024), FS(1024 * h, 1024 * h + 1024), 1.0, CY + PLUS)
+    if SEL:
+        for h in set(range(2)) - set(SEL):
+            for t in range(5):
+                dma("s", R("yv", 2048 * t + 1024 * h, 2048 * t + 1024 * h + 1024), R("yv", 1024 * SEL[0], 1024 * SEL[0] + 1024), 512)
+        iota(R("pt0", 0, 256), [[16, 128], [-2048, 2]], 2048, 0)
+        lin("av", R("pt0", 0, 256), R("pt0", 0, 256), 1.0, col(CJ))
+        iota(R("gi", 0, 256), [[0, 256]], -2 ** 20, 0)
+        lin("av", R("ik2", 0, 128), ID, CKID / FAR)
+        lin("av", R("two", 0, 128), ID, 2.0)
+    step(0, "val3")
+    for a in (2048, 4096, 6144):
+        dma("s", R("kt", a, a + 2048), R("kt", 0, 2048), 512, after=[R("ft", 0, 8), R("ft", 1024, 1032)])
+    step(-1, "belts")
     lin("av", R("sc0", 1, 16, 2), R("cn", 128, 136))
-    lin("av", R("land0", 0, 8), R("cn", 128, 136))
-    lin("av", R("sc1", 1, 16, 2), R("pt0", 1, 16, 2))
-    ts(col(CWM), col(CJ), 7.5, 0.5, A.is_lt, A.subtract)
+    iota(R("fx", 0, 16), [[0, 16]], 0, 0)
+    for h in range(2):
+        iota(win(h, WF_ + 4, WH_), [[0, 4]], 0, 0)
+        lin("av", FF(h), R("cn", 128 + 4 * h, 132 + 4 * h), 1.0, -0.5)
+    lin("av", R("sc1", 1, 16, 2), R("mv", 0, 8), 1.0, col(CJ))
     scan(R("sco", 0, 16), R("sc0", 0, 16), R("sc1", 0, 16), A.mult, A.add)
     cp(R("ofb", 0, 8), R("sco", 1, 16, 2))
-    lin("av", R("cand", 0, 256), R("z0", 0, 256), 1.0, 0.25)
-    lin("av", R("cand", 256, 512), R("z0", 128, 384), 1.0, 0.25)
-    lin("av", R("cm", 0, 144), R("bc", 0, 144), col(CWM))
-    lin("av", R("land0", 8, 136), IND(R("cand", 0, 384), R("ofb", 0, 8)))
-    lin("av", R("cd", 0, 144), R("bc", 0, 144), -0.5 if PLAN["sign"] else -1.0)
-    lin("av", R("land0", 136, 264), IND(R("cand", 128, 512), R("ofb", 0, 8)))
+    lin("av", R("c0", 0, 384), R("u0", 0, 384))
+    cp(R("ke", 0, 128), IND(R("c0", 0, 256), R("ofb", 0, 8)))
+    cp(R("ke", 128, 256), IND(R("c0", 128, 384), R("ofb", 0, 8)))
+    for h in range(2):
+        lin("av", R("sc1", 8 * h + 1, 8 * h + 8, 2), R("sc1", 8 * h + 1, 8 * h + 8, 2), 1.0, WCK - 64.0 * h)
+    ts(R("abi", 0, 128), R("ke", 0, 128), 1, 2047, A.arith_shift_right, A.bitwise_and)
+    cp(R("ofk", 0, 128), R("abi", 0, 128))
+    step(-1, "vals")
+    to_val(R("u1", 0, 256), R("ke", 0, 256), R("t4", 0, 256), R("t5", 0, 256), R("u1", 256, 512))
+    ts(R("land0", 0, 128), R("u1", 128, 256), MID + 0.25, None, A.add)
+    for h in range(2):
+        lin("av", K(h), R("u1", 64 * h, 64 * h + 64), 1.0, 0.25)
+        lin("av", H(h), R("u1", 128 + 64 * h, 192 + 64 * h), 1.0, 0.25)
 
     def late_constants():
-        lin("av", R("nw", 128, 256), R("pt0", 0, 256, 2), 1.0, 0.5)
-        ms(R("nw", 256, 512, 2), 0.0)
+        lin("av", col(CM), col(CJ), 1.0, 2056.5)
+        lin("av", R("cn", 128, 256), R("mv", 0, 128), 1.0, col(CM))
 
     def last_constants():
         cp(R("kf", 0, 256), R("ki", 0, 256))
-        dma("s", T.y0[:, 0:2048], R("kf", 0, 128), 64, after=[R("kt", 0, 2048)])
-        dma("s", T.y1[:, 0:2048], R("kf", 128, 256), 64, after=[R("kt", 0, 2048)])
-        ts(col(CX8), col(CJ), 8.0, None, A.mult)
-        ts(R("lt", 16, 32), R("li", 48, 64), col(CGG), col(CJ), A.mult, A.add)
-        ts(R("lt", 0, 16), R("li", 32, 48), col(CGG), col(CX8), A.mult, A.add)
+        dma("s", T.yx[:, 0:2048], T.faces[:], 512, after=[R("ofk", 0, 8)])
+        dma("s", T.y0[:, 0:2048], R("kf", 0, 128), 64)
+        dma("s", T.y1[:, 0:2048], R("kf", 128, 256), 64)
+        lin("av", col(CX8), col(CJ), 8.0)
+        lin("av", R("lt", 16, 32), R("li", 48, 64), col(CGG), col(CJ))
+        lin("av", R("lt", 0, 16), R("li", 32, 48), col(CGG), col(CX8))
         tt(R("lt", 0, 32), R("lt", 0, 32), R("li", 0, 32), A.add)
         cp(R("lu", 0, 32), R("lt", 0, 32))
 
-    FT = R("ft", 0, 8192)
-    GO = R("nw", 257, 512, 2)
-    PR = R("db", 256, 512)
+    FT = R("ft", 0, 8208)
 
-    def gather(eng, out, a, b, win, offbuf, off0, scale=1.0, bias=0.0, base=0):
-        lin(eng, R(out, base + a, base + b), IND(win, R(offbuf, off0 + a // 16, off0 + b // 16)), scale, bias)
+    def gather(eng, out, a, b, win, offbuf, off0=0):
+        lin(eng, R(out, a, b), IND(win, R(offbuf, off0 + a // 16, off0 + b // 16)))
 
     def prep(t):
-        L = "land%d" % t
-        K = R(L, 8, 136)
-        if t > 0:
-            recv(t, "k", 0, 136)
-            recv(t, "h", 136, 264)
-        ts(R("ofh", 0, 128), R(L, 136, 264), 4095.5, None, A.add)
-        if PLAN["sign"]:
-            act(R("s2", 0, 128), K, 1.0, 0.0, F.Sign)
-            act(R("ab", 0, 128), K, 0.5, 0.0, F.Abs)
-        else:
-            ts(R("s2", 0, 128), K, 0.0, 0.5, A.is_gt, A.subtract)
-            tt(R("ab", 0, 128), R("s2", 0, 128), K, A.mult)
-            act(R("ab", 0, 128), K, 0.5, 0.0, F.Abs)
-            either()
-        if t == 0:
-            ts(R("abi", 0, 128), R("ab", 0, 128), 2.0, -0.5, A.mult, A.add)
-            ts(R("abi", 0, 128), R("abi", 0, 128), 2047, None, A.bitwise_and)
-            cp(R("ofk", 0, 128), R("abi", 0, 128))
-        else:
-            ts(R("ofk", 0, 128), R("ab", 0, 128), 2.0, -0.5, A.mult, A.add)
+        for h in range(2):
+            a, b = 64 * h, 64 * h + 64
+            step(t, "conv%d" % h)
+            recv(t, h)
+            ts(win(h, WK, WSK), R("land%d" % t, 136 * h, 136 * h + 136), -MID, None, A.add)
+            AB, RR, X = R("ab", a, b), R("rr", a, b), R("xa", 384 + a, 384 + b)
+            act(AB, K(h), 1.0, 0.0, F.Abs)
+            ts(R("ng", a, b), R("land%d" % t, 136 * h, 136 * h + 64), MID, 4096.0, A.is_lt, A.mult)
+            ts(RR, AB, C16, -C16, A.add, A.add)
+            mm([(X, [(ID, R("ng", a, b)), (R("rc", 0, 128), AB), (R("ra", 0, 128), RR), (R("rb", 0, 128), RR)])])
+            ts(R("ofk", a, b), X, 1919.0, None, A.add)
 
     def visit(t):
-        L, S, last = "land%d" % t, "snd%d" % t, t == 3
-        KT = R("kt", 0, 2048 if t == 0 else 4096)
-        yb = 2048 * (t + 1)
-        FF, K, H, KH = R(L, 0, 8), R(L, 8, 136), R(L, 136, 264), R(L, 8, 264)
-        FN = R(S, 0, 8)
+        S, last = "snd%d" % t, t == 3
+        KT = R("kt", 0, 2048 if t == 0 else 8192)
 
-        def kid(e, a, b):
-            gather(e, "g1", a, b, KT, "ofk", 0)
+        def DK(h):
+            return R("ms", 256 + 64 * h, 320 + 64 * h)
 
-        def fw(e, a, b):
-            gather(e, "fw", a, b, FT, "ofh", 0)
+        def DH(h):
+            return R("ms", 384 + 64 * h, 448 + 64 * h)
 
-        def extract(c):
-            X = "xa" if c == 0 else "xb"
-            mm([(R(X, 64 * n, 64 * n + 64), [(ext(w, i), R("g1", 1024 * c + i, 1024 * c + 1024, 16)) for i in range(16)])
-                for n, w in enumerate(("cd", "cm"))])
+        def pick(out, w, c):
+            mm([(out, [(ext(w, i), R("g1", 1024 * c + i, 1024 * c + 1024, 16)) for i in range(16)])])
 
         def kids_of(c):
             X = "xa" if c == 0 else "xb"
             lo, hi = 64 * c, 64 * c + 64
-            tt(R("sd", lo, hi), R(X, 0, 64), R("s2", lo, hi), A.mult)
-            tt(R("uu", lo, hi), R(X, 64, 128), R("sd", lo, hi), A.add)
-            tt(R("nw", lo, hi), R(X, 64, 128), R("sd", lo, hi), A.subtract)
-            ts(R("ofu", lo, hi), R("uu", lo, hi), 4095.5, None, A.add)
+            step(t, "u%d" % c)
+            if t == 0:
+                pick(R(X, 0, 64), "cu", c)
+                pick(R(X, 64, 128), "ca", c)
+                tt(R("sd", lo, hi), R(X, 0, 64), R("t5", lo, hi), A.mult)
+                tt(R("uu", lo, hi), R(X, 64, 128), R("sd", lo, hi), A.add)
+                tt(R("cn", 384 + lo, 384 + hi), R(X, 64, 128), R("sd", lo, hi), A.subtract)
+                ts(R("ofu", lo, hi), R("uu", lo, hi), MID, None, A.add)
+            else:
+                U = R("xa", lo, hi)
+                pick(U, "cp", c)
+                ts(R("ofu", lo, hi), U, MID, None, A.add)
+                step(t, "a%d" % c)
+                pick(R("cn", 384 + lo, 384 + hi), "cr", c)
+                if c:
+                    step(t, "uu1")
+                    lin("av", R("uu", 0, 128), R("xa", 0, 128))
 
         def diff(a, b):
             tt(R("dd", a, b), IND(FT, R("ofu", a // 16, b // 16)), R("fw", a, b), A.subtract)
@@ -528,157 +737,230 @@ def rank_program(g, core, T, topo):
 
         def q_(n, q):
             return R(n, 512 * q, 512 * q + 512)
-        ID, HID, NID = R("idp", 12, 140), R("hid", 0, 128), R("nid", 0, 128)
-
-        def mean(q, own):
-            mm([(R("z%d" % (q % 2), 0, 512), [(ID, q_("dd", q)), (ID if own else HID, q_("fw", q))])])
-
-        def rnd(q):
-            lin("av", R("yv", yb + 512 * q, yb + 512 * q + 512), R("z%d" % (q % 2), 0, 512), 0.5 - 2.0 ** -11, CY)
 
         def values(q):
+            step(t, "val%d" % q)
             if q in PLAN["own"]:
-                X = R("xa" if q % 2 == 0 else "xb", 0, 512)
-                gather("a", "dd", 512 * q, 512 * q + 512, FT, "ofu", 0)
+                X = R("xb", 0, 512)
+                gather("a", "dd", 512 * q, 512 * q + 512, FT, "ofu")
                 mm([(X, [(ID, q_("dd", q)), (NID, q_("fw", q))])])
                 ts(q_("ind", q), X, C32, C32, A.add, A.is_equal)
-            elif q == 0 and PLAN["big"]:
-                diff(0, 1024)
-                near(0, 1024)
-            elif q != 1 or not PLAN["big"]:
+            else:
                 diff(512 * q, 512 * q + 512)
-                near(512 * q, 512 * q + 512)
+                if q ^ 1 in PLAN["own"]:
+                    near(512 * q, 512 * q + 512)
+                elif q % 2:
+                    near(512 * q - 512, 512 * q + 512)
+
+        def bank(b):
+            return R("u%d" % b, 0, 512)
+
+        def oldf(b, base, w="ft"):
+            a = base + 1024 * (b // 2) + b % 2
+            return R(w, a, a + 1023, 2)
+
+        def change(b):
+            step(t, "change%d" % b)
+            if b // 2 in SEL:
+                acc([(bank(b), ID if b in PLAN["own"] else R("two", 0, 128), q_("fw", b))], first=True)
+                acc([(bank(b), ID, q_("dd", b))], final=True)
+                step(t, "round%d" % b)
+                lin("av", R("yv", 2048 * (t + 1) + 512 * b, 2048 * (t + 1) + 512 * b + 512), bank(b), 0.5 - 2.0 ** -11, CY)
+                return
+            step(t, "start")
+            acc([(bank(b), NID, oldf(b, POS if t == 0 else UP))], first=True)
+            step(t, "change%d" % b)
+            for w, n in (("f", "fw"), ("d", "dd")):
+                qs = (2 * (b // 2), 2 * (b // 2) + 1)
+                lw = [R("hid" if w == "d" else "wh" if q in PLAN["own"] else "wf", 0, 128) for q in qs]
+                if lw[0] == lw[1]:
+                    acc([(bank(b), lw[0], R(n, 512 * qs[0] + b % 2, 512 * qs[0] + 1024, 2))])
+                else:
+                    acc([(R("u%d" % b, 256 * h, 256 * h + 256), lw[h], R(n, 512 * q + b % 2, 512 * q + 512, 2)) for h, q in enumerate(qs)])
+
+        def renew(b):
+            def wipe(m):
+                return [(R("u%d" % b, jj, 512, 8), R("lj", 128 * (2 * jj + b % 2), 128 * (2 * jj + b % 2) + 128), R(m, 64 * (b // 2), 64 * (b // 2) + 64))
+                        for jj in range(8)]
+            step(t, "renew%d" % b)
+            if b // 2 in SEL:
+                lin("av", R("ft", UP + 512 * b, UP + 512 * b + 512), IND(R("yv", 0, 2048 * (t + 2)), R("ptu", 32 * b, 32 * b + 32)), 1.0, -CY - (PLUS if last else 0.0))
+                return
+            acc(wipe("gz"))
+            if last and b in PLAN["tadd"]:
+                acc(wipe("gn"), final=True)
+                lin("av", oldf(b, 0, "fs"), oldf(b, UP), 1.0, -1.0)
+                tt(oldf(b, UP), oldf(b, 0, "fs"), bank(b), A.add)
+            elif not last and b in PLAN["vadd"]:
+                acc(wipe("gn"), final=True)
+                tt(oldf(b, UP), oldf(b, UP), bank(b), A.add)
+            else:
+                acc(wipe("gn") + [(bank(b), ID, oldf(b, POS if t == 0 else UP))], final=True)
+                lin("av", oldf(b, UP), bank(b), 1.0, -1.0 if last else 0.0)
 
         GQ = PLAN["gq"]
         for a in range(0, 2048, GQ):
-            kid("av", a, a + GQ)
-        extract(0)
-        extract(1)
+            step(t, "kid%d" % (a // 512))
+            gather("av", "g1", a, a + GQ, KT, "ofk")
         for a, b in PLAN["fq"]:
-            fw("av", a, b)
-        kids_of(0)
-        kids_of(1)
+            step(t, "fw%d" % (a // 512))
+            gather("av", "fw", a, b, FT, "land%d" % t, 72 * (1 + a // 1024) if t else 0)
+        step(t, "")
         if t == 0:
             late_constants()
+            step(t, "val1")
             for n, w in enumerate(("cp", "cr")):
-                mm([(R("db", 256 + 128 * n, 384 + 128 * n), [(ext(w, i), R("kt", i, 2048, 16)) for i in range(16)])])
-        for q in range(4):
-            values(q)
-        count(0)
-        count(1)
-        def slots(b, k, h, X, at, scale):
-            def fm(n):
-                return R("fm", 128 * n, 128 * n + 128)
-            mm([(R(X, 0, 128), [(fm(b), k), (fm(2 + b), h)]), (R(X, 128, 256), [(fm(2 + b), k), (fm(4 + b), h)])])
-            act(R("hy", 512 * b + at, 512 * b + at + 256), R(X, 0, 256), scale, -0.5, F.Abs)
+                mm([(R("ms", 128 * n, 128 * n + 128), [(ext(w, i), R("kt", i, 2048, 16)) for i in range(16)])])
+            pieces(0)
+        kids_of(0)
+        kids_of(1)
+        step(t, "kc")
+        K0, K1 = (R("ms", 0, 128), R("ms", 128, 256)) if last else (R("ms", 128, 256), R("ms", 0, 128))
+        IDF, NIDF, UU = R("idf", 0, 128), R("nidf", 0, 128), R("uu", 0, 128)
 
-        tt(R("db", 0, 256), R("nw", 0, 256), KH, A.subtract)
-        if t > 0:
-            act(R("thr", 8, 16), R("cn", 136, 144), -1.0, 0.0, F.Identity, R("thr", 1, 2))
-            ts(R("thr", 3, 4), R("thr", 1, 2), C2, -C2, A.add, A.add)
-            act(R("thr", 0, 1), R("thr", 3, 4), -1.0, R("thr", 1, 2), F.Abs)
+        def kept(p, m):
+            return [(K0 if r > 1 else K1, m if last and r < 2 else p, piece(r, min(t, 1))) for r in range(4)]
+        acc([(PR, ZB, R("h0", 0, 256))] + kept(NID, ID), first=True)
+        acc([(R("ms", K1[1] + 64 * h, K1[1] + 64 * h + 64), IDF if last else NIDF, H(h)) for h in range(2)])
+        acc([(K0, IDF, UU)])
+
+        def slots(b, w, ks, hs, X, at):
+            def fm(n):
+                return R(w, 128 * n, 128 * n + 128)
+            mm([(R(X, 128 * f + 64 * h, 128 * f + 64 * h + 64), [(fm(2 * f + b), k(h)) for k in ks] + [(fm(2 * f + 2 + b), k(h)) for k in hs])
+                for f in range(2) for h in range(2)])
+            act(R("hy", 512 * b + at, 512 * b + at + 256), R(X, 0, 256), -2.0, -0.5, F.Abs)
+
+        step(t, "g")
         if last:
             for b in range(2):
-                slots(b, K, H, "z%d" % b, 256, -2.0)
-            lin("av", R("lf", 0, 8), FF, 128.0)
+                slots(b, "fm", [K], [H], "xb", 256)
+            for h in range(2):
+                lin("av", R("lf", 4 * h, 4 * h + 4), FF(h), 128.0, 64.0 + 64 * h - WCK)
             tt(R("sc1", 1, 16, 2), R("sc1", 1, 16, 2), R("lf", 0, 8), A.add)
             ms(R("sc1", 0, 16, 2), 256.0)
-        elif PLAN["pec"]:
-            lin("av", R("sc1", 0, 16, 2), FF, 256.0, 256.0)
-            mm([(R("rb", 0, 128), [(R("neg", 128, 256), H)]), (R("rb", 128, 256), [(R("shf", 0, 128), K)]),
-                (R("rb", 256, 384), [(R("shf", 128, 256), H)]), (R("rb", 384, 512), [(R("neg", 128, 256), K)])])
-            lin("av", R("cand", 256, 768), R("rb", 0, 512))
         else:
-            lin("av", R("sc1", 0, 16, 2), FF, 256.0, 256.0)
-            mm([(R("rb", 0, 128), [(R("shf", 0, 128), K)]), (R("rb", 128, 256), [(R("shf", 128, 256), H)])])
-            lin("av", R("cand", 384, 640), R("rb", 0, 256))
-            lin("av", R("cand", 256, 384), H, -1.0)
-            lin("av", R("cand", 640, 768), K, -1.0)
-        tt(R("dpr", 0, 128), R("uu", 0, 128), R("db", 256, 384), A.subtract)
-        tt(R("dpr", 128, 256), H, R("db", 384, 512), A.subtract)
-        ts(R("spl", 0, 128), R("cn", 0, 128), R("thr", 0, 1), 8.5, A.subtract, A.is_ge)
-        mm([(R("cn", 128, 136), [(ext("bc", x), R("spl", x, 128, 16)) for x in range(16)])])
-        mm([(R("rb", 0, 128), [(R("wm", 0, 128), R("spl", 0, 128)), (R("i32", 0, 128), R("spl", 0, 128))])])
+            for h in range(2):
+                lin("av", R("sc1", 8 * h, 8 * h + 8, 2), FF(h), -float(WH_), 0.5 * WH_ - WCK)
+                dma("s", win(h, 0, WK, (1, 128)), win(h, WH_, WSK, (0, 127)), 32)
+                dma("s", win(h, WSK, WCK, (0, 127)), win(h, WK, WF_, (1, 128)), 32)
+                dma("s", win(h, 0, WK, (0, 128, 16)), win(h, WH_, WSK, (15, 128, 16)), 2)
+                dma("s", win(h, WSK, WCK, (15, 128, 16)), win(h, WK, WF_, (0, 128, 16)), 2)
         for q in range(4):
-            mean(q, q in PLAN["own"])
-            rnd(q)
-        tt(R("db", 0, 128), R("db", 0, 128), R("spl", 0, 128), A.mult)
-        tt(R("db", 128, 256), R("db", 128, 256), R("spl", 0, 128), A.mult)
-        ts(R("sc0", 1, 16, 2), R("cn", 128, 136), 4.5, None, A.is_lt)
-        tt(R("cand", 0, 256), R("db", 0, 256), KH, A.add)
-        scan(R("sco", 0, 16), R("sc0", 0, 16), R("sc1", 0, 16), A.mult, A.add)
-        tt(FN, FF, R("sc0", 1, 16, 2), A.not_equal)
-        cp(R("ofb", 0, 8), R("sco", 1, 16, 2))
-        OFF = R("ofb", 0, 8)
-        if not last:
-            lin("av", R(S, 8, 136), IND(R("cand", 0, 640), OFF))
-            lin("av", R(S, 136, 264), IND(R("cand", 128, 768), OFF))
-            send(t + 1, "k", 0, 136)
-            send(t + 1, "h", 136, 264)
-            mm([(R("cn", 136, 144), [(R("one", 0, 128), R("sc0", 1, 16, 2))])])
-        pa, pb = ("pt0", "pt1") if t % 2 == 0 else ("pt1", "pt0")
-        YV = R("yv", 0, yb + 2048)
-
-        def pointers():
-            ts(GO, R("rb", 0, 128), 36.5, None, A.is_ge)
-            scan(R(pb, 0, 256), R("nw", 256, 512), R(pa, 0, 256), A.mult, A.max)
-            tt(R("dpr", 0, 128), GO, R("dpr", 0, 128), A.mult)
-            cp(R("ptu", 0, 128), R(pb, 1, 256, 2))
+            values(q)
+        for c in range(2):
+            step(t, "count%d" % c)
+            count(c)
+        for b in range(4):
+            change(b)
+        for h in range(2):
+            step(t, "dk%d" % h)
+            tt(DK(h), K(h), R("cn", 384 + 64 * h, 448 + 64 * h), A.subtract)
+            tt(DH(h), H(h), R("cn", 128 + 64 * h, 192 + 64 * h), A.subtract)
+        step(t, "thr")
+        if t > 0:
+            act(R("thr", 8, 16), R("xa", 128, 136), -1.0, 0.0, F.Identity, R("thr", 1, 2))
+            ts(R("thr", 3, 4), R("thr", 1, 2), C2, -C2, A.add, A.add)
+            act(R("thr", 0, 1), R("thr", 3, 4), -1.0, R("thr", 1, 2), F.Abs)
+        PARTS = ((0, 64), (64, 128)) if PLUS or t in PLAN["split"] else ((0, 128),)
+        for h in range(2):
+            a, b = 64 * h, 64 * h + 64
+            SPL, NS = R("spl", a, b), R("xa", 256 + a, 256 + b)
+            step(t, "spl%d" % h)
+            ts(SPL, R("cn", a, b), R("thr", 0, 1), 8.5, A.subtract, A.is_ge)
+            mm([(NS, [(ID, R("dg", a, b)), (R("w0", 0, 128), SPL)])])
+            step(t, "open%d" % h)
+            scan(R("sd", a, b), R("dg", 128 + a, 128 + b), NS, A.add, A.min)
+            tt(DK(h), DK(h), SPL, A.mult)
+            tt(DH(h), DH(h), SPL, A.mult)
+            ts(R("sc0", 8 * h + 1, 8 * h + 8, 2), R("sd", a + 15, b, 16), 4.5, None, A.is_lt)
+            tt(win(h, WCK, WCH), DK(h), K(h), A.subtract)
+            tt(win(h, WCH, WEND), DH(h), H(h), A.subtract)
             if not last:
-                lin("av", R(pb, 0, 256, 2), R(pb, 0, 256, 2), 1.0, 2048.0)
-
-        def select(e, a, b):
-            gather(e, "ft", a, b, YV, "ptu", 0, 1.0, -CY, 6144)
-            if last:
-                dma("s", T.yx[:, 2048 + a:2048 + b], R("ft", 6144 + a, 6144 + b), (b - a) // 4)
-
-        def turn(a, b):
-            lin("av", R("ft", 2047 - a, (2047 - b) if b < 2048 else None, -1), R("ft", 6144 + a, 6144 + b), -1.0, 255.0)
-
-        def kids_new(out):
-            tt(R("dpr", 128, 256), GO, R("dpr", 128, 256), A.mult)
-            tt(out, PR, R("dpr", 0, 256), A.add)
-
+                scan(R("sco", 8 * h, 8 * h + 8), R("sc0", 8 * h, 8 * h + 8), R("sc1", 8 * h, 8 * h + 8), A.mult, A.add)
+                cp(R("ofb", 4 * h, 4 * h + 4), R("sco", 8 * h + 1, 8 * h + 8, 2))
+            tt(R("fx", 8 * h, 8 * h + 4), FF(h), R("sc0", 8 * h + 1, 8 * h + 8, 2), A.subtract)
+            if not last:
+                OFF = R("ofb", 4 * h, 4 * h + 4)
+                ts(R(S, 136 * h + 64, 136 * h + 72), R("fx", 8 * h, 8 * h + 8), -0.5, MID - 0.5, A.not_equal, A.add)
+                ts(R(S, 136 * h, 136 * h + 64), IND(win(h, 0, WCH), OFF), -1.0, MID, A.mult, A.add)
+                ts(R(S, 136 * h + 72, 136 * h + 136), IND(win(h, WK, WEND), OFF), -1.0, MID, A.mult, A.add)
+                send(t + 1, h)
+        for a, b in PARTS:
+            step(t, "spl%d" % (b // 128))
+            mm([(R("cn", 256 + a, 256 + b), [(R("wm", 0, 128), R("spl", a, b))])])
+        step(t, "open1")
+        OFF = R("ofb", 0, 8)
+        if last:
+            scan(R("sco", 0, 16), R("sc0", 0, 16), R("sc1", 0, 16), A.mult, A.add)
+            cp(OFF, R("sco", 1, 16, 2))
+        else:
+            mm([(R("xa", 128, 136), [(ONE, R("sc0", 1, 16, 2))])])
+        wipe_kids = []
+        for a, b in PARTS:
+            step(t, "go%d" % (b // 128))
+            ts(R("gz", a, b), R("cn", 256 + a, 256 + b), 36.5, KEEP, A.is_lt, A.max)
+            if a // 64 in SEL:
+                pa, pb = ("pt0", "pt1") if t % 2 == 0 else ("pt1", "pt0")
+                lin("av", R("gi", 2 * a + 1, 2 * b, 2), R("gz", a, b), -FAR)
+                scan(R(pb, 2 * a, 2 * b), R("gi", 2 * a, 2 * b), R(pa, 2 * a, 2 * b), A.add, A.max)
+                cp(R("ptu", a, b), R(pb, 2 * a + 1, 2 * b, 2))
+                if not last and b == 64 * max(SEL) + 64:
+                    step(t, "turn1")
+                    lo, hi = 128 * min(SEL), 128 * max(SEL) + 128
+                    lin("av", R(pb, lo, hi, 2), R(pb, lo, hi, 2), 1.0, 2048.0)
+                wipe_kids += [(R("ms", k + a, k + b), R("ik2", 0, 128), R("gi", 2 * a + 1, 2 * b, 2)) for k in (0, 128)]
+            else:
+                lin("av", R("gn", a, b), R("gz", a, b), -1.0)
+                wipe_kids += [(R("ms", k + a, k + b), IK, R("gn", a, b)) for k in (0, 128)]
+        step(t, "kids1")
+        acc([(k, IK, R("gz", 0, 128)) for k in (K0, K1)])
+        acc(wipe_kids + kept(ID, NID), final=True)
         if not last:
-            pointers()
-            for a in range(0, 2048, PLAN["sq"]):
-                select("av", a, a + PLAN["sq"])
+            pieces(1)
+            for r in range(8):
+                dma("sa"[r % 2], R("kt", 4096 * (r // 4), 4096 * (r // 4) + 4096, 1, (4 * (r % 4), 128, 16)), R("hl", 256 * ((r + r // 4 * 2) % 4), 256 * ((r + r // 4 * 2) % 4) + 256), 64)
+            for b in range(4):
+                renew(b)
             for a in range(0, 2048, PLAN["tq"]):
-                turn(a, a + PLAN["tq"])
-            kids_new(PR)
-            hilo(PR)
-            for h, B in enumerate(("xa", "rb")):
-                mm([(R(B, a, 256, 4), [(R("su", 160 * a + 12 + 4 * a - 4 * r, 160 * a + 140 + 4 * a - 4 * r),
-                                        R("hl", PIECE[r] + 64 * h, PIECE[r] + 64 * h + 64)) for r in range(4)]) for a in range(4)])
-            for jl in range(4):
-                lin("av", R("kt", 2048 + jl, 3072, 4), R("xa", 0, 256), col(MK + jl))
-            for jl in range(4):
-                lin("av", R("kt", 3072 + jl, 4096, 4), R("rb", 0, 256), col(MK + jl))
+                b = a + PLAN["tq"]
+                step(t, "turn%d" % (a // 1024))
+                lin("av", R("ft", 2047 - a, (2047 - b) if b < 2048 else None, -1), R("ft", UP + a, UP + b), -1.0, 255.0 + 2 * PLUS)
             prep(t + 1)
+            step(t, "")
             if t == 1:
                 last_constants()
-        else:
+        if last:
+            step(t, "slots")
+            for h in range(2):
+                lin("av", R("h0", 128 * h, 128 * h + 128), win(h, WCK, WEND))
+                tt(R("h0", 256 + 128 * h, 384 + 128 * h), win(h, WCK, WEND), R("h0", 128 * h, 128 * h + 128), A.subtract)
+
+            def part(a):
+                return lambda h: R("h0", a + 128 * h, a + 128 * h + 64)
             for b in range(2):
-                slots(b, R("cand", 0, 128), R("cand", 128, 256), "xa" if b == 0 else "xb", 0, 2.0)
-            pointers()
-            for a in range(0, 2048, 512):
-                select("av", a, a + 512)
-            kids_new(R("old", 256, 512))
-            lin("av", R("fnb", 0, 8), FN)
-            act(R("tr0", 0, 256), IND(R("old", 256, 512), R("lu", 0, 16)), 2.0, -0.5, F.Abs)
-            mm([(R("z1", x, 128, 16, (0, 8)), [(R("idp", 12 + x, 140, 16), R("fnb", 0, 8))]) for x in range(16)])
+                slots(b, "fmb", [part(0), part(256)], [part(64), part(320)], "u0" if b == 0 else "xb", 0)
+            for b in range(4):
+                renew(b)
+                for a in ((512 * b,) if b // 2 in SEL else (512 * b - 512, 512 * b) if b % 2 else ()):
+                    dma("sa"[a // 512 % 2], T.yx[:, 2048 + a:2560 + a], R("ft", UP + a, UP + a + 512), 128)
+            step(t, "out0")
+            lin("av", R("old", 0, 256), PR)
+            act(R("tr0", 0, 256), IND(R("old", 0, 256), R("lu", 0, 16)), 2.0, -0.5, F.Abs)
             add("v", lambda: g.vector.transpose(ap(R("tr1", 0, 256)), ap(R("tr0", 0, 256))), [R("tr0", 0, 256)], [R("tr1", 0, 256)], 262.0)
-            lin("av", R("tr2", 0, 256), IND(R("tr1", 0, 256), R("lu", 16, 32)), 1.0, -0.5)
-            for b in range(2):
-                lin("av", R("yb1", b, 256, 2), IND(R("hy", 512 * b, 512 * b + 512), OFF), 1.0, -0.5)
+            lin("av", R("tr2", 0, 256), IND(R("tr1", 0, 256), R("lu", 16, 32)), 1.0, -16.5)
             dma("s", T.y0[:, 2048:4096], R("tr2", 0, 128), 64)
             for gq in range(8):
                 dma("s" if gq % 2 else "a", T.y1[gq ^ 1, 2048:4096], R("tr2", 128, 256, 1, (16 * gq, 16 * gq + 16)), 8)
-            lin("av", R("yfo", 0, 128, 1, (0, 8)), R("z1", 0, 128, 1, (0, 8)))
+            step(t, "out1")
+            ts(R("fnb", 0, 16), R("fx", 0, 16), -0.5, None, A.not_equal)
+            mm([(R("cn", 384 + 64 * h + x, 448 + 64 * h, 16, (0, 8)), [(R("idp", 12 + x, 140, 16), R("fnb", 8 * h, 8 * h + 4))]) for x in range(16) for h in range(2)])
+            for b in range(2):
+                lin("av", R("yb1", b, 256, 2), IND(R("hy", 512 * b, 512 * b + 512), OFF), 1.0, -16.5)
+            lin("av", R("yfo", 0, 128, 1, (0, 8)), R("cn", 384, 512, 1, (0, 8)))
             dma("s", T.yb[:], R("yb1", 0, 256), 128)
             dma("s", T.yf[:], R("yfo", 0, 128, 1, (0, 8)), 4)
 
-    prep(0)
     for t in range(4):
         visit(t)
 
@@ -706,6 +988,8 @@ def rank_program(g, core, T, topo):
                 bank[s[0]][o["e"]] = n
         newest = {}
         for d in deps:
+            if o["e"] == "p" and ops[d]["e"] == "p":
+                continue
             k = ops[d]["e"] if ops[d]["k"] == "c" else d
             newest[k] = max(newest.get(k, -1), d)
         o["deps"] = sorted(newest.values())

import numpy as np
from concourse.mybir import dt, AluOpType as A, AxisListType, ActivationFunctionType as F

F32, BF, I32, U16 = "float32", "bfloat16", "int32", "uint16"
SCRATCH = {}
for _n, _w, _d in [
    ("ft", 8208, BF), ("kt", 8192, BF), ("nidf", 128, F32), ("ra", 128, BF), ("rb", 128, BF), ("rc", 128, F32), ("ab", 128, F32), ("rr", 128, BF), ("ng", 128, BF),
    ("two", 128, BF), ("ik2", 128, BF), ("gi", 256, BF), ("yv", 10240, F32), ("pt0", 256, F32), ("pt1", 256, F32), ("ptu", 128, U16),
    ("w0", 128, BF), ("dg", 256, BF), ("fs", 2048, BF), ("lj", 2048, BF), ("g1", 2048, BF), ("fw", 2048, BF), ("dd", 2048, BF),
    ("ind", 2048, BF), ("wn", 784, F32), ("c0", 384, F32), ("land0", 272, U16), ("land1", 272, U16), ("land2", 272, U16), ("land3", 272, U16),
    ("snd0", 272, U16), ("snd1", 272, U16), ("snd2", 272, U16), ("ofb", 8, U16), ("fx", 16, F32),
    ("old", 256, F32), ("abi", 128, I32), ("ofk", 128, U16), ("ofu", 128, U16), ("ramp", 8, F32),
    ("sd", 128, F32), ("spl", 128, BF), ("gz", 128, BF), ("gn", 128, BF), ("uu", 256, F32), ("mv", 128, F32),
    ("h0", 512, BF), ("hl", 1024, BF), ("sc0", 16, F32), ("sc1", 16, F32), ("sco", 16, F32), ("fnb", 16, BF), ("thr", 16, F32),
    ("ki", 256, I32), ("bi", 256, I32), ("fi", 128, I32), ("fb", 128, BF), ("t1", 256, I32), ("t2", 256, F32),
    ("t4", 256, I32), ("t5", 256, F32), ("ke", 256, I32), ("bv", 256, F32),
    ("kf", 256, F32), ("iv", 384, F32), ("pi", 8, I32), ("ci", 8, I32), ("cf", 32, F32), ("ex", 864, BF), ("e8", 16, BF),
    ("b8", 144, BF), ("idp", 160, BF), ("nid", 128, BF), ("hid", 128, BF), ("wm", 128, BF), ("wf", 128, BF), ("wh", 128, BF),
    ("ik", 128, BF), ("idf", 128, F32), ("zb", 128, BF), ("zf", 128, F32), ("eps", 128, BF),
    ("im", 768, F32), ("fm", 768, F32), ("fmb", 768, BF), ("shf", 256, F32), ("one", 128, F32), ("oneb", 160, BF),
    ("li", 64, F32), ("lt", 32, F32), ("lu", 32, U16), ("tr0", 256, F32), ("tr1", 256, F32), ("tr2", 256, F32),
    ("hy", 1024, F32), ("lf", 8, F32), ("yb1", 256, F32), ("yfo", 128, F32),
]:
    SCRATCH[_n] = ("sbuf", [128, _w], _d)
PSUM = ["xa", "xb", "cn", "ms", "u0", "u1", "u2", "u3"]
for _n in PSUM:
    SCRATCH[_n] = ("psum", [128, 512], F32)
NDMA = 90
SEMAPHORES = ["ev", "ea", "ep", "eg"] + ["%s%d%d" % (_a, _t, _h) for _a in ("arr", "out") for _t in (1, 2, 3) for _h in (0, 1)] + ["dm%d" % _i for _i in range(NDMA)]

CY = 1.5 * 2.0 ** 23
C2 = 1.5 * 2.0 ** 24
C16 = 1.5 * 2.0 ** 27
FAR = 16384.0
C32 = 1.5 * 2.0 ** 28
KEEP = 2.0 ** -17
CFACE = 1.5 * 2.0 ** 40
CKID = 1.5 * 2.0 ** 39
MID = 4103.5
POS, UP = 4112, 6160
WK, WF_, WH_, WSK, WCK, WCH, WEND = 64, 128, 136, 200, 264, 328, 392


def R(name, a, b, step=1, p=None):
    return (name, a, b, step, p)


def IND(win, off):
    return ("*", win, off)


def _cols(s):
    return range(s[1], s[2], s[3]) if s[3] > 0 else range(s[1], -1 if s[2] is None else s[2], s[3])


def _bits(r):
    m = 0
    for c in r:
        m |= 1 << c
    return m


PLAN = {"sel": (0, 1), "split": (0, 1, 2, 3), "pe": 0.5, "pf": 4.0, "gat": 1.56, "hop": 3500.0, "wake": 160.0, "ov": 60, "oa": 100, "big": 1, "tq": 1024, "dlat": 2000.0,
        "fq": ((0, 512), (512, 1024), (1024, 1536), (1536, 2048)), "seed": 1, "mean": 0.03, "steps": 500, "heat": 150.0, "own": (3,), "cycle": 12400.0, "tries": 0, "shake": 2500.0, "warm": 200.0, "first": 5300.0, "pin": 4, "gq": 512,
        "vadd": (), "tadd": (), "bias": 300.0, "span": 10000.0, "look": 8000.0, "sweeps": 24}
_PLANS = {}
STEP = {"flip": (2.2, "v"), "kids": (2.8, "a"), "pos": (3.1, "a"), "neg": (5.6, "v"), "belts": (3.0, "a"), "vals": (7.0, "a"), "marks": (1.5, "g"),
        "conv0": (0.0, "v"), "conv1": (2.2, "v"), "fw0": (1.2, "a"), "fw1": (2.8, "a"), "fw2": (4.3, "a"), "fw3": (5.0, "a"),
        "kid0": (2.0, "v"), "kid1": (2.0, "a"), "kid2": (4.2, "v"), "kid3": (4.2, "a"), "u0": (2.9, "v"), "u1": (5.1, "v"), "a0": (3.6, "p"), "a1": (5.8, "p"), "uu1": (7.0, "a"),
        "val0": (3.6, "v"), "val1": (4.9, "v"), "val2": (6.6, "v"), "val3": (5.9, "a"), "count0": (6.0, "p"), "count1": (8.4, "p"), "kc": (7.6, "p"), "start": (-0.5, "p"),
        "change0": (4.5, "p"), "change1": (5.7, "p"), "change2": (7.4, "p"), "change3": (6.8, "p"), "g": (3.0, "a"), "dk0": (5.8, "v"), "dk1": (7.5, "v"), "thr": (-1.0, "a"),
        "round0": (6.7, "a"), "round1": (7.2, "a"), "round2": (8.2, "a"), "round3": (7.7, "a"), "spl0": (6.7, "v"), "spl1": (9.1, "v"), "open0": (7.6, "v"), "open1": (9.4, "v"),
        "go0": (8.6, "a"), "go1": (9.2, "a"), "kids1": (9.6, "a"), "renew0": (9.0, "a"), "renew1": (9.8, "a"), "renew2": (11.0, "v"), "renew3": (11.0, "a"),
        "turn0": (11.8, "v"), "turn1": (12.3, "v"), "slots": (10.0, "a"), "out0": (9.8, "a"), "out1": (11.0, "a")}


def _len(s):
    if s[0] == "*":
        return 16 * _len(s[2])
    return len(_cols(s))


def _cost(e, out, a, b=None):
    n = _len(out)
    if a[0] == "*":
        return PLAN["ov" if e == "v" else "oa"] + n * PLAN["gat"] * 0.83
    k = 1.0
    if b is not None:
        k = 1.0 if a[0] in PSUM or b[0] in PSUM else 2.0
    elif e == "v" and SCRATCH[out[0]][2] in (BF, U16) and SCRATCH[a[0]][2] in (BF, U16):
        k = 0.5
    return PLAN["ov" if e == "v" else "oa"] + max(64, n * k) * 0.83


def _edges(ops):
    hist, masks, out = {}, {}, []
    for n, o in enumerate(ops):
        deps = {}
        acc = [(s, False) for s in o["r"]] + [(s, True) for s in o["w"]]
        for s, wr in acc:
            if s[1:] not in masks:
                masks[s[1:]] = (_bits(_cols(s)), _bits(range(128) if s[4] is None else range(*s[4])))
            m, pm = masks[s[1:]]
            for (m2, pm2), n2, w2 in hist.get(s[0], ()):
                if (wr or w2) and m & m2 and pm & pm2:
                    deps[n2] = deps.get(n2, False) or (w2 and not wr)
        for s, wr in acc:
            hist.setdefault(s[0], []).append((masks[s[1:]], n, wr))
        out.append(deps)
    return out


def _plan(ops, edges):
    n = len(ops)
    pre = [set(d) for d in edges]
    for i, o in enumerate(ops):
        if o["k"] == "x":
            pre[i].add(max(j for j in range(i) if ops[j]["k"] == "r" and ops[j]["sem"][0][3:] == o["sem"][0][3:]))
    pre = [[j for j in p if not any(j in pre[k] for k in p)] for p in pre]
    loads = [i for i in range(n) if ops[i]["k"] == "d" and not edges[i]]
    post = [[] for _ in ops]
    for i in range(n):
        for j in pre[i]:
            post[j].append(i)
    wake = PLAN["wake"]
    cost = [{e: c for e, (_, c) in o["alt"].items()} for o in ops]
    lat = [o["lat"] + wake for o in ops]
    banks = [sorted(set(s[0] for s in o["r"] + o["w"] if s[0] in PSUM)) for o in ops]
    pe = [o["k"] == "c" and "p" in o["alt"] for o in ops]
    fore = [[(j, 0.0 if pe[i] and pe[j] else lat[j]) for j in pre[i]] for i in range(n)]
    aft = [[(j, 0.0 if pe[i] and pe[j] else lat[i]) for j in post[i]] for i in range(n)]

    def fit(busy, i, e, t):
        c, mine = cost[i][e], busy[e]
        while True:
            t1 = t
            k = len(mine)
            while k and mine[k - 1][1] > t:
                k -= 1
            while k < len(mine) and mine[k][0] < t + c:
                t = mine[k][1]
                k += 1
            for b in banks[i]:
                for s0, s1, e2 in busy[b]:
                    if s1 + wake > t and s0 < t + c + wake and e2 != e:
                        t = s1 + wake
            if t == t1 or not banks[i]:
                return t, k

    def place(seq, eng, back, bias=None):
        busy = {k: [] for k in list("vapgsx") + PSUM}
        start, end = [0.0] * n, [0.0] * n
        for i in (seq if back else loads + [i for i in seq if i > loads[-1]]):
            t = lat[i] if back else 0.0
            for j, d in (aft[i] if back else fore[i]):
                if end[j] + d > t:
                    t = end[j] + d
            e = eng[i]
            if bias is not None and len(cost[i]) > 1:
                ta, tv = fit(busy, i, "a", t)[0] + cost[i]["a"], fit(busy, i, "v", t)[0] + cost[i]["v"]
                e = eng[i] = "a" if ta <= tv + bias else "v"
            t, k = fit(busy, i, e, t)
            c = cost[i][e]
            busy[e].insert(k, (t, t + c))
            for b in banks[i]:
                busy[b].append((t, t + c, e))
            start[i], end[i] = t, t + c
        return max(end[i] + lat[i] for i in range(n)) + PLAN["mean"] * sum(end) / n, start, end

    def ranked(key):
        key = list(key)
        for i in range(n):
            for j in pre[i]:
                if key[j] > key[i]:
                    key[i] = key[j]
        return sorted(range(n), key=lambda i: key[i])

    def justify(seq, eng, bias):
        v, start, end = place(seq, eng, False, bias)
        for _ in range(2):
            _, _, e2 = place(sorted(range(n), key=lambda i: (-end[i], -i)), eng, True)
            s2 = sorted(range(n), key=lambda i: (-e2[i], i))
            v2, st2, en2 = place(s2, eng, False)
            if v2 >= v - 1.0:
                break
            v, seq, start, end = v2, s2, st2, en2
        return v, seq, start, end

    prio = [0.0] * n
    for i in range(n - 1, -1, -1):
        prio[i] = min(cost[i].values()) + lat[i] + max([prio[j] for j in post[i]] + [0.0])
    rng = np.random.RandomState(PLAN["seed"])
    eng = [("a" if "a" in c else list(c)[0]) for c in cost]
    key = [max(prio) - p for p in prio]
    best, seq, start, end = justify(ranked(key), eng, PLAN["bias"])
    zero = [start[i] for i in range(n) if ops[i]["k"] == "x"]
    zero = [zero[0] - PLAN["cycle"]] + [zero[0] + k * PLAN["cycle"] for k in range(3)]
    zero = [z - zero[0] + PLAN["first"] for z in zero] + [0.0]
    for i, o in enumerate(ops):
        key[i] = start[i]
        if o["at"]:
            x, e = STEP[o["at"][1]]
            key[i] = zero[o["at"][0]] + 1000.0 * x
            if e in cost[i]:
                eng[i] = e
        elif o["k"] == "c" and start[i] < zero[1]:
            key[i] = 0.5 * (max(prio) - prio[i])
    twin, seen = {}, {}
    for i, o in enumerate(ops):
        k = o["at"] or i
        seen[k] = seen.get(k, 0) + 1
        twin.setdefault((o["at"][1], seen[k]) if o["at"] and o["at"][0] in (1, 2) else i, []).append(i)
    twin = [l for l in twin.values() if ops[l[0]]["k"] != "x" and l[0] not in loads]
    cur = place(ranked(key), eng, False)[0]
    keep = (cur, key, eng)
    for it, (r0, r1, r2, r3) in enumerate(rng.rand(PLAN["tries"], 4).tolist()):
        k2, e2, l = list(key), eng, twin[int(r0 * len(twin))]
        if r1 < 0.3 and len(cost[l[0]]) > 1:
            e2 = list(eng)
            for i in l:
                e2[i] = "v" if eng[l[0]] == "a" else "a"
        else:
            for i in l:
                k2[i] += (r2 - 0.5) * PLAN["shake"]
        x = place(ranked(k2), e2, False)[0]
        if x <= cur + PLAN["warm"] * r3 * (1.0 - it / PLAN["tries"]):
            cur, key, eng = x, k2, e2
            if x < keep[0]:
                keep = (x, k2, e2)
    eng = list(keep[2])
    best, seq, start, end = justify(ranked(keep[1]), eng, None)
    posts = [set(p) for p in post]
    span, look = PLAN["span"], PLAN["look"]
    for sweep in range(PLAN["sweeps"]):
        t0 = -rng.rand() * span * 0.5
        while t0 < best:
            seq = sorted(range(n), key=lambda i: (start[i], i))
            _, _, tail = place(sorted(range(n), key=lambda i: (-end[i], -i)), eng, True)
            head = [i for i in seq if start[i] < t0 or i in loads]
            mine = [i for i in seq if t0 <= start[i] < t0 + span + look and i not in loads]
            rest = [i for i in seq if start[i] >= t0 + span + look]
            t0 += span * 0.5
            if len(mine) < 2:
                continue
            base = {k: [] for k in list("vapgsx") + PSUM}
            for i in head:
                if end[i] > t0 - span:
                    base[eng[i]].append((start[i], end[i], i))
                    for b in banks[i]:
                        base[b].append((start[i], end[i], eng[i], i))
            floor = start[mine[0]]
            inside = set(mine)
            out = {i: max([d + tail[j] for j, d in aft[i] if j not in inside] + [lat[i]]) for i in mine}
            nxt = {}
            for i in reversed(rest):
                nxt[eng[i]] = tail[i]
            st, en, why = list(start), list(end), [-1] * n

            def attempt(s, e_):
                busy = {k: list(l) for k, l in base.items()}
                top, arg, tot = 0.0, -1, 0.0
                for i in s:
                    t, y = floor, -1
                    for j, d in fore[i]:
                        if en[j] + d > t:
                            t, y = en[j] + d, j
                    e = e_[i]
                    c, q = cost[i][e], busy[e]
                    while True:
                        t1 = t
                        k = len(q)
                        while k and q[k - 1][1] > t:
                            k -= 1
                        while k < len(q) and q[k][0] < t + c:
                            t, y = q[k][1], q[k][2]
                            k += 1
                        for b in banks[i]:
                            for s0, s1, e2, j in busy[b]:
                                if s1 + wake > t and s0 < t + c + wake and e2 != e:
                                    t, y = s1 + wake, j
                        if t == t1 or not banks[i]:
                            break
                    q.insert(k, (t, t + c, i))
                    for b in banks[i]:
                        busy[b].append((t, t + c, e, i))
                    st[i], en[i], why[i] = t, t + c, y
                    tot += t
                    if t + c + out[i] > top:
                        top, arg = t + c + out[i], i
                for e, x in nxt.items():
                    if e in "vap" and busy[e] and busy[e][-1][1] + x > top:
                        top, arg = busy[e][-1][1] + x, busy[e][-1][2]
                return top + PLAN["mean"] * tot / len(s), arg

            def chain(i):
                c = []
                while i in inside:
                    c.append(i)
                    i = why[i]
                return c
            cur, arg = attempt(mine, eng)
            crit, s1, e1 = chain(arg), mine, eng
            keep = (cur, s1, e1)
            flx = [i for i in mine if len(cost[i]) > 1 and (sweep >= PLAN["pin"] or not ops[i]["at"])]
            for r0, r1, r2, r3, r4, r5 in rng.rand(PLAN["steps"], 6).tolist():
                s2, e2 = s1, e1
                if r0 < 0.25 and flx:
                    cf = [i for i in crit if i in flx]
                    i = cf[int(r1 * len(cf))] if r5 < 0.4 and cf else flx[int(r1 * len(flx))]
                    e2 = list(e1)
                    e2[i] = "v" if e1[i] == "a" else "a"
                    j = flx[int(r2 * len(flx))]
                    if r3 < 0.5 and e1[j] != e1[i]:
                        e2[j] = e1[i]
                elif r0 < 0.55 and len(crit) > 1:
                    k = int(r1 * (len(crit) - 1))
                    i, j = crit[k], crit[k + 1]
                    p, q = s1.index(j), s1.index(i)
                    if i in posts[j] or p > q:
                        continue
                    mid = s1[p:q + 1]
                    if r2 < 0.5:
                        need = {i}
                        for y in reversed(mid):
                            if posts[y] & need:
                                need.add(y)
                    else:
                        late = {j}
                        for y in mid:
                            if any(y in posts[z] for z in late):
                                late.add(y)
                        need = set(mid) - late
                    if j in need or i not in need:
                        continue
                    s2 = s1[:p] + [y for y in mid if y in need] + [y for y in mid if y not in need] + s1[q + 1:]
                else:
                    s2 = list(s1)
                    p = s1.index(crit[int(r1 * len(crit))]) if r5 < 0.5 and crit else int(r1 * len(s1))
                    i = s2.pop(p)
                    q = p
                    if r2 < 0.5:
                        far = max(0, p - 1 - int(r3 * 25))
                        while q > far and i not in posts[s2[q - 1]]:
                            q -= 1
                    else:
                        far = min(len(s2), p + 1 + int(r3 * 25))
                        while q < far and s2[q] not in posts[i]:
                            q += 1
                    if q == p:
                        continue
                    s2.insert(q, i)
                x, arg = attempt(s2, e2)
                if x <= cur + PLAN["heat"] * r4 * (1.0 - sweep / PLAN["sweeps"]):
                    cur, s1, e1, crit = x, s2, e2, chain(arg)
                    if x < keep[0]:
                        keep = (x, s2, e2)
            attempt(keep[1], keep[2])
            x, s2, st2, en2 = justify(head + sorted(mine, key=lambda i: (st[i], i)) + rest, list(keep[2]), None)
            if x <= best + 30.0:
                best, start, end, eng = x, st2, en2, keep[2]
    end = [end[i] + lat[i] for i in range(n)]
    order = sorted(range(n), key=lambda i: (start[i], i))
    return [(i, eng[i]) for i in loads + [i for i in order if i not in loads]]


def rank_program(g, core, T, topo):
    rank = T.rank_of(core)
    if rank is None:
        return
    N = len(T.cores)
    nxt, prv = T.cores[(rank + 1) % N], T.cores[(rank - 1) % N]
    ops = []

    def ap(s):
        if isinstance(s, tuple):
            if s[0] == "*":
                return ap(s[1]).indirect(ap(s[2]))
            ps = slice(None) if s[4] is None else slice(*s[4])
            cs = slice(s[1], s[2]) if s[3] == 1 else slice(s[1], s[2], s[3])
            return T[s[0]][ps, cs]
        return s

    def flat(l):
        o = []
        for s in l:
            if isinstance(s, tuple):
                o += [s[1], s[2]] if s[0] == "*" else [s]
        return o

    def add(eng, fn, rd, wr, cost, kind="c", sem=None, lat=0.0):
        ops.append({"alt": {eng: (fn, cost)}, "r": flat(rd), "w": flat(wr), "k": kind, "sem": sem, "lat": lat, "at": tag[0]})

    tag = [None]

    def step(t, name):
        tag[0] = (t, name) if name in STEP else None

    def either():
        o = ops.pop()
        ops[-1]["alt"].update(o["alt"])
        ops[-1]["r"] = ops[-1]["r"] + [s for s in o["r"] if s not in ops[-1]["r"]]

    def ts(out, in0, s1, s2, o0, o1=None):
        if o1 is None:
            add("v", lambda: g.vector.tensor_scalar(ap(out), ap(in0), ap(s1), None, o0), [in0, s1], [out], _cost("v", out, in0))
        else:
            add("v", lambda: g.vector.tensor_scalar(ap(out), ap(in0), ap(s1), ap(s2), o0, o1), [in0, s1, s2], [out], _cost("v", out, in0))

    def tt(out, a, b, op):
        add("v", lambda: g.vector.tensor_tensor(ap(out), ap(a), ap(b), op), [a, b], [out], _cost("v", out, a, b))

    def cp(out, a):
        add("v", lambda: g.vector.tensor_copy(ap(out), ap(a)), [a], [out], _cost("v", out, a))

    def ms(out, c):
        add("v", lambda: g.vector.memset(ap(out), c), [], [out], _cost("v", out, out))

    def scan(out, d0, d1, o0, o1):
        add("v", lambda: g.vector.tensor_tensor_scan(ap(out), ap(d0), ap(d1), 0.0, o0, o1), [d0, d1], [out], _cost("v", out, d0))

    def act(out, a, scale=1.0, bias=0.0, func=F.Identity, acc=None):
        add("a", lambda: g.scalar.activation(ap(out), ap(a), func, bias=ap(bias), scale=ap(scale), accum_out=ap(acc)),
            [a, scale, bias], [out, acc], _cost("a", out, a))

    def lin(eng, out, a, scale=1.0, bias=0.0):
        if "a" in eng:
            act(out, a, scale, bias)
        if "v" in eng:
            if scale == 1.0 and bias == 0.0:
                cp(out, a)
            elif bias == 0.0:
                ts(out, a, scale, None, A.mult)
            else:
                ts(out, a, scale, bias, A.mult, A.add)
        if len(eng) == 2:
            either()

    def acc(terms, first=False, final=False):
        def fn():
            for n, (o, l, r) in enumerate(terms):
                ins = g.tensor.matmul(ap(o), ap(l), ap(r), first and n == 0, final and n == len(terms) - 1)
            return ins
        c = sum(max(min(64, _len(l)), _len(r)) * (4 if SCRATCH[l[0]][2] == F32 else 1) * PLAN["pe"] + PLAN["pf"] for _, l, r in terms)
        add("p", fn, [x for t in terms for x in t[1:]], sorted(set(t[0] for t in terms), key=repr), c)

    def mm(groups):
        def fn():
            for out, terms in groups:
                for n, (l, r) in enumerate(terms):
                    ins = g.tensor.matmul(ap(out), ap(l), ap(r), n == 0, n == len(terms) - 1)
            return ins
        c = sum(max(min(64, _len(l)), _len(r)) * (4 if SCRATCH[l[0]][2] == F32 else 1) * PLAN["pe"] + PLAN["pf"] for _, terms in groups for l, r in terms)
        add("p", fn, [x for _, terms in groups for t in terms for x in t], [o for o, _ in groups], c)

    def iota(out, pat, base, cm):
        if SCRATCH[out[0]][2] == I32:
            add("g", lambda: g.iota(ap(out), pat, base, cm), [], [out], 130 + 1.66 * _len(out))
        else:
            add("g", lambda: g.iota(ap(out), pat, base, cm, allow_small_or_imprecise_dtypes=True), [], [out], 130 + 1.66 * _len(out))

    def asel(out, a, pat, base, cm, op=A.is_equal, fill=0.0):
        add("g", lambda: g.affine_select(ap(out), ap(a), pat, op, fill, base, cm), [a], [out], 170 + 1.66 * _len(out))

    def band(out, a, pat, cm, lo, hi):
        asel(out, a, pat, -lo, cm, A.is_ge)
        asel(out, out, [[-s, c] for s, c in pat], hi, -cm, A.is_ge)

    def diag(out, a, v):
        asel(out, a, [[1, 128]], 0, -1, A.not_equal, v)

    ndma = [0]

    def dma(q, out, a, kb, after=()):
        sem = "dm%d" % ndma[0]
        ndma[0] += 1
        add(q, lambda: (g.sync if q == "s" else g.scalar).dma_start(ap(out), ap(a)), [a] + list(after), [out],
            60.0 + (4.0 * kb if q == "s" else 0.0), "d", (sem, 16), PLAN["dlat"] + (4.0 * kb if q == "a" else 0.0))

    def send(t, h):
        rid, pid, _ = topo.addr(nxt)
        m = topo.mask(core, nxt)
        a, b = 136 * h, 136 * h + 136
        add("g", lambda: g.remote_dma(T["land%d" % t][:, a:b], T["snd%d" % (t - 1)][:, a:b], T.sem["arr%d%d" % (t, h)], T.sem["out%d%d" % (t, h)], pid, rid, m),
            [R("snd%d" % (t - 1), a, b)], [], 300.0, "r", ("out%d%d" % (t, h), len(topo.engines(core, nxt))), PLAN["hop"])

    def recv(t, h):
        add("x", None, [], [R("land%d" % t, 136 * h, 136 * h + 136)], 0.0, "x", ("arr%d%d" % (t, h), len(topo.engines(prv, core))))

    def col(k):
        return R("cf", k, k + 1)
    CJ, CG, CGG, CJ3, CJQ, CPC, CX8, CM, CSD, MK = range(10)
    ID, NID, HID, IK = R("idp", 12, 140), R("nid", 0, 128), R("hid", 0, 128), R("ik", 0, 128)
    ZB, ZF, ONE = R("zb", 0, 128), R("zf", 0, 128), R("one", 0, 128)
    EXT = {"bc": 0, "cu": 144, "ca": 288, "cp": 432, "cr": 576, "ch": 720}
    W = "wn"

    def win(h, a, b, p=None):
        return R(W, WEND * h + a, WEND * h + b, 1, p)

    def FF(h):
        return win(h, WF_, WF_ + 4)

    def K(h):
        return win(h, WK, WF_)

    def H(h):
        return win(h, WH_, WSK)

    def ext(w, i):
        return R("ex", EXT[w] + 15 - i, EXT[w] + 143 - i)

    dma("s", R("ki", 0, 128), T.kid0[:], 64)
    dma("a", R("ki", 128, 256), T.kid1[:], 64)
    dma("s", R("bi", 0, 256), T.belts[:], 128)
    dma("a", R("fi", 0, 128, 1, (0, 8)), T.flip[:], 4)
    SEL = PLAN["sel"]
    PLUS = 0.0 if len(SEL) == 2 else 1.0

    def FS(a, b):
        return R("fs", a, b) if PLUS else R("ft", POS + a, POS + b)
    dma("s", FS(0, 1024), T.faces[:, 0:1024], 256)
    dma("s", FS(1024, 2048), T.faces[:, 1024:2048], 256)
    if not PLUS:
        dma("a", R("ft", UP, UP + 2048), T.faces[:], 512)

    iota(R("pi", 0, 1), [[1, 1]], 0, 1)
    iota(R("iv", 0, 384), [[-1, 3], [-64, 8], [-2, 16]], 0, 0)
    ms(R("kt", 0, 2048), 0.0)
    ms(R("oneb", 0, 160), 1.0)
    dma("a", R("ex", 0, 720), R("kt", 0, 720), 180)
    iota(R("sc0", 0, 16), [[0, 16]], 0, 0)
    iota(R("sc1", 0, 16), [[0, 16]], 128, 0)
    iota(R("thr", 0, 16), [[0, 16]], 0, 0)
    iota(R("ft", 4096, POS), [[0, 16]], 0, 0)
    pi = R("pi", 0, 1)
    ts(R("ci", 0, 1), pi, 15, None, A.bitwise_and)
    ts(R("ci", 1, 2), pi, 112, None, A.bitwise_and)
    ts(R("ci", 2, 3), pi, 4, 1, A.arith_shift_right, A.bitwise_and)
    cp(R("cf", 0, 3), R("ci", 0, 3))
    asel(R("b8", 0, 144, 1, (0, 8)), R("oneb", 0, 144, 1, (0, 8)), [[1, 144]], -15, -16)
    lin("av", col(CPC), col(CG), 4.0, col(CJ))
    for b in range(2):
        ts(R("im", 384 * b, 384 * b + 384), R("iv", 0, 384), col(CPC), -16.0 * b, A.add, A.is_equal)
    iota(ZB, [[0, 128]], 0, 0)
    iota(ONE, [[0, 128]], 1, 0)
    iota(R("e8", 0, 8), [[0, 8]], 0, 0)
    for w, rows in (("bc", ((15, 1.0),)), ("cu", ((15, -1.0), (7, 1.0))), ("ca", ((15, 0.5),)), ("cp", ((7, 1.0),)), ("cr", ((15, 1.0), (7, 0.0)))):
        o, src = R("ex", EXT[w] + 15, EXT[w] + 143, 16), R("e8", 0, 8)
        for hi, v in rows:
            asel(o, src, [[-16, 8]], -hi, 1, A.is_gt, v)
            src = o
        asel(o, o, [[-16, 8]], 0, 1, A.is_ge)
    asel(R("idp", 0, 160), R("oneb", 0, 160), [[1, 160]], -12, -1)
    for w, v, off in (("nid", -1.0, 0.0), ("hid", 0.5, 0.0), ("wf", 1.0, -KEEP), ("wh", 0.5, -KEEP), ("idf", 1.0, 0.0), ("ik", CKID, 0.0), ("nidf", -1.0, 0.0),
                      ("ra", -256.0, 0.0), ("rb", 0.0625, 0.0), ("rc", 256.0, 0.0)):
        if PLUS or not (off or w == "hid"):
            lin("av", R(w, 0, 128), ID, v - off, off)
    band(R("w0", 0, 128), R("oneb", 0, 128), [[-16, 8], [0, 16]], 1, 0, 15)
    diag(R("wm", 0, 128), R("w0", 0, 128), 33.0)
    iota(R("dg", 0, 128), [[0, 8], [1, 16]], 0, 0)
    ts(R("dg", 0, 128), R("dg", 0, 128), col(CJ), 64.0, A.not_equal, A.mult)
    iota(R("dg", 128, 256), [[0, 128]], 0, 0)
    iota(R("dg", 128, 256, 16), [[0, 8]], 128, 0)
    iota(R("mv", 0, 128), [[16, 128]], 0, 0)
    step(-1, "marks")
    for a in ((0, 1024) if PLUS else ()):
        asel(R("lj", a, a + 1024), R("kt", a, a + 1024), [[-1, 8], [-16, 8], [0, 16]], -(a // 128), 1, A.not_equal, CFACE)
    step(1, "kid0")
    iota(R("li", 0, 16), [[1, 8], [128, 2]], 0, 0)
    iota(R("li", 16, 32), [[16, 2], [32, 8]], 0, 0)
    iota(R("li", 32, 48), [[0, 8], [-256, 2]], 128, 0)
    iota(R("li", 48, 64), [[-32, 2], [0, 8]], 16, 0)
    for w, src in (("fm", "one"), ("fmb", "oneb")):
        for n, k in enumerate((0, -16, 1, -15, 2, -14)):
            asel(R(w, 128 * n, 128 * n + 128), R(src, 0, 128), [[32, 8], [1, 16]], -k, -2)
        asel(R(w, 512, 640, 16), R(src, 0, 8), [[32, 8]], 30, -2)

    def to_val(dst, src, ti, tsh, te):
        ts(ti, src, 1, None, A.bitwise_and)
        ts(te, src, 16.5, None, A.add)
        ts(tsh, ti, -1.0, 0.5, A.mult, A.add)
        tt(dst, tsh, te, A.mult)

    PR = R("ms", 0, 256)
    PIECE = (0, 256, 128, 384)

    def piece(r, up):
        return R("hl", 256 * r + 128 * up, 256 * r + 128 * up + 128)

    def hilo(w, src):
        lin("av", R(w, 0, 256), src)
        tt(R(w, 256, 512), src, R(w, 0, 256), A.subtract)

    def pieces(up):
        for k in range(2):
            lin("av", piece(2 * k, up), R("ms", 128 * k, 128 * k + 128))
            tt(piece(2 * k + 1, up), R("ms", 128 * k, 128 * k + 128), piece(2 * k, up), A.subtract)

    step(-1, "kids")
    ts(R("t1", 0, 256), R("ki", 0, 256), 1, None, A.bitwise_and)
    ts(R("xa", 256, 512), R("ki", 0, 256), 16.5, None, A.add)
    ts(R("t2", 0, 256), R("t1", 0, 256), -1.0, 0.5, A.mult, A.add)
    tt(R("xa", 256, 512), R("xa", 256, 512), R("t2", 0, 256), A.mult)
    lin("av", R("xa", 0, 128), R("xa", 384, 512), -1.0, -0.25)
    lin("av", R("xa", 128, 256), R("xa", 256, 384), 1.0, 0.25)
    hilo("h0", R("xa", 0, 256))
    for r, a in enumerate(PIECE):
        dma("sa"[r % 2], R("kt", 0, 2048, 1, (4 * r, 128, 16)), R("h0", a, a + 128), 32)
    step(-1, "flip")
    cp(R("fb", 0, 128, 1, (0, 8)), R("fi", 0, 128, 1, (0, 8)))
    mm([(R("cn", 128, 136), [(R("b8", 15 - x, 143 - x, 1, (0, 8)), R("fb", x, 128, 16, (0, 8))) for x in range(16)])])
    ts(R("im", 256 + 15, 384, 16), R("iv", 15, 128, 16), col(CPC), -30.0, A.add, A.is_equal)
    cp(R("bv", 0, 256), R("bi", 0, 256))
    mm([(R("u0", 128 * n, 128 * n + 128), [(R("im", 384 * b + 128 * n, 384 * b + 128 * n + 128), R("bv", b, 256, 2)) for b in range(2)])
        for n in range(3)])
    for a in (0, 1024):
        step(-1, "pos")
        if PLUS:
            lin("av", R("ft", POS + a, POS + a + 1024), R("fs", a, a + 1024), 1.0, 1.0)
            dma("s", R("ft", UP + a, UP + a + 1024), R("ft", POS + a, POS + a + 1024), 256)
        step(-1, "neg")
        lin("av", R("ft", 4095 - a, 3071 - a, -1), FS(a, a + 1024), -1.0, 255.0 + PLUS)
        dma("a", R("ft", 1024 - a, 2048 - a), R("ft", 3072 - a, 4096 - a), 256)
    step(0, "round3")
    for h in SEL:
        lin("av", R("yv", 1024 * h, 1024 * h + 1024), FS(1024 * h, 1024 * h + 1024), 1.0, CY + PLUS)
    if SEL:
        for h in set(range(2)) - set(SEL):
            for t in range(5):
                dma("s", R("yv", 2048 * t + 1024 * h, 2048 * t + 1024 * h + 1024), R("yv", 1024 * SEL[0], 1024 * SEL[0] + 1024), 512)
        iota(R("pt0", 0, 256), [[16, 128], [-2048, 2]], 2048, 0)
        lin("av", R("pt0", 0, 256), R("pt0", 0, 256), 1.0, col(CJ))
        iota(R("gi", 0, 256), [[0, 256]], -2 ** 20, 0)
        lin("av", R("ik2", 0, 128), ID, CKID / FAR)
        lin("av", R("two", 0, 128), ID, 2.0)
    step(0, "val3")
    for a in (2048, 4096, 6144):
        dma("s", R("kt", a, a + 2048), R("kt", 0, 2048), 512, after=[R("ft", 0, 8), R("ft", 1024, 1032)])
    step(-1, "belts")
    lin("av", R("sc0", 1, 16, 2), R("cn", 128, 136))
    iota(R("fx", 0, 16), [[0, 16]], 0, 0)
    for h in range(2):
        iota(win(h, WF_ + 4, WH_), [[0, 4]], 0, 0)
        lin("av", FF(h), R("cn", 128 + 4 * h, 132 + 4 * h), 1.0, -0.5)
    lin("av", R("sc1", 1, 16, 2), R("mv", 0, 8), 1.0, col(CJ))
    scan(R("sco", 0, 16), R("sc0", 0, 16), R("sc1", 0, 16), A.mult, A.add)
    cp(R("ofb", 0, 8), R("sco", 1, 16, 2))
    lin("av", R("c0", 0, 384), R("u0", 0, 384))
    cp(R("ke", 0, 128), IND(R("c0", 0, 256), R("ofb", 0, 8)))
    cp(R("ke", 128, 256), IND(R("c0", 128, 384), R("ofb", 0, 8)))
    for h in range(2):
        lin("av", R("sc1", 8 * h + 1, 8 * h + 8, 2), R("sc1", 8 * h + 1, 8 * h + 8, 2), 1.0, WCK - 64.0 * h)
    ts(R("abi", 0, 128), R("ke", 0, 128), 1, 2047, A.arith_shift_right, A.bitwise_and)
    cp(R("ofk", 0, 128), R("abi", 0, 128))
    step(-1, "vals")
    to_val(R("u1", 0, 256), R("ke", 0, 256), R("t4", 0, 256), R("t5", 0, 256), R("u1", 256, 512))
    ts(R("land0", 0, 128), R("u1", 128, 256), MID + 0.25, None, A.add)
    for h in range(2):
        lin("av", K(h), R("u1", 64 * h, 64 * h + 64), 1.0, 0.25)
        lin("av", H(h), R("u1", 128 + 64 * h, 192 + 64 * h), 1.0, 0.25)

    def late_constants():
        lin("av", col(CM), col(CJ), 1.0, 2056.5)
        lin("av", R("cn", 128, 256), R("mv", 0, 128), 1.0, col(CM))

    def last_constants():
        cp(R("kf", 0, 256), R("ki", 0, 256))
        dma("s", T.yx[:, 0:2048], T.faces[:], 512, after=[R("ofk", 0, 8)])
        dma("s", T.y0[:, 0:2048], R("kf", 0, 128), 64)
        dma("s", T.y1[:, 0:2048], R("kf", 128, 256), 64)
        lin("av", col(CX8), col(CJ), 8.0)
        lin("av", R("lt", 16, 32), R("li", 48, 64), col(CGG), col(CJ))
        lin("av", R("lt", 0, 16), R("li", 32, 48), col(CGG), col(CX8))
        tt(R("lt", 0, 32), R("lt", 0, 32), R("li", 0, 32), A.add)
        cp(R("lu", 0, 32), R("lt", 0, 32))

    FT = R("ft", 0, 8208)

    def gather(eng, out, a, b, win, offbuf, off0=0):
        lin(eng, R(out, a, b), IND(win, R(offbuf, off0 + a // 16, off0 + b // 16)))

    def prep(t):
        for h in range(2):
            a, b = 64 * h, 64 * h + 64
            step(t, "conv%d" % h)
            recv(t, h)
            ts(win(h, WK, WSK), R("land%d" % t, 136 * h, 136 * h + 136), -MID, None, A.add)
            AB, RR, X = R("ab", a, b), R("rr", a, b), R("xa", 384 + a, 384 + b)
            act(AB, K(h), 1.0, 0.0, F.Abs)
            ts(R("ng", a, b), R("land%d" % t, 136 * h, 136 * h + 64), MID, 4096.0, A.is_lt, A.mult)
            ts(RR, AB, C16, -C16, A.add, A.add)
            mm([(X, [(ID, R("ng", a, b)), (R("rc", 0, 128), AB), (R("ra", 0, 128), RR), (R("rb", 0, 128), RR)])])
            ts(R("ofk", a, b), X, 1919.0, None, A.add)

    def visit(t):
        S, last = "snd%d" % t, t == 3
        KT = R("kt", 0, 2048 if t == 0 else 8192)

        def DK(h):
            return R("ms", 256 + 64 * h, 320 + 64 * h)

        def DH(h):
            return R("ms", 384 + 64 * h, 448 + 64 * h)

        def pick(out, w, c):
            mm([(out, [(ext(w, i), R("g1", 1024 * c + i, 1024 * c + 1024, 16)) for i in range(16)])])

        def kids_of(c):
            X = "xa" if c == 0 else "xb"
            lo, hi = 64 * c, 64 * c + 64
            step(t, "u%d" % c)
            if t == 0:
                pick(R(X, 0, 64), "cu", c)
                pick(R(X, 64, 128), "ca", c)
                tt(R("sd", lo, hi), R(X, 0, 64), R("t5", lo, hi), A.mult)
                tt(R("uu", lo, hi), R(X, 64, 128), R("sd", lo, hi), A.add)
                tt(R("cn", 384 + lo, 384 + hi), R(X, 64, 128), R("sd", lo, hi), A.subtract)
                ts(R("ofu", lo, hi), R("uu", lo, hi), MID, None, A.add)
            else:
                U = R("xa", lo, hi)
                pick(U, "cp", c)
                ts(R("ofu", lo, hi), U, MID, None, A.add)
                step(t, "a%d" % c)
                pick(R("cn", 384 + lo, 384 + hi), "cr", c)
                if c:
                    step(t, "uu1")
                    lin("av", R("uu", 0, 128), R("xa", 0, 128))

        def diff(a, b):
            tt(R("dd", a, b), IND(FT, R("ofu", a // 16, b // 16)), R("fw", a, b), A.subtract)

        def near(a, b):
            ts(R("ind", a, b), R("dd", a, b), C32, C32, A.add, A.is_equal)

        def count(c):
            mm([(R("cn", 64 * c, 64 * c + 64), [(ext("bc", i), R("ind", 1024 * c + i, 1024 * c + 1024, 16)) for i in range(16)])])

        def q_(n, q):
            return R(n, 512 * q, 512 * q + 512)

        def values(q):
            step(t, "val%d" % q)
            if q in PLAN["own"]:
                X = R("xb", 0, 512)
                gather("a", "dd", 512 * q, 512 * q + 512, FT, "ofu")
                mm([(X, [(ID, q_("dd", q)), (NID, q_("fw", q))])])
                ts(q_("ind", q), X, C32, C32, A.add, A.is_equal)
            else:
                diff(512 * q, 512 * q + 512)
                if q ^ 1 in PLAN["own"]:
                    near(512 * q, 512 * q + 512)
                elif q % 2:
                    near(512 * q - 512, 512 * q + 512)

        def bank(b):
            return R("u%d" % b, 0, 512)

        def oldf(b, base, w="ft"):
            a = base + 1024 * (b // 2) + b % 2
            return R(w, a, a + 1023, 2)

        def change(b):
            step(t, "change%d" % b)
            if b // 2 in SEL:
                acc([(bank(b), ID if b in PLAN["own"] else R("two", 0, 128), q_("fw", b))], first=True)
                acc([(bank(b), ID, q_("dd", b))], final=True)
                step(t, "round%d" % b)
                lin("av", R("yv", 2048 * (t + 1) + 512 * b, 2048 * (t + 1) + 512 * b + 512), bank(b), 0.5 - 2.0 ** -11, CY)
                return
            step(t, "start")
            acc([(bank(b), NID, oldf(b, POS if t == 0 else UP))], first=True)
            step(t, "change%d" % b)
            for w, n in (("f", "fw"), ("d", "dd")):
                qs = (2 * (b // 2), 2 * (b // 2) + 1)
                lw = [R("hid" if w == "d" else "wh" if q in PLAN["own"] else "wf", 0, 128) for q in qs]
                if lw[0] == lw[1]:
                    acc([(bank(b), lw[0], R(n, 512 * qs[0] + b % 2, 512 * qs[0] + 1024, 2))])
                else:
                    acc([(R("u%d" % b, 256 * h, 256 * h + 256), lw[h], R(n, 512 * q + b % 2, 512 * q + 512, 2)) for h, q in enumerate(qs)])

        def renew(b):
            def wipe(m):
                return [(R("u%d" % b, jj, 512, 8), R("lj", 128 * (2 * jj + b % 2), 128 * (2 * jj + b % 2) + 128), R(m, 64 * (b // 2), 64 * (b // 2) + 64))
                        for jj in range(8)]
            step(t, "renew%d" % b)
            if b // 2 in SEL:
                lin("av", R("ft", UP + 512 * b, UP + 512 * b + 512), IND(R("yv", 0, 2048 * (t + 2)), R("ptu", 32 * b, 32 * b + 32)), 1.0, -CY - (PLUS if last else 0.0))
                return
            acc(wipe("gz"))
            if last and b in PLAN["tadd"]:
                acc(wipe("gn"), final=True)
                lin("av", oldf(b, 0, "fs"), oldf(b, UP), 1.0, -1.0)
                tt(oldf(b, UP), oldf(b, 0, "fs"), bank(b), A.add)
            elif not last and b in PLAN["vadd"]:
                acc(wipe("gn"), final=True)
                tt(oldf(b, UP), oldf(b, UP), bank(b), A.add)
            else:
                acc(wipe("gn") + [(bank(b), ID, oldf(b, POS if t == 0 else UP))], final=True)
                lin("av", oldf(b, UP), bank(b), 1.0, -1.0 if last else 0.0)

        GQ = PLAN["gq"]
        for a in range(0, 2048, GQ):
            step(t, "kid%d" % (a // 512))
            gather("av", "g1", a, a + GQ, KT, "ofk")
        for a, b in PLAN["fq"]:
            step(t, "fw%d" % (a // 512))
            gather("av", "fw", a, b, FT, "land%d" % t, 72 * (1 + a // 1024) if t else 0)
        step(t, "")
        if t == 0:
            late_constants()
            step(t, "val1")
            for n, w in enumerate(("cp", "cr")):
                mm([(R("ms", 128 * n, 128 * n + 128), [(ext(w, i), R("kt", i, 2048, 16)) for i in range(16)])])
            pieces(0)
        kids_of(0)
        kids_of(1)
        step(t, "kc")
        K0, K1 = (R("ms", 0, 128), R("ms", 128, 256)) if last else (R("ms", 128, 256), R("ms", 0, 128))
        IDF, NIDF, UU = R("idf", 0, 128), R("nidf", 0, 128), R("uu", 0, 128)

        def kept(p, m):
            return [(K0 if r > 1 else K1, m if last and r < 2 else p, piece(r, min(t, 1))) for r in range(4)]
        acc([(PR, ZB, R("h0", 0, 256))] + kept(NID, ID), first=True)
        acc([(R("ms", K1[1] + 64 * h, K1[1] + 64 * h + 64), IDF if last else NIDF, H(h)) for h in range(2)])
        acc([(K0, IDF, UU)])

        def slots(b, w, ks, hs, X, at):
            def fm(n):
                return R(w, 128 * n, 128 * n + 128)
            mm([(R(X, 128 * f + 64 * h, 128 * f + 64 * h + 64), [(fm(2 * f + b), k(h)) for k in ks] + [(fm(2 * f + 2 + b), k(h)) for k in hs])
                for f in range(2) for h in range(2)])
            act(R("hy", 512 * b + at, 512 * b + at + 256), R(X, 0, 256), -2.0, -0.5, F.Abs)

        step(t, "g")
        if last:
            for b in range(2):
                slots(b, "fm", [K], [H], "xb", 256)
            for h in range(2):
                lin("av", R("lf", 4 * h, 4 * h + 4), FF(h), 128.0, 64.0 + 64 * h - WCK)
            tt(R("sc1", 1, 16, 2), R("sc1", 1, 16, 2), R("lf", 0, 8), A.add)
            ms(R("sc1", 0, 16, 2), 256.0)
        else:
            for h in range(2):
                lin("av", R("sc1", 8 * h, 8 * h + 8, 2), FF(h), -float(WH_), 0.5 * WH_ - WCK)
                dma("s", win(h, 0, WK, (1, 128)), win(h, WH_, WSK, (0, 127)), 32)
                dma("s", win(h, WSK, WCK, (0, 127)), win(h, WK, WF_, (1, 128)), 32)
                dma("s", win(h, 0, WK, (0, 128, 16)), win(h, WH_, WSK, (15, 128, 16)), 2)
                dma("s", win(h, WSK, WCK, (15, 128, 16)), win(h, WK, WF_, (0, 128, 16)), 2)
        for q in range(4):
            values(q)
        for c in range(2):
            step(t, "count%d" % c)
            count(c)
        for b in range(4):
            change(b)
        for h in range(2):
            step(t, "dk%d" % h)
            tt(DK(h), K(h), R("cn", 384 + 64 * h, 448 + 64 * h), A.subtract)
            tt(DH(h), H(h), R("cn", 128 + 64 * h, 192 + 64 * h), A.subtract)
        step(t, "thr")
        if t > 0:
            act(R("thr", 8, 16), R("xa", 128, 136), -1.0, 0.0, F.Identity, R("thr", 1, 2))
            ts(R("thr", 3, 4), R("thr", 1, 2), C2, -C2, A.add, A.add)
            act(R("thr", 0, 1), R("thr", 3, 4), -1.0, R("thr", 1, 2), F.Abs)
        PARTS = ((0, 64), (64, 128)) if PLUS or t in PLAN["split"] else ((0, 128),)
        for h in range(2):
            a, b = 64 * h, 64 * h + 64
            SPL, NS = R("spl", a, b), R("xa", 256 + a, 256 + b)
            step(t, "spl%d" % h)
            ts(SPL, R("cn", a, b), R("thr", 0, 1), 8.5, A.subtract, A.is_ge)
            mm([(NS, [(ID, R("dg", a, b)), (R("w0", 0, 128), SPL)])])
            step(t, "open%d" % h)
            scan(R("sd", a, b), R("dg", 128 + a, 128 + b), NS, A.add, A.min)
            tt(DK(h), DK(h), SPL, A.mult)
            tt(DH(h), DH(h), SPL, A.mult)
            ts(R("sc0", 8 * h + 1, 8 * h + 8, 2), R("sd", a + 15, b, 16), 4.5, None, A.is_lt)
            tt(win(h, WCK, WCH), DK(h), K(h), A.subtract)
            tt(win(h, WCH, WEND), DH(h), H(h), A.subtract)
            if not last:
                scan(R("sco", 8 * h, 8 * h + 8), R("sc0", 8 * h, 8 * h + 8), R("sc1", 8 * h, 8 * h + 8), A.mult, A.add)
                cp(R("ofb", 4 * h, 4 * h + 4), R("sco", 8 * h + 1, 8 * h + 8, 2))
            tt(R("fx", 8 * h, 8 * h + 4), FF(h), R("sc0", 8 * h + 1, 8 * h + 8, 2), A.subtract)
            if not last:
                OFF = R("ofb", 4 * h, 4 * h + 4)
                ts(R(S, 136 * h + 64, 136 * h + 72), R("fx", 8 * h, 8 * h + 8), -0.5, MID - 0.5, A.not_equal, A.add)
                ts(R(S, 136 * h, 136 * h + 64), IND(win(h, 0, WCH), OFF), -1.0, MID, A.mult, A.add)
                ts(R(S, 136 * h + 72, 136 * h + 136), IND(win(h, WK, WEND), OFF), -1.0, MID, A.mult, A.add)
                send(t + 1, h)
        for a, b in PARTS:
            step(t, "spl%d" % (b // 128))
            mm([(R("cn", 256 + a, 256 + b), [(R("wm", 0, 128), R("spl", a, b))])])
        step(t, "open1")
        OFF = R("ofb", 0, 8)
        if last:
            scan(R("sco", 0, 16), R("sc0", 0, 16), R("sc1", 0, 16), A.mult, A.add)
            cp(OFF, R("sco", 1, 16, 2))
        else:
            mm([(R("xa", 128, 136), [(ONE, R("sc0", 1, 16, 2))])])
        wipe_kids = []
        for a, b in PARTS:
            step(t, "go%d" % (b // 128))
            ts(R("gz", a, b), R("cn", 256 + a, 256 + b), 36.5, KEEP, A.is_lt, A.max)
            if a // 64 in SEL:
                pa, pb = ("pt0", "pt1") if t % 2 == 0 else ("pt1", "pt0")
                lin("av", R("gi", 2 * a + 1, 2 * b, 2), R("gz", a, b), -FAR)
                scan(R(pb, 2 * a, 2 * b), R("gi", 2 * a, 2 * b), R(pa, 2 * a, 2 * b), A.add, A.max)
                cp(R("ptu", a, b), R(pb, 2 * a + 1, 2 * b, 2))
                if not last and b == 64 * max(SEL) + 64:
                    step(t, "turn1")
                    lo, hi = 128 * min(SEL), 128 * max(SEL) + 128
                    lin("av", R(pb, lo, hi, 2), R(pb, lo, hi, 2), 1.0, 2048.0)
                wipe_kids += [(R("ms", k + a, k + b), R("ik2", 0, 128), R("gi", 2 * a + 1, 2 * b, 2)) for k in (0, 128)]
            else:
                lin("av", R("gn", a, b), R("gz", a, b), -1.0)
                wipe_kids += [(R("ms", k + a, k + b), IK, R("gn", a, b)) for k in (0, 128)]
        step(t, "kids1")
        acc([(k, IK, R("gz", 0, 128)) for k in (K0, K1)])
        acc(wipe_kids + kept(ID, NID), final=True)
        if not last:
            pieces(1)
            for r in range(8):
                dma("sa"[r % 2], R("kt", 4096 * (r // 4), 4096 * (r // 4) + 4096, 1, (4 * (r % 4), 128, 16)), R("hl", 256 * ((r + r // 4 * 2) % 4), 256 * ((r + r // 4 * 2) % 4) + 256), 64)
            for b in range(4):
                renew(b)
            for a in range(0, 2048, PLAN["tq"]):
                b = a + PLAN["tq"]
                step(t, "turn%d" % (a // 1024))
                lin("av", R("ft", 2047 - a, (2047 - b) if b < 2048 else None, -1), R("ft", UP + a, UP + b), -1.0, 255.0 + 2 * PLUS)
            prep(t + 1)
            step(t, "")
            if t == 1:
                last_constants()
        if last:
            step(t, "slots")
            for h in range(2):
                lin("av", R("h0", 128 * h, 128 * h + 128), win(h, WCK, WEND))
                tt(R("h0", 256 + 128 * h, 384 + 128 * h), win(h, WCK, WEND), R("h0", 128 * h, 128 * h + 128), A.subtract)

            def part(a):
                return lambda h: R("h0", a + 128 * h, a + 128 * h + 64)
            for b in range(2):
                slots(b, "fmb", [part(0), part(256)], [part(64), part(320)], "u0" if b == 0 else "xb", 0)
            for b in range(4):
                renew(b)
                for a in ((512 * b,) if b // 2 in SEL else (512 * b - 512, 512 * b) if b % 2 else ()):
                    dma("sa"[a // 512 % 2], T.yx[:, 2048 + a:2560 + a], R("ft", UP + a, UP + a + 512), 128)
            step(t, "out0")
            lin("av", R("old", 0, 256), PR)
            act(R("tr0", 0, 256), IND(R("old", 0, 256), R("lu", 0, 16)), 2.0, -0.5, F.Abs)
            add("v", lambda: g.vector.transpose(ap(R("tr1", 0, 256)), ap(R("tr0", 0, 256))), [R("tr0", 0, 256)], [R("tr1", 0, 256)], 262.0)
            lin("av", R("tr2", 0, 256), IND(R("tr1", 0, 256), R("lu", 16, 32)), 1.0, -16.5)
            dma("s", T.y0[:, 2048:4096], R("tr2", 0, 128), 64)
            for gq in range(8):
                dma("s" if gq % 2 else "a", T.y1[gq ^ 1, 2048:4096], R("tr2", 128, 256, 1, (16 * gq, 16 * gq + 16)), 8)
            step(t, "out1")
            ts(R("fnb", 0, 16), R("fx", 0, 16), -0.5, None, A.not_equal)
            mm([(R("cn", 384 + 64 * h + x, 448 + 64 * h, 16, (0, 8)), [(R("idp", 12 + x, 140, 16), R("fnb", 8 * h, 8 * h + 4))]) for x in range(16) for h in range(2)])
            for b in range(2):
                lin("av", R("yb1", b, 256, 2), IND(R("hy", 512 * b, 512 * b + 512), OFF), 1.0, -16.5)
            lin("av", R("yfo", 0, 128, 1, (0, 8)), R("cn", 384, 512, 1, (0, 8)))
            dma("s", T.yb[:], R("yb1", 0, 256), 128)
            dma("s", T.yf[:], R("yfo", 0, 128, 1, (0, 8)), 4)

    for t in range(4):
        visit(t)

    key = repr(sorted(PLAN.items()))
    if key not in _PLANS:
        edges = _edges(ops)
        _PLANS[key] = (edges, _plan(ops, edges))
    edges, order = _PLANS[key]
    pos = {i: n for n, (i, _) in enumerate(order)}
    for i, e in order:
        ops[i]["e"] = e
        ops[i]["fn"] = ops[i]["alt"][e][0]
        ops[i]["pre"] = edges[i]
    ops = [ops[i] for i, _ in order]
    bank = {}
    for n, o in enumerate(ops):
        deps = set()
        for j, raw in o["pre"].items():
            deps.add(pos[j])
        for s in o["r"] + o["w"]:
            if s[0] in PSUM:
                deps.update(n2 for e2, n2 in bank.setdefault(s[0], {}).items() if e2 != o["e"])
        for s in o["r"] + o["w"]:
            if s[0] in PSUM:
                bank[s[0]][o["e"]] = n
        newest = {}
        for d in deps:
            if o["e"] == "p" and ops[d]["e"] == "p":
                continue
            k = ops[d]["e"] if ops[d]["k"] == "c" else d
            newest[k] = max(newest.get(k, -1), d)
        o["deps"] = sorted(newest.values())
    seen = {}
    for o in ops:
        keep = []
        for d in o["deps"]:
            k = (o["e"], ops[d]["e"] if ops[d]["k"] == "c" else d)
            if seen.get(k, -1) < d:
                seen[k] = d
                keep.append(d)
                ops[d]["need"] = True
        o["deps"] = keep
    cnt = {"v": 0, "a": 0, "p": 0, "g": 0}
    for o in ops:
        if o["k"] == "c" and o.get("need"):
            cnt[o["e"]] += 1
            o["sem"] = ("e" + o["e"], cnt[o["e"]])
    Q = {"v": g.vector, "a": g.scalar, "p": g.tensor, "g": g, "s": g.sync}
    for o in ops:
        if o["k"] == "x":
            continue
        for d in o["deps"]:
            Q[o["e"]].wait_ge(T.sem[ops[d]["sem"][0]], ops[d]["sem"][1])
        ins = o["fn"]()
        if o["k"] == "d":
            ins.then_inc(T.sem[o["sem"][0]], 16)
        elif o["k"] == "c" and o.get("need"):
            ins.then_inc(T.sem[o["sem"][0]], 1)
    for o in ops:
        if o["k"] in "dr" and not o.get("need"):
            (g if o["k"] == "r" else g.sync).wait_ge(T.sem[o["sem"][0]], o["sem"][1])
